import numpy as np
import ml_dtypes


def mxq(x, axis, fmt="e4m3"):
    dtype, down = {"e4m3": (ml_dtypes.float8_e4m3fn, 7), "e5m2": (ml_dtypes.float8_e5m2, 14)}[fmt]
    v = np.moveaxis(np.asarray(x, np.float32).astype(ml_dtypes.bfloat16).astype(np.float64), axis, -1)
    blocks = v.reshape(v.shape[:-1] + (-1, 32))
    amax = np.abs(blocks).max(-1, keepdims=True)
    byte = np.maximum(np.where(amax > 0, np.frexp(amax)[1] - 1 + 127, 0) - down, 1)
    scale = np.exp2(byte - 127.0)
    codes = (blocks / scale).astype(np.float32).astype(dtype).astype(np.float64)
    return np.moveaxis((codes * scale).reshape(v.shape), -1, axis)


WIDE = False


def mx_kscale(k):
    if not WIDE:
        return np.ones(k)
    levels = np.array([10, -10, 5, -5, 0])
    if k % 512:
        return np.exp2(np.random.permutation(np.resize(levels, k // 32))).repeat(32)
    a = np.empty((k // 512, 16))
    for p in range(k // 512):
        a[p, :8] = np.random.permutation(np.resize(levels, 8))
        for g in range(8):
            far = levels[np.abs(levels - a[p, g]) >= 10]
            a[p, g + 8] = far[np.random.randint(len(far))]
    return np.exp2(a.ravel()).repeat(32)


def f64(x):
    return np.asarray(x).astype(np.float64)


def striped(idx):
    return np.tile(idx.reshape(-1, 16).T, (8, 1)).astype(np.uint16)


def unstriped(offs):
    return offs[:16].T.reshape(-1).astype(np.int64)


E2M1 = np.array([0.0, 0.5, 1.0, 1.5, 2.0, 3.0, 4.0, 6.0, -0.0, -0.5, -1.0, -1.5, -2.0, -3.0, -4.0, -6.0])


def pack_weight(w, fmt):
    k, n = w.shape
    w = f64(np.asarray(w, np.float32).astype(ml_dtypes.bfloat16)).reshape(k // 32, 32, n)
    amax = np.abs(w).max(1)
    if fmt == "e4m3":
        byte = np.frexp(amax)[1] - 1 + 127 - 7
    else:
        mant, ex = np.frexp(amax / 6.0)
        byte = np.where(mant > 0.5, ex, ex - 1) + 127
    byte = np.clip(np.where(amax > 0, byte, 1), 1, 254)
    scaled = (w * np.exp2(127.0 - byte)[:, None, :]).reshape(k, n).astype(np.float32)
    by_word = np.ascontiguousarray(scaled.reshape(k // 512, 128, 4, n).transpose(0, 1, 3, 2))
    if fmt == "e4m3":
        words = by_word.astype(ml_dtypes.float8_e4m3fn).view(np.uint8)
    else:
        c = by_word.astype(ml_dtypes.float4_e2m1fn).view(np.uint8) & 0xF
        words = (c[..., 0::2] | (c[..., 1::2] << 4)).reshape(k // 512, 128, 2 * n)
    return np.ascontiguousarray(words), np.ascontiguousarray(byte.astype(np.uint8).reshape(k // 512, 16, n))


def unpack_weight(words, scales, fmt):
    g, _, n = scales.shape
    words = np.ascontiguousarray(words).reshape(g, 128, n, -1)
    if fmt == "e4m3":
        vals = words.view(ml_dtypes.float8_e4m3fn).astype(np.float64)
    else:
        nib = np.empty((g, 128, n, 4), np.uint8)
        nib[..., 0::2] = words & 0xF
        nib[..., 1::2] = words >> 4
        vals = E2M1[nib]
    vals = vals * np.repeat(np.exp2(scales.astype(np.float64) - 127.0), 8, axis=1)[..., None]
    return vals.transpose(0, 1, 3, 2).reshape(g * 512, n)


def gelu(v):
    return 0.5 * v * (1.0 + np.tanh(np.sqrt(2.0 / np.pi) * (v + 0.044715 * v**3)))


def striped8(idx):
    return np.concatenate([v.reshape(-1, 16).T for v in idx]).astype(np.uint16)


def unstriped8(offs):
    return np.stack([offs[16 * g:16 * g + 16].T.reshape(-1) for g in range(8)]).astype(np.int64)


def put_heads(h, wgs, idx8, t2):
    r = np.arange(h.shape[0])
    page = np.zeros((h.shape[0], t2))
    page[r[:, None], idx8[r % 512 // 64]] = wgs[r // 4 % 128] * h
    return page


K, H, N, T, S, T2 = 1024, 1024, 512, 2048, 1024, 2048


def setup_inputs():
    n = np.random.standard_normal
    s = mx_kscale(K)[:, None]
    u = mx_kscale(H)[:, None]
    tab_words, tab_scales = pack_weight(n((K, T)) * s, "e4m3")
    wc_words, wc_scales = pack_weight(n((H, N)) / np.sqrt(H) / u, "e2m1")
    bins = [np.random.permutation(T2)[:S] for _ in range(8)]
    return {
        "tab_words": tab_words,
        "tab_scales": tab_scales,
        "offs": striped(np.random.permutation(T)[:S]),
        "wf": (n((K, H)) / np.sqrt(K) / s).astype(np.float32),
        "wgs": np.repeat(np.random.uniform(0.5, 2.0, (8, S)), 16, axis=0).astype(np.float32),
        "offs2": striped8(np.stack(bins)),
        "stock": (np.exp(0.5 * n((H, T2))) * u).astype(np.float32),
        "wc_words": wc_words,
        "wc_scales": wc_scales,
    }


def reference(tab_words, tab_scales, offs, wf, wgs, offs2, stock, wc_words, wc_scales):
    v = unpack_weight(tab_words, tab_scales, "e4m3")[:, unstriped(offs)]
    a = mxq(f64(wf), 0, "e4m3").T @ v
    h = np.log(1.0 + np.exp(a))
    page = put_heads(h, f64(wgs), unstriped8(offs2), T2)
    z = np.exp(-page) * f64(stock)
    wc = unpack_weight(wc_words, wc_scales, "e2m1")
    return wc.T @ mxq(z, 0, "e4m3")

@@ -1,0 +1,292 @@
+from contextlib import ExitStack
+
+import concourse.mybir as mybir
+
+K, H, N, T, S, T2 = 1024, 1024, 512, 2048, 1024, 2048
+FLOPS = 2 * K * H * S + 2 * H * N * T2
+
+F32 = mybir.dt.float32
+BF16 = mybir.dt.bfloat16
+I32 = mybir.dt.int32
+U32 = mybir.dt.uint32
+U16 = mybir.dt.uint16
+U8 = mybir.dt.uint8
+FP8X4 = mybir.dt.float8_e4m3fn_x4
+FP4X4 = mybir.dt.float4_e2m1fn_x4
+ACT = mybir.ActivationFunctionType
+ALU = mybir.AluOpType
+
+P = 128
+PACK = 4
+KP = P * PACK
+BANK = 512
+PASSES = K // KP
+TILES = H // P
+CHUNKS = T2 // BANK
+HALVES = S // BANK
+PAGES = 4
+EARLY = 2
+FUSED = 2
+
+
+def tile_list_parts_depletion_kernel(tc, tab_words, tab_scales, offs, wf, wgs, offs2, stock, wc_words, wc_scales, out):
+    nc = tc.nc
+    with ExitStack() as ctx:
+        keep = ctx.enter_context(tc.tile_pool(name="keep", bufs=1))
+        ring = ctx.enter_context(tc.tile_pool(name="ring", bufs=1))
+        psum = ctx.enter_context(tc.psum_pool(name="psum", bufs=1))
+
+        parts = keep.tile([P, S // 16], U16, name="parts")
+        bins = keep.tile([P, S // 16], U16, name="bins")
+        tab_w = [ring.tile([P, T], I32, name="tab_w%d" % a, tag="window%d" % a, bufs=1, align_bytes=64) for a in range(PASSES)]
+        tab_s = keep.tile([P, T], U8, name="tab_s", align_bytes=64)
+        v_w = [keep.tile([P, S], U32, name="v_w%d" % a, align_bytes=64) for a in range(PASSES)]
+        v_s = keep.tile([P, S], U8, name="v_s", align_bytes=64)
+        wf_w = {(a, b): keep.tile([P, KP], U32, name="wf_w%d%d" % (a, b), align_bytes=64) for a in range(PASSES) for b in range(PASSES)}
+        wf_s = {(a, b): keep.tile([P, KP], U8, name="wf_s%d%d" % (a, b), align_bytes=64) for a in range(PASSES) for b in range(PASSES)}
+        weights = keep.tile([P, S], F32, name="weights")
+        rates = [keep.tile([P, S], F32, name="rates%d" % i) for i in range(4)]
+        pages = [keep.tile([P, T2], F32, name="page%d" % i) for i in range(PAGES - PASSES)]
+        z_w = {(b, c): keep.tile([P, BANK], U32, name="z_w%d%d" % (b, c), align_bytes=64) for b in range(PASSES) for c in range(CHUNKS)}
+        z_s = {(b, c): keep.tile([P, BANK], U8, name="z_s%d%d" % (b, c), align_bytes=64) for b in range(PASSES) for c in range(CHUNKS)}
+        wc_w = keep.tile([P, PASSES, 2 * N], U8, name="wc_w", align_bytes=64)
+        wc_s = keep.tile([P, PASSES, N], U8, name="wc_s", align_bytes=64)
+        banks = [psum.tile([P, BANK], F32, name="bank%d" % i) for i in range(8)]
+
+        nc.vector.memset(tab_s[:].bitcast(I32), 0)
+        nc.vector.memset(wc_s[:].rearrange("p a n -> p (a n)").bitcast(I32), 0)
+        for page in pages:
+            nc.vector.memset(page[:], 0.0)
+
+        def load_wf(a, b):
+            raw = ring.tile([P, PACK, KP], F32, name="raw", tag="big", bufs=8)
+            nc.sync.dma_start(out=raw[:], in_=wf[KP * a : KP * (a + 1), KP * b : KP * (b + 1)].rearrange("(p j) c -> p j c", j=PACK))
+            return raw
+
+        def load_table(a):
+            nc.sync.dma_start(out=tab_w[a][:], in_=tab_words[a].rearrange("p t i -> p (t i)").bitcast(I32))
+
+        def load_stock(b, c):
+            st = ring.tile([P, PACK, BANK], F32, name="st", tag="stock", bufs=5)
+            nc.sync.dma_start(out=st[:], in_=stock[KP * b : KP * (b + 1), BANK * c : BANK * (c + 1)].rearrange("(p t) m -> p t m", t=PACK))
+            return st
+
+        nc.sync.dma_start(parts[:], offs)
+        load_table(0)
+        for q in range(4):
+            nc.sync.dma_start(out=tab_s[32 * q : 32 * q + 4 * PASSES, :].bitcast(I32), in_=tab_scales[:, 4 * q : 4 * q + 4, :].bitcast(I32))
+        raws = {}
+        raws[0, 0] = load_wf(0, 0)
+        raws[1, 0] = load_wf(1, 0)
+        load_table(1)
+        nc.sync.dma_start(bins[:], offs2)
+        nc.sync.dma_start(out=weights[:], in_=wgs)
+        raws[0, 1] = load_wf(0, 1)
+        raws[1, 1] = load_wf(1, 1)
+        nc.sync.dma_start(out=wc_w[:].bitcast(I32), in_=wc_words.rearrange("a p n -> p a n").bitcast(I32))
+        for q in range(4):
+            nc.sync.dma_start(out=wc_s[32 * q : 32 * q + 4, :, :].bitcast(I32), in_=wc_scales[:, 4 * q : 4 * q + 4, :].rearrange("a r n -> r a n").bitcast(I32))
+        stocks = {}
+        for c in range(CHUNKS):
+            stocks[0, c] = load_stock(0, c)
+
+        def half(n):
+            return slice(BANK * n, BANK * (n + 1))
+
+        def entries(n):
+            return slice(BANK // 16 * n, BANK // 16 * (n + 1))
+
+        def gather_words(a, n):
+            nc.vector.tensor_copy(v_w[a][:, half(n)], tab_w[a][:].bitcast(U32).indirect(parts[:, entries(n)]))
+
+        def gather_scales(n):
+            nc.vector.tensor_copy(v_s[:, half(n)], tab_s[:].indirect(parts[:, entries(n)]))
+
+        def round_wf(a, b, on_scalar):
+            grouped = ring.tile([P, PACK * KP], BF16, name="grouped", tag="bf16", bufs=7, align_bytes=64)
+            dst = grouped[:].rearrange("p (t m j) -> p m j t", t=PACK, j=PACK)
+            src = raws[a, b][:].rearrange("p j (m t) -> p m j t", t=PACK)
+            if on_scalar:
+                nc.scalar.copy(out=dst, in_=src)
+            else:
+                nc.vector.tensor_copy(out=dst, in_=src)
+            return grouped
+
+        def quantize_wf(a, b, grouped, lo, hi):
+            nc.vector.quantize_mx(out=wf_w[a, b][:, P * lo : P * hi].bitcast(FP8X4), scales=wf_s[a, b][:, P * lo : P * hi], in_=grouped[:, KP * lo : KP * hi])
+
+        def first_product(k):
+            b, t = divmod(k, PACK)
+            rows = slice(P * t, P * (t + 1))
+            for n in range(HALVES):
+                cols = slice(BANK * n, BANK * (n + 1))
+                for a in range(PASSES):
+                    nc.tensor.matmul_mx(
+                        out=banks[(HALVES * k + n) % 8][:],
+                        lhsT=wf_w[a, b][:, rows].bitcast(FP8X4),
+                        lhsT_scale=wf_s[a, b][:, rows],
+                        rhs=v_w[a][:, cols].bitcast(FP8X4),
+                        rhs_scale=v_s[4 * a : P, cols],
+                        start=(a == 0),
+                        stop=(a == PASSES - 1),
+                    )
+
+        def halves(k):
+            return [(banks[(HALVES * k + n) % 8][:], rates[k % 4][:, BANK * n : BANK * (n + 1)]) for n in range(HALVES)]
+
+        def magnitude(k):
+            for acc, part in halves(k):
+                nc.scalar.activation(out=part, in_=acc, func=ACT.Abs)
+
+        def decay(k):
+            for acc, part in halves(k):
+                nc.scalar.activation(out=part, in_=part, func=ACT.Exp, scale=-1.0)
+
+        def log_one_plus(k):
+            for acc, part in halves(k):
+                nc.scalar.activation(out=part, in_=part, func=ACT.Ln, bias=1.0)
+
+        def finish(k):
+            for acc, part in halves(k):
+                nc.vector.scalar_tensor_tensor(out=part, in0=acc, scalar=0.0, in1=part, op0=ALU.max, op1=ALU.add)
+
+        def weigh(k):
+            for n in range(HALVES):
+                part = rates[k % 4][:, half(n)]
+                nc.gpsimd.tensor_tensor(part, part, weights[:, half(n)], ALU.mult)
+
+        def scatter(k, cut):
+            page = pages[k % PAGES]
+            pieces = [(half(n), entries(n)) for n in range(HALVES)] if cut else [(slice(0, S), slice(0, S // 16))]
+            for cols, names in pieces:
+                if k < FUSED:
+                    nc.vector.tensor_tensor(page[:].indirect(bins[:, names]), rates[k % 4][:, cols], weights[:, cols], ALU.mult)
+                else:
+                    nc.vector.tensor_copy(page[:].indirect(bins[:, names]), rates[k % 4][:, cols])
+
+        kept = {}
+
+        def thin(k):
+            b, t = divmod(k, PACK)
+            for c in range(CHUNKS):
+                if t == 0:
+                    kept[b, c] = ring.tile([P, PACK, BANK], F32, name="kept", tag="big", bufs=8)
+                nc.scalar.activation(out=kept[b, c][:, t, :], in_=pages[k % PAGES][:, BANK * c : BANK * (c + 1)], func=ACT.Exp, scale=-1.0)
+
+        zs = {}
+
+        def new_z(b, c):
+            zs[b, c] = ring.tile([P, PACK * BANK], BF16, name="z", tag="bf16", bufs=7, align_bytes=64)
+            return zs[b, c]
+
+        def deplete(engine, dst, b, c, ts):
+            engine.tensor_tensor(
+                dst,
+                kept[b, c][:, ts, :].rearrange("p t (m i) -> p m t i", i=2),
+                stocks[b, c][:, ts, :].rearrange("p t (m i) -> p m t i", i=2),
+                ALU.mult,
+            )
+
+        def deplete_pair_in_place(engine, b, c, pair):
+            z = new_z(b, c) if pair == 0 else zs[b, c]
+            ts = slice(2 * pair, 2 * pair + 2)
+            deplete(engine, z[:].rearrange("p (m i t) -> p m t i", i=2, t=PACK)[:, :, ts, :], b, c, ts)
+
+        def deplete_pair(engine, dst, b, c, pair):
+            deplete(engine, dst.rearrange("p (m i t) -> p m t i", i=2, t=2), b, c, slice(2 * pair, 2 * pair + 2))
+
+        def deplete_whole(b, c):
+            deplete(nc.vector, new_z(b, c)[:].rearrange("p (m i t) -> p m t i", i=2, t=PACK), b, c, slice(0, PACK))
+
+        def quantize_z(b, c):
+            nc.vector.quantize_mx(out=z_w[b, c][:].bitcast(FP8X4), scales=z_s[b, c][:], in_=zs[b, c][:])
+
+        def second_product(c):
+            for nt in range(N // P):
+                i = (N // P * c + nt) % 8
+                for b in range(PASSES):
+                    nc.tensor.matmul_mx(
+                        out=banks[i][:],
+                        lhsT=wc_w[:, b, 2 * P * nt : 2 * P * (nt + 1)].bitcast(FP4X4),
+                        lhsT_scale=wc_s[:, b, P * nt : P * (nt + 1)],
+                        rhs=z_w[b, c][:].bitcast(FP8X4),
+                        rhs_scale=z_s[b, c][:],
+                        start=(b == 0),
+                        stop=(b == PASSES - 1),
+                    )
+                staged = rates[i // 2][:, BANK * (i % 2) : BANK * (i % 2 + 1)]
+                if c == CHUNKS - 1 and nt % 2 == 1:
+                    nc.vector.tensor_copy(out=staged, in_=banks[i][:])
+                else:
+                    nc.scalar.copy(out=staged, in_=banks[i][:])
+                nc.sync.dma_start(out=out[P * nt : P * (nt + 1), BANK * c : BANK * (c + 1)], in_=staged)
+
+        gather_words(0, 0)
+        gather_scales(0)
+        g00 = round_wf(0, 0, True)
+        g10 = round_wf(1, 0, False)
+        quantize_wf(0, 0, g00, 0, 2)
+        quantize_wf(1, 0, g10, 0, 2)
+        gather_words(1, 0)
+        gather_words(0, 1)
+        gather_scales(1)
+        gather_words(1, 1)
+        quantize_wf(0, 0, g00, 2, 4)
+        quantize_wf(1, 0, g10, 2, 4)
+
+        batches = [[0], [1], [2, 3], [4, 5], [6, 7]]
+        thin_with = {3: [0, 1], 4: [2, 3]}
+        for i, batch in enumerate(batches):
+            for k in batch:
+                first_product(k)
+            for k in batch:
+                magnitude(k)
+            for k in batch:
+                decay(k)
+            for k in thin_with.get(i, []):
+                thin(k)
+            for k in batch:
+                log_one_plus(k)
+            for k in batch:
+                finish(k)
+            for k in batch:
+                if k >= FUSED:
+                    weigh(k)
+            for k in batch:
+                scatter(k, k % 2 == 0)
+            if i == 0:
+                for a in range(PASSES):
+                    page = ring.tile([P, T2], F32, name="page", tag="window%d" % a, bufs=1, align_bytes=64)
+                    nc.vector.memset(page[:], 0.0)
+                    pages.append(page)
+                g01 = round_wf(0, 1, False)
+                g11 = round_wf(1, 1, False)
+                quantize_wf(0, 1, g01, 0, 4)
+                quantize_wf(1, 1, g11, 0, 4)
+            if i >= 3:
+                for c in range(CHUNKS):
+                    deplete_pair_in_place(nc.gpsimd, 0, c, i - 3)
+        for c in range(CHUNKS):
+            quantize_z(0, c)
+            stocks[1, c] = load_stock(1, c)
+        thin(4)
+        thin(5)
+        twos = {}
+        for c in range(EARLY):
+            twos[c] = keep.tile([P, 2, 2 * BANK], BF16, name="twos%d" % c)
+            deplete_pair(nc.gpsimd, twos[c][:, 0, :], 1, c, 0)
+        thin(6)
+        thin(7)
+        for c in range(CHUNKS + 1):
+            if c < EARLY:
+                deplete_pair(nc.vector, twos[c][:, 1, :], 1, c, 1)
+            elif c < CHUNKS:
+                deplete_whole(1, c)
+            if c > 0:
+                quantize_z(1, c - 1)
+                second_product(c - 1)
+            if c < EARLY:
+                nc.vector.tensor_copy(
+                    out=new_z(1, c)[:].bitcast(F32).rearrange("p (m u) -> p m u", u=2),
+                    in_=twos[c][:].rearrange("p u w -> p (u w)").bitcast(F32).rearrange("p (u m) -> p m u", u=2),
+                )

@@ -25,7 +25,6 @@ TILES = H // P
 CHUNKS = T2 // BANK
 HALVES = S // BANK
 PAGES = 4
-EARLY = 2
 FUSED = 2
 
 
@@ -38,28 +37,31 @@ def tile_list_parts_depletion_kernel(tc, tab_words, tab_scales, offs, wf, wgs, o
 
         parts = keep.tile([P, S // 16], U16, name="parts")
         bins = keep.tile([P, S // 16], U16, name="bins")
-        tab_w = [ring.tile([P, T], I32, name="tab_w%d" % a, tag="window%d" % a, bufs=1, align_bytes=64) for a in range(PASSES)]
+        tab_w = [ring.tile([P, T], I32, name="tab_w%d" % a, tag="big", bufs=7) for a in range(PASSES)]
         tab_s = keep.tile([P, T], U8, name="tab_s", align_bytes=64)
         v_w = [keep.tile([P, S], U32, name="v_w%d" % a, align_bytes=64) for a in range(PASSES)]
         v_s = keep.tile([P, S], U8, name="v_s", align_bytes=64)
         wf_w = {(a, b): keep.tile([P, KP], U32, name="wf_w%d%d" % (a, b), align_bytes=64) for a in range(PASSES) for b in range(PASSES)}
         wf_s = {(a, b): keep.tile([P, KP], U8, name="wf_s%d%d" % (a, b), align_bytes=64) for a in range(PASSES) for b in range(PASSES)}
         weights = keep.tile([P, S], F32, name="weights")
-        rates = [keep.tile([P, S], F32, name="rates%d" % i) for i in range(4)]
-        pages = [keep.tile([P, T2], F32, name="page%d" % i) for i in range(PAGES - PASSES)]
+        rates = [ring.tile([P, S], F32, name="rates%d" % i, tag="rates%d" % i, bufs=1, align_bytes=64) for i in range(4)]
+        pages = [keep.tile([P, T2], F32, name="page%d" % i) for i in range(PAGES - 2)]
         z_w = {(b, c): keep.tile([P, BANK], U32, name="z_w%d%d" % (b, c), align_bytes=64) for b in range(PASSES) for c in range(CHUNKS)}
-        z_s = {(b, c): keep.tile([P, BANK], U8, name="z_s%d%d" % (b, c), align_bytes=64) for b in range(PASSES) for c in range(CHUNKS)}
+        z_s = {(1, c): keep.tile([P, BANK], U8, name="z_s1%d" % c, align_bytes=64)[:] for c in range(CHUNKS)}
         wc_w = keep.tile([P, PASSES, 2 * N], U8, name="wc_w", align_bytes=64)
         wc_s = keep.tile([P, PASSES, N], U8, name="wc_s", align_bytes=64)
         banks = [psum.tile([P, BANK], F32, name="bank%d" % i) for i in range(8)]
 
         nc.vector.memset(tab_s[:].bitcast(I32), 0)
-        nc.vector.memset(wc_s[:].rearrange("p a n -> p (a n)").bitcast(I32), 0)
         for page in pages:
             nc.vector.memset(page[:], 0.0)
+        nc.gpsimd.memset(wc_s[:].rearrange("p a n -> p (a n)").bitcast(I32), 0)
 
         def load_wf(a, b):
-            raw = ring.tile([P, PACK, KP], F32, name="raw", tag="big", bufs=8)
+            if (a, b) == (1, 1):
+                raw = ring.tile([P, PACK, KP], F32, name="raw", tag="last_raw", bufs=1)
+            else:
+                raw = ring.tile([P, PACK, KP], F32, name="raw", tag="big", bufs=7)
             nc.sync.dma_start(out=raw[:], in_=wf[KP * a : KP * (a + 1), KP * b : KP * (b + 1)].rearrange("(p j) c -> p j c", j=PACK))
             return raw
 
@@ -67,22 +69,23 @@ def tile_list_parts_depletion_kernel(tc, tab_words, tab_scales, offs, wf, wgs, o
             nc.sync.dma_start(out=tab_w[a][:], in_=tab_words[a].rearrange("p t i -> p (t i)").bitcast(I32))
 
         def load_stock(b, c):
-            st = ring.tile([P, PACK, BANK], F32, name="st", tag="stock", bufs=5)
+            st = ring.tile([P, PACK, BANK], F32, name="st", tag="stock", bufs=6)
             nc.sync.dma_start(out=st[:], in_=stock[KP * b : KP * (b + 1), BANK * c : BANK * (c + 1)].rearrange("(p t) m -> p t m", t=PACK))
             return st
 
         nc.sync.dma_start(parts[:], offs)
-        load_table(0)
+        landing = [ring.tile([P, T // 4], I32, name="landing", tag="page%d" % i, bufs=1) for i in range(2)]
         for q in range(4):
-            nc.sync.dma_start(out=tab_s[32 * q : 32 * q + 4 * PASSES, :].bitcast(I32), in_=tab_scales[:, 4 * q : 4 * q + 4, :].bitcast(I32))
+            nc.sync.dma_start(out=landing[q // 2][32 * q : 32 * q + 4 * PASSES, :], in_=tab_scales[:, 4 * q : 4 * q + 4, :].bitcast(I32))
+        load_table(0)
         raws = {}
         raws[0, 0] = load_wf(0, 0)
         raws[1, 0] = load_wf(1, 0)
         load_table(1)
         nc.sync.dma_start(bins[:], offs2)
-        nc.sync.dma_start(out=weights[:], in_=wgs)
         raws[0, 1] = load_wf(0, 1)
         raws[1, 1] = load_wf(1, 1)
+        nc.sync.dma_start(out=weights[:], in_=wgs)
         nc.sync.dma_start(out=wc_w[:].bitcast(I32), in_=wc_words.rearrange("a p n -> p a n").bitcast(I32))
         for q in range(4):
             nc.sync.dma_start(out=wc_s[32 * q : 32 * q + 4, :, :].bitcast(I32), in_=wc_scales[:, 4 * q : 4 * q + 4, :].rearrange("a r n -> r a n").bitcast(I32))
@@ -102,11 +105,11 @@ def tile_list_parts_depletion_kernel(tc, tab_words, tab_scales, offs, wf, wgs, o
         def gather_scales(n):
             nc.vector.tensor_copy(v_s[:, half(n)], tab_s[:].indirect(parts[:, entries(n)]))
 
-        def round_wf(a, b, on_scalar):
+        def round_wf(a, b):
             grouped = ring.tile([P, PACK * KP], BF16, name="grouped", tag="bf16", bufs=7, align_bytes=64)
             dst = grouped[:].rearrange("p (t m j) -> p m j t", t=PACK, j=PACK)
             src = raws[a, b][:].rearrange("p j (m t) -> p m j t", t=PACK)
-            if on_scalar:
+            if (a, b) == (0, 0):
                 nc.scalar.copy(out=dst, in_=src)
             else:
                 nc.vector.tensor_copy(out=dst, in_=src)
@@ -146,9 +149,12 @@ def tile_list_parts_depletion_kernel(tc, tab_words, tab_scales, offs, wf, wgs, o
             for acc, part in halves(k):
                 nc.scalar.activation(out=part, in_=part, func=ACT.Ln, bias=1.0)
 
+        done = {}
+
         def finish(k):
-            for acc, part in halves(k):
-                nc.vector.scalar_tensor_tensor(out=part, in0=acc, scalar=0.0, in1=part, op0=ALU.max, op1=ALU.add)
+            done[k] = ring.tile([P, S], F32, name="first_rates", tag="last_raw", bufs=1) if k == 0 else rates[k % 4]
+            for n, (acc, part) in enumerate(halves(k)):
+                nc.vector.scalar_tensor_tensor(out=done[k][:, half(n)], in0=acc, scalar=0.0, in1=part, op0=ALU.max, op1=ALU.add)
 
         def weigh(k):
             for n in range(HALVES):
@@ -160,17 +166,17 @@ def tile_list_parts_depletion_kernel(tc, tab_words, tab_scales, offs, wf, wgs, o
             pieces = [(half(n), entries(n)) for n in range(HALVES)] if cut else [(slice(0, S), slice(0, S // 16))]
             for cols, names in pieces:
                 if k < FUSED:
-                    nc.vector.tensor_tensor(page[:].indirect(bins[:, names]), rates[k % 4][:, cols], weights[:, cols], ALU.mult)
+                    nc.vector.tensor_tensor(page[:].indirect(bins[:, names]), done[k][:, cols], weights[:, cols], ALU.mult)
                 else:
                     nc.vector.tensor_copy(page[:].indirect(bins[:, names]), rates[k % 4][:, cols])
 
         kept = {}
 
-        def thin(k):
+        def thin(k, chunks):
             b, t = divmod(k, PACK)
-            for c in range(CHUNKS):
+            for c in chunks:
                 if t == 0:
-                    kept[b, c] = ring.tile([P, PACK, BANK], F32, name="kept", tag="big", bufs=8)
+                    kept[b, c] = ring.tile([P, PACK, BANK], F32, name="kept", tag="big", bufs=7)
                 nc.scalar.activation(out=kept[b, c][:, t, :], in_=pages[k % PAGES][:, BANK * c : BANK * (c + 1)], func=ACT.Exp, scale=-1.0)
 
         zs = {}
@@ -192,14 +198,11 @@ def tile_list_parts_depletion_kernel(tc, tab_words, tab_scales, offs, wf, wgs, o
             ts = slice(2 * pair, 2 * pair + 2)
             deplete(engine, z[:].rearrange("p (m i t) -> p m t i", i=2, t=PACK)[:, :, ts, :], b, c, ts)
 
-        def deplete_pair(engine, dst, b, c, pair):
-            deplete(engine, dst.rearrange("p (m i t) -> p m t i", i=2, t=2), b, c, slice(2 * pair, 2 * pair + 2))
-
         def deplete_whole(b, c):
             deplete(nc.vector, new_z(b, c)[:].rearrange("p (m i t) -> p m t i", i=2, t=PACK), b, c, slice(0, PACK))
 
         def quantize_z(b, c):
-            nc.vector.quantize_mx(out=z_w[b, c][:].bitcast(FP8X4), scales=z_s[b, c][:], in_=zs[b, c][:])
+            nc.vector.quantize_mx(out=z_w[b, c][:].bitcast(FP8X4), scales=z_s[b, c], in_=zs[b, c][:])
 
         def second_product(c):
             for nt in range(N // P):
@@ -210,21 +213,28 @@ def tile_list_parts_depletion_kernel(tc, tab_words, tab_scales, offs, wf, wgs, o
                         lhsT=wc_w[:, b, 2 * P * nt : 2 * P * (nt + 1)].bitcast(FP4X4),
                         lhsT_scale=wc_s[:, b, P * nt : P * (nt + 1)],
                         rhs=z_w[b, c][:].bitcast(FP8X4),
-                        rhs_scale=z_s[b, c][:],
+                        rhs_scale=z_s[b, c],
                         start=(b == 0),
                         stop=(b == PASSES - 1),
                     )
-                staged = rates[i // 2][:, BANK * (i % 2) : BANK * (i % 2 + 1)]
+                staged = (rates[:3] + [weights])[i // 2][:, BANK * (i % 2) : BANK * (i % 2 + 1)]
                 if c == CHUNKS - 1 and nt % 2 == 1:
                     nc.vector.tensor_copy(out=staged, in_=banks[i][:])
                 else:
                     nc.scalar.copy(out=staged, in_=banks[i][:])
                 nc.sync.dma_start(out=out[P * nt : P * (nt + 1), BANK * c : BANK * (c + 1)], in_=staged)
 
+        for q in range(4):
+            rows = slice(32 * q, 32 * q + 4 * PASSES)
+            nc.vector.tensor_copy(out=tab_s[rows, :].bitcast(I32), in_=landing[q // 2][rows, :])
+        for i in range(2):
+            page = ring.tile([P, T2], F32, name="page", tag="page%d" % i, bufs=1)
+            nc.gpsimd.memset(page[:], 0.0)
+            pages.append(page)
         gather_words(0, 0)
         gather_scales(0)
-        g00 = round_wf(0, 0, True)
-        g10 = round_wf(1, 0, False)
+        g00 = round_wf(0, 0)
+        g10 = round_wf(1, 0)
         quantize_wf(0, 0, g00, 0, 2)
         quantize_wf(1, 0, g10, 0, 2)
         gather_words(1, 0)
@@ -233,18 +243,23 @@ def tile_list_parts_depletion_kernel(tc, tab_words, tab_scales, offs, wf, wgs, o
         gather_words(1, 1)
         quantize_wf(0, 0, g00, 2, 4)
         quantize_wf(1, 0, g10, 2, 4)
+        for a in range(PASSES):
+            quantize_wf(a, 1, round_wf(a, 1), 0, 4)
 
         batches = [[0], [1], [2, 3], [4, 5], [6, 7]]
-        thin_with = {3: [0, 1], 4: [2, 3]}
+        thin_with = {3: [(0, range(4)), (1, range(2))], 4: [(1, range(2, 4)), (2, range(4)), (3, range(1))]}
+        pairs_after = {3: [(0, 0), (1, 0)], 4: [(2, 0), (3, 0), (0, 1)]}
         for i, batch in enumerate(batches):
             for k in batch:
                 first_product(k)
             for k in batch:
                 magnitude(k)
+            for k, chunks in thin_with.get(i, []):
+                thin(k, chunks)
+            if i == 4:
+                scatter(5, False)
             for k in batch:
                 decay(k)
-            for k in thin_with.get(i, []):
-                thin(k)
             for k in batch:
                 log_one_plus(k)
             for k in batch:
@@ -252,41 +267,26 @@ def tile_list_parts_depletion_kernel(tc, tab_words, tab_scales, offs, wf, wgs, o
             for k in batch:
                 if k >= FUSED:
                     weigh(k)
-            for k in batch:
-                scatter(k, k % 2 == 0)
-            if i == 0:
-                for a in range(PASSES):
-                    page = ring.tile([P, T2], F32, name="page", tag="window%d" % a, bufs=1, align_bytes=64)
-                    nc.vector.memset(page[:], 0.0)
-                    pages.append(page)
-                g01 = round_wf(0, 1, False)
-                g11 = round_wf(1, 1, False)
-                quantize_wf(0, 1, g01, 0, 4)
-                quantize_wf(1, 1, g11, 0, 4)
-            if i >= 3:
-                for c in range(CHUNKS):
-                    deplete_pair_in_place(nc.gpsimd, 0, c, i - 3)
+            scatter(batch[0], batch[0] % 2 == 0)
+            if i == 2:
+                scatter(3, False)
+            for c, pair in pairs_after.get(i, []):
+                deplete_pair_in_place(nc.gpsimd, 0, c, pair)
+        thin(3, range(1, CHUNKS))
+        scatter(7, False)
+        for c in range(1, CHUNKS):
+            deplete_pair_in_place(nc.gpsimd, 0, c, 1)
+        late = ring.tile([P, T2], U8, name="late", tag="rates3", bufs=1, align_bytes=64)
         for c in range(CHUNKS):
-            quantize_z(0, c)
+            z_s[0, c] = late[:, half(c)]
             stocks[1, c] = load_stock(1, c)
-        thin(4)
-        thin(5)
-        twos = {}
-        for c in range(EARLY):
-            twos[c] = keep.tile([P, 2, 2 * BANK], BF16, name="twos%d" % c)
-            deplete_pair(nc.gpsimd, twos[c][:, 0, :], 1, c, 0)
-        thin(6)
-        thin(7)
-        for c in range(CHUNKS + 1):
-            if c < EARLY:
-                deplete_pair(nc.vector, twos[c][:, 1, :], 1, c, 1)
-            elif c < CHUNKS:
-                deplete_whole(1, c)
-            if c > 0:
-                quantize_z(1, c - 1)
-                second_product(c - 1)
-            if c < EARLY:
-                nc.vector.tensor_copy(
-                    out=new_z(1, c)[:].bitcast(F32).rearrange("p (m u) -> p m u", u=2),
-                    in_=twos[c][:].rearrange("p u w -> p (u w)").bitcast(F32).rearrange("p (u m) -> p m u", u=2),
-                )
+        for k in range(PACK, TILES):
+            thin(k, range(CHUNKS))
+        quantize_z(0, 0)
+        quantize_z(0, 1)
+        for c in range(CHUNKS):
+            deplete_whole(1, c)
+            if c + 2 < CHUNKS:
+                quantize_z(0, c + 2)
+            quantize_z(1, c)
+            second_product(c)

@@ -25,7 +25,8 @@ TILES = H // P
 CHUNKS = T2 // BANK
 HALVES = S // BANK
 PAGES = 4
-FUSED = 2
+CAP = 43.5
+KIB = 1024
 
 
 def tile_list_parts_depletion_kernel(tc, tab_words, tab_scales, offs, wf, wgs, offs2, stock, wc_words, wc_scales, out):
@@ -33,65 +34,28 @@ def tile_list_parts_depletion_kernel(tc, tab_words, tab_scales, offs, wf, wgs, o
     with ExitStack() as ctx:
         keep = ctx.enter_context(tc.tile_pool(name="keep", bufs=1))
         ring = ctx.enter_context(tc.tile_pool(name="ring", bufs=1))
+        arena = ctx.enter_context(tc.tile_pool(name="arena", bufs=1))
         psum = ctx.enter_context(tc.psum_pool(name="psum", bufs=1))
 
         parts = keep.tile([P, S // 16], U16, name="parts")
         bins = keep.tile([P, S // 16], U16, name="bins")
-        tab_w = [ring.tile([P, T], I32, name="tab_w%d" % a, tag="big", bufs=7) for a in range(PASSES)]
+        landing = keep.tile([P, T // 4], I32, name="landing")
         tab_s = keep.tile([P, T], U8, name="tab_s", align_bytes=64)
         v_w = [keep.tile([P, S], U32, name="v_w%d" % a, align_bytes=64) for a in range(PASSES)]
         v_s = keep.tile([P, S], U8, name="v_s", align_bytes=64)
-        wf_w = {(a, b): keep.tile([P, KP], U32, name="wf_w%d%d" % (a, b), align_bytes=64) for a in range(PASSES) for b in range(PASSES)}
-        wf_s = {(a, b): keep.tile([P, KP], U8, name="wf_s%d%d" % (a, b), align_bytes=64) for a in range(PASSES) for b in range(PASSES)}
-        weights = keep.tile([P, S], F32, name="weights")
-        rates = [ring.tile([P, S], F32, name="rates%d" % i, tag="rates%d" % i, bufs=1, align_bytes=64) for i in range(4)]
-        pages = [keep.tile([P, T2], F32, name="page%d" % i) for i in range(PAGES - 2)]
+        pages = [keep.tile([P, T2], F32, name="page%d" % i) for i in range(PAGES)]
         z_w = {(b, c): keep.tile([P, BANK], U32, name="z_w%d%d" % (b, c), align_bytes=64) for b in range(PASSES) for c in range(CHUNKS)}
-        z_s = {(1, c): keep.tile([P, BANK], U8, name="z_s1%d" % c, align_bytes=64)[:] for c in range(CHUNKS)}
+        z_s = {(b, c): keep.tile([P, BANK], U8, name="z_s%d%d" % (b, c), align_bytes=64) for b in range(PASSES) for c in range(CHUNKS)}
         wc_w = keep.tile([P, PASSES, 2 * N], U8, name="wc_w", align_bytes=64)
         wc_s = keep.tile([P, PASSES, N], U8, name="wc_s", align_bytes=64)
+        weights = ring.tile([P, S], F32, name="weights", tag="weights", align_bytes=64)
         banks = [psum.tile([P, BANK], F32, name="bank%d" % i) for i in range(8)]
 
-        nc.vector.memset(tab_s[:].bitcast(I32), 0)
-        for page in pages:
-            nc.vector.memset(page[:], 0.0)
-        nc.gpsimd.memset(wc_s[:].rearrange("p a n -> p (a n)").bitcast(I32), 0)
+        def placed(shape, dtype, name, kib):
+            return arena.tile(shape, dtype, name=name, offset=int(kib * KIB), align_bytes=64)
 
-        def load_wf(a, b):
-            if (a, b) == (1, 1):
-                raw = ring.tile([P, PACK, KP], F32, name="raw", tag="last_raw", bufs=1)
-            else:
-                raw = ring.tile([P, PACK, KP], F32, name="raw", tag="big", bufs=7)
-            nc.sync.dma_start(out=raw[:], in_=wf[KP * a : KP * (a + 1), KP * b : KP * (b + 1)].rearrange("(p j) c -> p j c", j=PACK))
-            return raw
-
-        def load_table(a):
-            nc.sync.dma_start(out=tab_w[a][:], in_=tab_words[a].rearrange("p t i -> p (t i)").bitcast(I32))
-
-        def load_stock(b, c):
-            st = ring.tile([P, PACK, BANK], F32, name="st", tag="stock", bufs=6)
-            nc.sync.dma_start(out=st[:], in_=stock[KP * b : KP * (b + 1), BANK * c : BANK * (c + 1)].rearrange("(p t) m -> p t m", t=PACK))
-            return st
-
-        nc.sync.dma_start(parts[:], offs)
-        landing = [ring.tile([P, T // 4], I32, name="landing", tag="page%d" % i, bufs=1) for i in range(2)]
-        for q in range(4):
-            nc.sync.dma_start(out=landing[q // 2][32 * q : 32 * q + 4 * PASSES, :], in_=tab_scales[:, 4 * q : 4 * q + 4, :].bitcast(I32))
-        load_table(0)
-        raws = {}
-        raws[0, 0] = load_wf(0, 0)
-        raws[1, 0] = load_wf(1, 0)
-        load_table(1)
-        nc.sync.dma_start(bins[:], offs2)
-        raws[0, 1] = load_wf(0, 1)
-        raws[1, 1] = load_wf(1, 1)
-        nc.sync.dma_start(out=weights[:], in_=wgs)
-        nc.sync.dma_start(out=wc_w[:].bitcast(I32), in_=wc_words.rearrange("a p n -> p a n").bitcast(I32))
-        for q in range(4):
-            nc.sync.dma_start(out=wc_s[32 * q : 32 * q + 4, :, :].bitcast(I32), in_=wc_scales[:, 4 * q : 4 * q + 4, :].rearrange("a r n -> r a n").bitcast(I32))
-        stocks = {}
-        for c in range(CHUNKS):
-            stocks[0, c] = load_stock(0, c)
+        def slot(shape, dtype, name, tag):
+            return ring.tile(shape, dtype, name=name, tag=tag, align_bytes=64)
 
         def half(n):
             return slice(BANK * n, BANK * (n + 1))
@@ -99,194 +63,249 @@ def tile_list_parts_depletion_kernel(tc, tab_words, tab_scales, offs, wf, wgs, o
         def entries(n):
             return slice(BANK // 16 * n, BANK // 16 * (n + 1))
 
+        nc.vector.memset(tab_s[:].bitcast(I32), 0)
+        for i, page in enumerate(pages):
+            (nc.vector if i < 2 else nc.gpsimd).memset(page[:], 0.0)
+        nc.gpsimd.memset(wc_s[:].rearrange("p a n -> p (a n)").bitcast(I32), 0)
+
+        floor = keep.tile([P, 1], F32, name="floor")
+        nc.scalar.activation(out=floor[:], in_=pages[0][:, 0:1], func=ACT.Sigmoid, bias=-CAP)
+
+        tab_w = [placed([P, T], I32, "tab_w%d" % a, 8 * a) for a in range(PASSES)]
+        raws = {(a, b): placed([P, PACK, KP], F32, "raw%d%d" % (a, b), 34 + 16 * b + 8 * a) for a in range(PASSES) for b in range(PASSES)}
+        RATES, ZZ, PAIRS = 82, 114, 130
+        wf_w = {ab: placed([P, KP], U32, "wf_w%d%d" % ab, kib) for ab, kib in (((0, 0), 42), ((1, 0), RATES + 8), ((0, 1), RATES + 16), ((1, 1), 16))}
+        wf_s = {ab: placed([P, KP], U8, "wf_s%d%d" % ab, kib) for ab, kib in (((0, 0), RATES + 4), ((1, 0), RATES + 12), ((0, 1), RATES + 20), ((1, 1), RATES + 24))}
+        first_s = placed([P, P], U8, "first_s", RATES)
+
+        first_w = placed([P, P], U32, "first_w", RATES + 1)
+
+        def wf_words(a, b, lo, hi):
+            return (first_w[:] if (a, b, lo) == (0, 0, 0) else wf_w[a, b][:, P * lo : P * hi]).bitcast(FP8X4)
+
+        def wf_scales(a, b, lo, hi):
+            return first_s[:] if (a, b, lo) == (1, 0, 0) else wf_s[a, b][:, P * lo : P * hi]
+
+        def load_wf(a, b):
+            nc.sync.dma_start(out=raws[a, b][:], in_=wf[KP * a : KP * (a + 1), KP * b : KP * (b + 1)].rearrange("(p j) c -> p j c", j=PACK))
+
+        stocks = {}
+
+        def load_stock(u, into):
+            b, pair = divmod(u, 2)
+            stocks[u] = into
+            nc.sync.dma_start(out=into, in_=stock[KP * b : KP * (b + 1), :].rearrange("(p u t) m -> p u t m", u=2, t=2)[:, pair, :, :])
+
+        nc.sync.dma_start(parts[:], offs)
+        for q in range(4):
+            nc.sync.dma_start(out=landing[32 * q : 32 * q + 4 * PASSES, :], in_=tab_scales[:, 4 * q : 4 * q + 4, :].bitcast(I32))
+        for a in range(PASSES):
+            nc.sync.dma_start(out=tab_w[a][:], in_=tab_words[a].rearrange("p t i -> p (t i)").bitcast(I32))
+            load_wf(a, 0)
+        nc.sync.dma_start(bins[:], offs2)
+        load_wf(0, 1)
+        load_wf(1, 1)
+        nc.sync.dma_start(out=weights[:], in_=wgs)
+        nc.sync.dma_start(out=wc_w[:].bitcast(I32), in_=wc_words.rearrange("a p n -> p a n").bitcast(I32))
+        for q in range(4):
+            nc.sync.dma_start(out=wc_s[32 * q : 32 * q + 4, :, :].bitcast(I32), in_=wc_scales[:, 4 * q : 4 * q + 4, :].rearrange("a r n -> r a n").bitcast(I32))
+        load_stock(0, placed([P, 2, T2], F32, "stock0", 18)[:])
+        load_stock(1, placed([P, 2, T2], F32, "stock1", 66)[:])
+
         def gather_words(a, n):
             nc.vector.tensor_copy(v_w[a][:, half(n)], tab_w[a][:].bitcast(U32).indirect(parts[:, entries(n)]))
 
         def gather_scales(n):
             nc.vector.tensor_copy(v_s[:, half(n)], tab_s[:].indirect(parts[:, entries(n)]))
 
-        def round_wf(a, b):
-            grouped = ring.tile([P, PACK * KP], BF16, name="grouped", tag="bf16", bufs=7, align_bytes=64)
+        def round_wf(copy, grouped, a, b, ts):
             dst = grouped[:].rearrange("p (t m j) -> p m j t", t=PACK, j=PACK)
             src = raws[a, b][:].rearrange("p j (m t) -> p m j t", t=PACK)
-            if (a, b) == (0, 0):
-                nc.scalar.copy(out=dst, in_=src)
-            else:
-                nc.vector.tensor_copy(out=dst, in_=src)
-            return grouped
+            copy(out=dst[:, :, :, ts], in_=src[:, :, :, ts])
 
-        def quantize_wf(a, b, grouped, lo, hi):
-            nc.vector.quantize_mx(out=wf_w[a, b][:, P * lo : P * hi].bitcast(FP8X4), scales=wf_s[a, b][:, P * lo : P * hi], in_=grouped[:, KP * lo : KP * hi])
+        def quantize_wf(grouped, a, b, lo, hi):
+            nc.vector.quantize_mx(out=wf_words(a, b, lo, hi), scales=wf_scales(a, b, lo, hi), in_=grouped[:, KP * lo : KP * hi])
+
+        def bank(k, n):
+            return banks[(HALVES * k + n) % 8]
 
         def first_product(k):
             b, t = divmod(k, PACK)
-            rows = slice(P * t, P * (t + 1))
-            for n in range(HALVES):
-                cols = slice(BANK * n, BANK * (n + 1))
-                for a in range(PASSES):
+            for a in range(PASSES):
+                for n in range(HALVES):
                     nc.tensor.matmul_mx(
-                        out=banks[(HALVES * k + n) % 8][:],
-                        lhsT=wf_w[a, b][:, rows].bitcast(FP8X4),
-                        lhsT_scale=wf_s[a, b][:, rows],
-                        rhs=v_w[a][:, cols].bitcast(FP8X4),
-                        rhs_scale=v_s[4 * a : P, cols],
+                        out=bank(k, n)[:],
+                        lhsT=wf_words(a, b, t, t + 1),
+                        lhsT_scale=wf_scales(a, b, t, t + 1),
+                        rhs=v_w[a][:, half(n)].bitcast(FP8X4),
+                        rhs_scale=v_s[4 * a : P, half(n)],
                         start=(a == 0),
                         stop=(a == PASSES - 1),
                     )
 
-        def halves(k):
-            return [(banks[(HALVES * k + n) % 8][:], rates[k % 4][:, BANK * n : BANK * (n + 1)]) for n in range(HALVES)]
+        rates = {}
+        survival = {}
 
-        def magnitude(k):
-            for acc, part in halves(k):
-                nc.scalar.activation(out=part, in_=acc, func=ACT.Abs)
-
-        def decay(k):
-            for acc, part in halves(k):
-                nc.scalar.activation(out=part, in_=part, func=ACT.Exp, scale=-1.0)
-
-        def log_one_plus(k):
-            for acc, part in halves(k):
-                nc.scalar.activation(out=part, in_=part, func=ACT.Ln, bias=1.0)
-
-        done = {}
-
-        def finish(k):
-            done[k] = ring.tile([P, S], F32, name="first_rates", tag="last_raw", bufs=1) if k == 0 else rates[k % 4]
-            for n, (acc, part) in enumerate(halves(k)):
-                nc.vector.scalar_tensor_tensor(out=done[k][:, half(n)], in0=acc, scalar=0.0, in1=part, op0=ALU.max, op1=ALU.add)
-
-        def weigh(k):
+        def squash(k):
+            survival[k] = placed([P, S], F32, "survival%d" % k, 4 * k + 18 * (k // PACK))
             for n in range(HALVES):
-                part = rates[k % 4][:, half(n)]
-                nc.gpsimd.tensor_tensor(part, part, weights[:, half(n)], ALU.mult)
+                nc.scalar.activation(out=survival[k][:, half(n)], in_=bank(k, n)[:], func=ACT.Sigmoid, scale=-1.0)
 
-        def scatter(k, cut):
-            page = pages[k % PAGES]
-            pieces = [(half(n), entries(n)) for n in range(HALVES)] if cut else [(slice(0, S), slice(0, S // 16))]
-            for cols, names in pieces:
-                if k < FUSED:
-                    nc.vector.tensor_tensor(page[:].indirect(bins[:, names]), done[k][:, cols], weights[:, cols], ALU.mult)
-                else:
-                    nc.vector.tensor_copy(page[:].indirect(bins[:, names]), rates[k % 4][:, cols])
+        def logarithm(k):
+            rates[k] = placed([P, S], F32, "rates%d" % k, RATES + 4 * k)
+            for n in range(HALVES):
+                nc.scalar.activation(out=rates[k][:, half(n)], in_=survival[k][:, half(n)], func=ACT.Ln, bias=floor[:])
+
+        def finish(k, n):
+            part = rates[k][:, half(n)]
+            nc.vector.scalar_tensor_tensor(out=part, in0=part, scalar=-1.0, in1=bank(k, n)[:], op0=ALU.mult, op1=ALU.max)
+
+        def weigh(k, cols):
+            nc.gpsimd.tensor_tensor(rates[k][:, cols], rates[k][:, cols], weights[:, cols], ALU.mult)
+
+        def scatter_weighing(k, n):
+            nc.vector.tensor_tensor(pages[k % PAGES][:].indirect(bins[:, entries(n)]), rates[k][:, half(n)], weights[:, half(n)], ALU.mult)
+
+        def scatter(k, cols):
+            nc.vector.tensor_copy(pages[k % PAGES][:].indirect(bins[:, cols.start // 16 : cols.stop // 16]), rates[k][:, cols])
 
         kept = {}
 
         def thin(k, chunks):
-            b, t = divmod(k, PACK)
-            for c in chunks:
-                if t == 0:
-                    kept[b, c] = ring.tile([P, PACK, BANK], F32, name="kept", tag="big", bufs=7)
-                nc.scalar.activation(out=kept[b, c][:, t, :], in_=pages[k % PAGES][:, BANK * c : BANK * (c + 1)], func=ACT.Exp, scale=-1.0)
+            u, t = divmod(k, 2)
+            if u not in kept:
+                kept[u] = placed([P, CHUNKS, 2, BANK], F32, "kept%d" % u, (2, 34, 2, PAIRS)[u])
+            cols = slice(BANK * chunks.start, BANK * chunks.stop)
+            nc.scalar.activation(out=kept[u][:, chunks.start : chunks.stop, t, :], in_=pages[k % PAGES][:, cols].rearrange("p (c m) -> p c m", m=BANK), func=ACT.Exp, scale=-1.0)
 
-        zs = {}
-
-        def new_z(b, c):
-            zs[b, c] = ring.tile([P, PACK * BANK], BF16, name="z", tag="bf16", bufs=7, align_bytes=64)
-            return zs[b, c]
-
-        def deplete(engine, dst, b, c, ts):
+        def deplete(engine, u, c):
+            b, pair = divmod(u, 2)
             engine.tensor_tensor(
-                dst,
-                kept[b, c][:, ts, :].rearrange("p t (m i) -> p m t i", i=2),
-                stocks[b, c][:, ts, :].rearrange("p t (m i) -> p m t i", i=2),
+                pairs[b][:, c, pair, :].rearrange("p (m i t) -> p m t i", i=4, t=2),
+                kept[u][:, c, :, :].rearrange("p t (m i) -> p m t i", i=4),
+                stocks[u][:, :, half(c)].rearrange("p t (m i) -> p m t i", i=4),
                 ALU.mult,
             )
 
-        def deplete_pair_in_place(engine, b, c, pair):
-            z = new_z(b, c) if pair == 0 else zs[b, c]
-            ts = slice(2 * pair, 2 * pair + 2)
-            deplete(engine, z[:].rearrange("p (m i t) -> p m t i", i=2, t=PACK)[:, :, ts, :], b, c, ts)
-
-        def deplete_whole(b, c):
-            deplete(nc.vector, new_z(b, c)[:].rearrange("p (m i t) -> p m t i", i=2, t=PACK), b, c, slice(0, PACK))
+        def weave(copy, word, b, c):
+            copy(
+                out=zz[:, c, :].bitcast(word).rearrange("p (m i u) -> p m u i", u=2, i=2),
+                in_=pairs[b][:, c, :, :].bitcast(word).rearrange("p u (m i) -> p m u i", i=2),
+            )
 
         def quantize_z(b, c):
-            nc.vector.quantize_mx(out=z_w[b, c][:].bitcast(FP8X4), scales=z_s[b, c], in_=zs[b, c][:])
+            nc.vector.quantize_mx(out=z_w[b, c][:].bitcast(FP8X4), scales=z_s[b, c][:], in_=zz[:, c, :])
 
-        def second_product(c):
-            for nt in range(N // P):
-                i = (N // P * c + nt) % 8
-                for b in range(PASSES):
-                    nc.tensor.matmul_mx(
-                        out=banks[i][:],
-                        lhsT=wc_w[:, b, 2 * P * nt : 2 * P * (nt + 1)].bitcast(FP4X4),
-                        lhsT_scale=wc_s[:, b, P * nt : P * (nt + 1)],
-                        rhs=z_w[b, c][:].bitcast(FP8X4),
-                        rhs_scale=z_s[b, c],
-                        start=(b == 0),
-                        stop=(b == PASSES - 1),
-                    )
-                staged = (rates[:3] + [weights])[i // 2][:, BANK * (i % 2) : BANK * (i % 2 + 1)]
-                if c == CHUNKS - 1 and nt % 2 == 1:
-                    nc.vector.tensor_copy(out=staged, in_=banks[i][:])
-                else:
-                    nc.scalar.copy(out=staged, in_=banks[i][:])
-                nc.sync.dma_start(out=out[P * nt : P * (nt + 1), BANK * c : BANK * (c + 1)], in_=staged)
+        def second_product(b, c, nt):
+            nc.tensor.matmul_mx(
+                out=banks[(N // P * c + nt) % 8][:],
+                lhsT=wc_w[:, b, 2 * P * nt : 2 * P * (nt + 1)].bitcast(FP4X4),
+                lhsT_scale=wc_s[:, b, P * nt : P * (nt + 1)],
+                rhs=z_w[b, c][:].bitcast(FP8X4),
+                rhs_scale=z_s[b, c][:],
+                start=(b == 0),
+                stop=(b == PASSES - 1),
+            )
+
+        def store(c, nt):
+            i = N // P * c + nt
+            staged = rates[i // 2][:, half(i % 2)]
+            if c == CHUNKS - 1 and nt % 2 == 1:
+                nc.vector.tensor_copy(out=staged, in_=banks[i % 8][:])
+            else:
+                nc.scalar.copy(out=staged, in_=banks[i % 8][:])
+            nc.sync.dma_start(out=out[P * nt : P * (nt + 1), half(c)], in_=staged)
 
         for q in range(4):
             rows = slice(32 * q, 32 * q + 4 * PASSES)
-            nc.vector.tensor_copy(out=tab_s[rows, :].bitcast(I32), in_=landing[q // 2][rows, :])
-        for i in range(2):
-            page = ring.tile([P, T2], F32, name="page", tag="page%d" % i, bufs=1)
-            nc.gpsimd.memset(page[:], 0.0)
-            pages.append(page)
+            nc.vector.tensor_copy(out=tab_s[rows, :].bitcast(I32), in_=landing[rows, :])
         gather_words(0, 0)
         gather_scales(0)
-        g00 = round_wf(0, 0)
-        g10 = round_wf(1, 0)
-        quantize_wf(0, 0, g00, 0, 2)
-        quantize_wf(1, 0, g10, 0, 2)
-        gather_words(1, 0)
         gather_words(0, 1)
         gather_scales(1)
+        gather_words(1, 0)
         gather_words(1, 1)
-        quantize_wf(0, 0, g00, 2, 4)
-        quantize_wf(1, 0, g10, 2, 4)
-        for a in range(PASSES):
-            quantize_wf(a, 1, round_wf(a, 1), 0, 4)
+        g00, g10, g01, g11 = [placed([P, PACK * KP], BF16, "grouped%d" % i, ZZ + 4 * i) for i in range(4)]
+        round_wf(nc.scalar.copy, g00, 0, 0, slice(0, PACK))
+        quantize_wf(g00, 0, 0, 0, 1)
+        round_wf(nc.vector.tensor_copy, g10, 1, 0, slice(0, 2))
+        quantize_wf(g10, 1, 0, 0, 1)
+        round_wf(nc.scalar.copy, g10, 1, 0, slice(2, PACK))
+        for lo, hi in ((1, 2), (2, 4)):
+            quantize_wf(g00, 0, 0, lo, hi)
+            quantize_wf(g10, 1, 0, lo, hi)
+        round_wf(nc.vector.tensor_copy, g01, 0, 1, slice(0, PACK))
+        quantize_wf(g01, 0, 1, 0, PACK)
+        round_wf(nc.vector.tensor_copy, g11, 1, 1, slice(0, PACK))
+        quantize_wf(g11, 1, 1, 0, PACK)
+        load_stock(2, placed([P, 2, T2], F32, "stock2", 50)[:])
+        zz = placed([P, CHUNKS, PACK * BANK], BF16, "zz", ZZ)
+        pairs = {0: placed([P, CHUNKS, 2, 2 * BANK], BF16, "pairs0", PAIRS)}
 
-        batches = [[0], [1], [2, 3], [4, 5], [6, 7]]
-        thin_with = {3: [(0, range(4)), (1, range(2))], 4: [(1, range(2, 4)), (2, range(4)), (3, range(1))]}
-        pairs_after = {3: [(0, 0), (1, 0)], 4: [(2, 0), (3, 0), (0, 1)]}
-        for i, batch in enumerate(batches):
-            for k in batch:
-                first_product(k)
-            for k in batch:
-                magnitude(k)
-            for k, chunks in thin_with.get(i, []):
-                thin(k, chunks)
-            if i == 4:
-                scatter(5, False)
-            for k in batch:
-                decay(k)
-            for k in batch:
-                log_one_plus(k)
-            for k in batch:
-                finish(k)
-            for k in batch:
-                if k >= FUSED:
-                    weigh(k)
-            scatter(batch[0], batch[0] % 2 == 0)
-            if i == 2:
-                scatter(3, False)
-            for c, pair in pairs_after.get(i, []):
-                deplete_pair_in_place(nc.gpsimd, 0, c, pair)
-        thin(3, range(1, CHUNKS))
-        scatter(7, False)
-        for c in range(1, CHUNKS):
-            deplete_pair_in_place(nc.gpsimd, 0, c, 1)
-        late = ring.tile([P, T2], U8, name="late", tag="rates3", bufs=1, align_bytes=64)
-        for c in range(CHUNKS):
-            z_s[0, c] = late[:, half(c)]
-            stocks[1, c] = load_stock(1, c)
+        for k in range(PACK):
+            first_product(k)
+        squash(0)
+        logarithm(0)
+        for n in range(HALVES):
+            finish(0, n)
+            scatter_weighing(0, n)
+        squash(1)
+        squash(2)
+        squash(3)
+        for k in (1, 2, 3):
+            logarithm(k)
+        finish(1, 0)
+        scatter_weighing(1, 0)
+        whole = slice(0, S)
+        finish(1, 1)
+        weigh(1, half(1))
+        for k in (2, 3):
+            for n in range(HALVES):
+                finish(k, n)
+            weigh(k, whole)
+        scatter(1, half(1))
+        for k in (2, 3):
+            scatter(k, whole)
         for k in range(PACK, TILES):
-            thin(k, range(CHUNKS))
-        quantize_z(0, 0)
-        quantize_z(0, 1)
+            first_product(k)
+            squash(k)
         for c in range(CHUNKS):
-            deplete_whole(1, c)
-            if c + 2 < CHUNKS:
-                quantize_z(0, c + 2)
+            thin(0, range(c, c + 1))
+            thin(1, range(c, c + 1))
+            if c < CHUNKS - 1:
+                deplete(nc.gpsimd, 0, c)
+        for k in range(PACK, TILES):
+            logarithm(k)
+            for n in range(HALVES):
+                finish(k, n)
+            weigh(k, whole)
+            if k == PACK:
+                deplete(nc.gpsimd, 0, CHUNKS - 1)
+        load_stock(3, placed([P, 2, T2], F32, "stock3", 18)[:])
+        for k in range(PACK, TILES):
+            scatter(k, whole)
+            thin(k - 2, range(CHUNKS))
+        for c in range(CHUNKS):
+            deplete(nc.gpsimd, 1, c)
+            weave(nc.scalar.copy, U32, 0, c)
+            quantize_z(0, c)
+        pairs[1] = placed([P, CHUNKS, 2, 2 * BANK], BF16, "pairs1", 34)
+        for c in range(CHUNKS):
+            deplete(nc.gpsimd, 2, c)
+        thin(TILES - 2, range(CHUNKS))
+        for c in range(CHUNKS):
+            thin(TILES - 1, range(c, c + 1))
+        for c in range(2):
+            for nt in range(N // P):
+                second_product(0, c, nt)
+        deplete(nc.vector, 3, 0)
+        for c in range(CHUNKS):
+            weave(nc.vector.tensor_copy, F32, 1, c)
+            if c + 1 < CHUNKS:
+                deplete(nc.vector, 3, c + 1)
             quantize_z(1, c)
-            second_product(c)
+            for nt in range(N // P):
+                if c >= 2:
+                    second_product(0, c, nt)
+                second_product(1, c, nt)
+                store(c, nt)

@@ -27,6 +27,7 @@ HALVES = S // BANK
 PAGES = 4
 CAP = 43.5
 KIB = 1024
+RUN = 4
 
 
 def tile_list_parts_depletion_kernel(tc, tab_words, tab_scales, offs, wf, wgs, offs2, stock, wc_words, wc_scales, out):
@@ -41,10 +42,9 @@ def tile_list_parts_depletion_kernel(tc, tab_words, tab_scales, offs, wf, wgs, o
         bins = keep.tile([P, S // 16], U16, name="bins")
         landing = keep.tile([P, T // 4], I32, name="landing")
         tab_s = keep.tile([P, T], U8, name="tab_s", align_bytes=64)
-        v_w = [keep.tile([P, S], U32, name="v_w%d" % a, align_bytes=64) for a in range(PASSES)]
-        v_s = keep.tile([P, S], U8, name="v_s", align_bytes=64)
+        v_w = {an: keep.tile([P, BANK], U32, name="v_w%d%d" % an, align_bytes=64) for an in ((0, 0), (0, 1), (1, 0))}
+        v_s = {0: keep.tile([P, BANK], U8, name="v_s0", align_bytes=64)}
         pages = [keep.tile([P, T2], F32, name="page%d" % i) for i in range(PAGES)]
-        z_w = {(b, c): keep.tile([P, BANK], U32, name="z_w%d%d" % (b, c), align_bytes=64) for b in range(PASSES) for c in range(CHUNKS)}
         z_s = {(b, c): keep.tile([P, BANK], U8, name="z_s%d%d" % (b, c), align_bytes=64) for b in range(PASSES) for c in range(CHUNKS)}
         wc_w = keep.tile([P, PASSES, 2 * N], U8, name="wc_w", align_bytes=64)
         wc_s = keep.tile([P, PASSES, N], U8, name="wc_s", align_bytes=64)
@@ -72,29 +72,28 @@ def tile_list_parts_depletion_kernel(tc, tab_words, tab_scales, offs, wf, wgs, o
         nc.scalar.activation(out=floor[:], in_=pages[0][:, 0:1], func=ACT.Sigmoid, bias=-CAP)
 
         tab_w = [placed([P, T], I32, "tab_w%d" % a, 8 * a) for a in range(PASSES)]
-        raws = {(a, b): placed([P, PACK, KP], F32, "raw%d%d" % (a, b), 34 + 16 * b + 8 * a) for a in range(PASSES) for b in range(PASSES)}
-        RATES, ZZ, PAIRS = 82, 114, 130
-        wf_w = {ab: placed([P, KP], U32, "wf_w%d%d" % ab, kib) for ab, kib in (((0, 0), 42), ((1, 0), RATES + 8), ((0, 1), RATES + 16), ((1, 1), 16))}
-        wf_s = {ab: placed([P, KP], U8, "wf_s%d%d" % ab, kib) for ab, kib in (((0, 0), RATES + 4), ((1, 0), RATES + 12), ((0, 1), RATES + 20), ((1, 1), RATES + 24))}
-        first_s = placed([P, P], U8, "first_s", RATES)
-
-        first_w = placed([P, P], U32, "first_w", RATES + 1)
-
-        def wf_words(a, b, lo, hi):
-            return (first_w[:] if (a, b, lo) == (0, 0, 0) else wf_w[a, b][:, P * lo : P * hi]).bitcast(FP8X4)
-
-        def wf_scales(a, b, lo, hi):
-            return first_s[:] if (a, b, lo) == (1, 0, 0) else wf_s[a, b][:, P * lo : P * hi]
+        KEPT, SECOND, RATES, ZZ, LATE = 64, 80, 128, 160, 176
+        raws = {ab: placed([P, PACK, KP], F32, "raw%d%d" % ab, kib) for ab, kib in (((0, 0), 16), ((1, 0), RATES + 8), ((0, 1), KEPT), ((1, 1), KEPT + 8))}
+        wf_w = {(a, 0, 0): placed([P, 2 * P], U32, "wf_w%d00" % a, 24 + a) for a in range(PASSES)}
+        wf_s = {(a, 0, 0): placed([P, 2 * P], U8, "wf_s%d00" % a, 26 + a) for a in range(PASSES)}
+        wf_w[0, 0, 2] = placed([P, 2 * P], U32, "wf_w002", RATES + 12)
+        wf_w[1, 0, 2] = placed([P, 2 * P], U32, "wf_w102", RATES + 8)
+        wf_s[0, 0, 2] = placed([P, 2 * P], U8, "wf_s002", RATES + 2)
+        wf_s[1, 0, 2] = placed([P, 2 * P], U8, "wf_s102", RATES + 6)
+        wf_w[0, 1, 0] = placed([P, KP], U32, "wf_w01", RATES + 16)
+        wf_w[1, 1, 0] = placed([P, KP], U32, "wf_w11", KEPT)
+        wf_s[0, 1, 0] = placed([P, KP], U8, "wf_s01", RATES + 20)
+        wf_s[1, 1, 0] = placed([P, KP], U8, "wf_s11", RATES + 24)
+        v_s[1] = placed([P, BANK], U8, "v_s1", LATE)
+        v_w[1, 1] = placed([P, BANK], U32, "v_w11", LATE + 0.5)
 
         def load_wf(a, b):
             nc.sync.dma_start(out=raws[a, b][:], in_=wf[KP * a : KP * (a + 1), KP * b : KP * (b + 1)].rearrange("(p j) c -> p j c", j=PACK))
 
-        stocks = {}
+        stocks = [placed([P, PACK, T2], F32, "stock%d" % b, 32 + 64 * b) for b in range(PASSES)]
 
-        def load_stock(u, into):
-            b, pair = divmod(u, 2)
-            stocks[u] = into
-            nc.sync.dma_start(out=into, in_=stock[KP * b : KP * (b + 1), :].rearrange("(p u t) m -> p u t m", u=2, t=2)[:, pair, :, :])
+        def load_stock(b, ts):
+            nc.sync.dma_start(out=stocks[b][:, ts, :], in_=stock[KP * b : KP * (b + 1), :].rearrange("(p t) m -> p t m", t=PACK)[:, ts, :])
 
         nc.sync.dma_start(parts[:], offs)
         for q in range(4):
@@ -109,36 +108,41 @@ def tile_list_parts_depletion_kernel(tc, tab_words, tab_scales, offs, wf, wgs, o
         nc.sync.dma_start(out=wc_w[:].bitcast(I32), in_=wc_words.rearrange("a p n -> p a n").bitcast(I32))
         for q in range(4):
             nc.sync.dma_start(out=wc_s[32 * q : 32 * q + 4, :, :].bitcast(I32), in_=wc_scales[:, 4 * q : 4 * q + 4, :].rearrange("a r n -> r a n").bitcast(I32))
-        load_stock(0, placed([P, 2, T2], F32, "stock0", 18)[:])
-        load_stock(1, placed([P, 2, T2], F32, "stock1", 66)[:])
+        for b in range(PASSES):
+            load_stock(b, slice(0, 2))
+            load_stock(b, slice(2, 4))
 
         def gather_words(a, n):
-            nc.vector.tensor_copy(v_w[a][:, half(n)], tab_w[a][:].bitcast(U32).indirect(parts[:, entries(n)]))
+            nc.vector.tensor_copy(v_w[a, n][:], tab_w[a][:].bitcast(U32).indirect(parts[:, entries(n)]))
 
         def gather_scales(n):
-            nc.vector.tensor_copy(v_s[:, half(n)], tab_s[:].indirect(parts[:, entries(n)]))
+            nc.vector.tensor_copy(v_s[n][:], tab_s[:].indirect(parts[:, entries(n)]))
 
-        def round_wf(copy, grouped, a, b, ts):
-            dst = grouped[:].rearrange("p (t m j) -> p m j t", t=PACK, j=PACK)
+        grouped = {}
+
+        def round_wf(copy, a, b, lo, hi, kib):
+            grouped[a, b, lo] = placed([P, (hi - lo) * KP], BF16, "grouped%d%d%d" % (a, b, lo), kib)
             src = raws[a, b][:].rearrange("p j (m t) -> p m j t", t=PACK)
-            copy(out=dst[:, :, :, ts], in_=src[:, :, :, ts])
+            copy(out=grouped[a, b, lo][:].rearrange("p (t m j) -> p m j t", t=hi - lo, j=PACK), in_=src[:, :, :, lo:hi])
 
-        def quantize_wf(grouped, a, b, lo, hi):
-            nc.vector.quantize_mx(out=wf_words(a, b, lo, hi), scales=wf_scales(a, b, lo, hi), in_=grouped[:, KP * lo : KP * hi])
+        def quantize_wf(a, b, lo):
+            nc.vector.quantize_mx(out=wf_w[a, b, lo][:].bitcast(FP8X4), scales=wf_s[a, b, lo][:], in_=grouped[a, b, lo][:])
 
         def bank(k, n):
             return banks[(HALVES * k + n) % 8]
 
-        def first_product(k):
-            b, t = divmod(k, PACK)
+        def first_product(units):
             for a in range(PASSES):
-                for n in range(HALVES):
+                for k, n in units:
+                    b, t = divmod(k, PACK)
+                    lo = 2 * (t // 2) if b == 0 else 0
+                    rows = slice(P * (t - lo), P * (t - lo + 1))
                     nc.tensor.matmul_mx(
                         out=bank(k, n)[:],
-                        lhsT=wf_words(a, b, t, t + 1),
-                        lhsT_scale=wf_scales(a, b, t, t + 1),
-                        rhs=v_w[a][:, half(n)].bitcast(FP8X4),
-                        rhs_scale=v_s[4 * a : P, half(n)],
+                        lhsT=wf_w[a, b, lo][:, rows].bitcast(FP8X4),
+                        lhsT_scale=wf_s[a, b, lo][:, rows],
+                        rhs=v_w[a, n][:].bitcast(FP8X4),
+                        rhs_scale=v_s[n][4 * a : P, :],
                         start=(a == 0),
                         stop=(a == PASSES - 1),
                     )
@@ -146,54 +150,70 @@ def tile_list_parts_depletion_kernel(tc, tab_words, tab_scales, offs, wf, wgs, o
         rates = {}
         survival = {}
 
-        def squash(k):
-            survival[k] = placed([P, S], F32, "survival%d" % k, 4 * k + 18 * (k // PACK))
-            for n in range(HALVES):
-                nc.scalar.activation(out=survival[k][:, half(n)], in_=bank(k, n)[:], func=ACT.Sigmoid, scale=-1.0)
+        def squash(k, n):
+            if k not in survival:
+                survival[k] = placed([P, S], F32, "survival%d" % k, 4 * k if k < PACK else SECOND + 4 * (k - PACK))
+            nc.scalar.activation(out=survival[k][:, half(n)], in_=bank(k, n)[:], func=ACT.Sigmoid, scale=-1.0)
 
-        def logarithm(k):
-            rates[k] = placed([P, S], F32, "rates%d" % k, RATES + 4 * k)
-            for n in range(HALVES):
-                nc.scalar.activation(out=rates[k][:, half(n)], in_=survival[k][:, half(n)], func=ACT.Ln, bias=floor[:])
+        def logarithm(k, n):
+            if k < 2:
+                rates[k, n] = placed([P, BANK], F32, "rates%d%d" % (k, n), RATES + 4 * k + 2 * n)[:]
+            elif n == 0:
+                rates[k] = placed([P, S], F32, "rates%d" % k, RATES + 4 * k)
+                rates[k, 0], rates[k, 1] = rates[k][:, half(0)], rates[k][:, half(1)]
+            nc.scalar.activation(out=rates[k, n], in_=survival[k][:, half(n)], func=ACT.Ln, bias=floor[:])
 
         def finish(k, n):
-            part = rates[k][:, half(n)]
-            nc.vector.scalar_tensor_tensor(out=part, in0=part, scalar=-1.0, in1=bank(k, n)[:], op0=ALU.mult, op1=ALU.max)
+            nc.vector.scalar_tensor_tensor(out=rates[k, n], in0=rates[k, n], scalar=-1.0, in1=bank(k, n)[:], op0=ALU.mult, op1=ALU.max)
 
-        def weigh(k, cols):
-            nc.gpsimd.tensor_tensor(rates[k][:, cols], rates[k][:, cols], weights[:, cols], ALU.mult)
+        def weigh(part, cols):
+            nc.gpsimd.tensor_tensor(part, part, weights[:, cols], ALU.mult)
 
         def scatter_weighing(k, n):
-            nc.vector.tensor_tensor(pages[k % PAGES][:].indirect(bins[:, entries(n)]), rates[k][:, half(n)], weights[:, half(n)], ALU.mult)
+            nc.vector.tensor_tensor(pages[k % PAGES][:].indirect(bins[:, entries(n)]), rates[k, n], weights[:, half(n)], ALU.mult)
 
-        def scatter(k, cols):
-            nc.vector.tensor_copy(pages[k % PAGES][:].indirect(bins[:, cols.start // 16 : cols.stop // 16]), rates[k][:, cols])
+        def scatter(k, part, names):
+            nc.vector.tensor_copy(pages[k % PAGES][:].indirect(bins[:, names]), part)
 
         kept = {}
 
-        def thin(k, chunks):
-            u, t = divmod(k, 2)
-            if u not in kept:
-                kept[u] = placed([P, CHUNKS, 2, BANK], F32, "kept%d" % u, (2, 34, 2, PAIRS)[u])
-            cols = slice(BANK * chunks.start, BANK * chunks.stop)
-            nc.scalar.activation(out=kept[u][:, chunks.start : chunks.stop, t, :], in_=pages[k % PAGES][:, cols].rearrange("p (c m) -> p c m", m=BANK), func=ACT.Exp, scale=-1.0)
+        def thin_early(k):
+            kept[k] = placed([P, T2], F32, "kept%d" % k, KEPT + 8 * k)
+            nc.scalar.activation(out=kept[k][:], in_=pages[k][:], func=ACT.Exp, scale=-1.0)
 
-        def deplete(engine, u, c):
-            b, pair = divmod(u, 2)
-            engine.tensor_tensor(
-                pairs[b][:, c, pair, :].rearrange("p (m i t) -> p m t i", i=4, t=2),
-                kept[u][:, c, :, :].rearrange("p t (m i) -> p m t i", i=4),
-                stocks[u][:, :, half(c)].rearrange("p t (m i) -> p m t i", i=4),
+        def thin_late(k, c):
+            nc.scalar.activation(out=kept_late[:, c, k - PACK, :], in_=pages[k % PAGES][:, half(c)], func=ACT.Exp, scale=-1.0)
+
+        def planes(chunks):
+            return kept_late[:, chunks, 2:4, :].rearrange("p c u m -> p c (u m)").bitcast(BF16).rearrange("p c (t m) -> p c t m", t=PACK)
+
+        def deplete_plane(t, chunks):
+            cols = slice(BANK * chunks.start, BANK * chunks.stop)
+            nc.gpsimd.tensor_tensor(
+                planes(chunks)[:, :, t, :],
+                kept[t][:, cols].rearrange("p (c m) -> p c m", m=BANK),
+                stocks[0][:, t, cols].rearrange("p (c m) -> p c m", m=BANK),
                 ALU.mult,
             )
 
-        def weave(copy, word, b, c):
-            copy(
-                out=zz[:, c, :].bitcast(word).rearrange("p (m i u) -> p m u i", u=2, i=2),
-                in_=pairs[b][:, c, :, :].bitcast(word).rearrange("p u (m i) -> p m u i", i=2),
+        def interleave(c):
+            nc.scalar.copy(
+                out=zz[:, c, :].rearrange("p (m i t) -> p m t i", i=RUN, t=PACK),
+                in_=planes(slice(c, c + 1))[:, 0, :, :].rearrange("p t (m i) -> p m t i", i=RUN),
             )
 
+        def deplete_whole(c):
+            nc.vector.tensor_tensor(
+                zz[:, c, :].rearrange("p (m i t) -> p m t i", i=RUN, t=PACK),
+                kept_late[:, c, :, :].rearrange("p t (m i) -> p m t i", i=RUN),
+                stocks[1][:, :, half(c)].rearrange("p t (m i) -> p m t i", i=RUN),
+                ALU.mult,
+            )
+
+        z_w = {}
+
         def quantize_z(b, c):
+            z_w[b, c] = placed([P, BANK], U32, "z_w%d%d" % (b, c), KEPT + 8 * b + 2 * c)
             nc.vector.quantize_mx(out=z_w[b, c][:].bitcast(FP8X4), scales=z_s[b, c][:], in_=zz[:, c, :])
 
         def second_product(b, c, nt):
@@ -209,7 +229,7 @@ def tile_list_parts_depletion_kernel(tc, tab_words, tab_scales, offs, wf, wgs, o
 
         def store(c, nt):
             i = N // P * c + nt
-            staged = rates[i // 2][:, half(i % 2)]
+            staged = rates[divmod(i, 2)]
             if c == CHUNKS - 1 and nt % 2 == 1:
                 nc.vector.tensor_copy(out=staged, in_=banks[i % 8][:])
             else:
@@ -222,87 +242,81 @@ def tile_list_parts_depletion_kernel(tc, tab_words, tab_scales, offs, wf, wgs, o
         gather_words(0, 0)
         gather_scales(0)
         gather_words(0, 1)
-        gather_scales(1)
         gather_words(1, 0)
+        round_wf(nc.scalar.copy, 0, 0, 0, 2, ZZ)
+        round_wf(nc.scalar.copy, 0, 0, 2, 4, ZZ + 2)
+        quantize_wf(0, 0, 0)
+        round_wf(nc.vector.tensor_copy, 1, 0, 0, 2, LATE + 0.4375)
+        quantize_wf(1, 0, 0)
+        round_wf(nc.scalar.copy, 1, 0, 2, 4, ZZ + 4)
+        gather_scales(1)
         gather_words(1, 1)
-        g00, g10, g01, g11 = [placed([P, PACK * KP], BF16, "grouped%d" % i, ZZ + 4 * i) for i in range(4)]
-        round_wf(nc.scalar.copy, g00, 0, 0, slice(0, PACK))
-        quantize_wf(g00, 0, 0, 0, 1)
-        round_wf(nc.vector.tensor_copy, g10, 1, 0, slice(0, 2))
-        quantize_wf(g10, 1, 0, 0, 1)
-        round_wf(nc.scalar.copy, g10, 1, 0, slice(2, PACK))
-        for lo, hi in ((1, 2), (2, 4)):
-            quantize_wf(g00, 0, 0, lo, hi)
-            quantize_wf(g10, 1, 0, lo, hi)
-        round_wf(nc.vector.tensor_copy, g01, 0, 1, slice(0, PACK))
-        quantize_wf(g01, 0, 1, 0, PACK)
-        round_wf(nc.vector.tensor_copy, g11, 1, 1, slice(0, PACK))
-        quantize_wf(g11, 1, 1, 0, PACK)
-        load_stock(2, placed([P, 2, T2], F32, "stock2", 50)[:])
+        for a in range(PASSES):
+            quantize_wf(a, 0, 2)
+        for a in range(PASSES):
+            round_wf(nc.vector.tensor_copy, a, 1, 0, PACK, ZZ + 8 + 4 * a)
+            quantize_wf(a, 1, 0)
         zz = placed([P, CHUNKS, PACK * BANK], BF16, "zz", ZZ)
-        pairs = {0: placed([P, CHUNKS, 2, 2 * BANK], BF16, "pairs0", PAIRS)}
 
-        for k in range(PACK):
-            first_product(k)
-        squash(0)
-        logarithm(0)
-        for n in range(HALVES):
-            finish(0, n)
-            scatter_weighing(0, n)
-        squash(1)
-        squash(2)
-        squash(3)
-        for k in (1, 2, 3):
-            logarithm(k)
-        finish(1, 0)
-        scatter_weighing(1, 0)
-        whole = slice(0, S)
+        opening = [(0, 0), (1, 0)]
+        first_product(opening)
+        for step in (squash, logarithm):
+            for k, n in opening:
+                step(k, n)
+        for k, n in opening:
+            finish(k, n)
+            scatter_weighing(k, n)
+        second = [(0, 1), (1, 1)] + [(k, n) for k in (2, 3) for n in range(HALVES)]
+        for unit in second:
+            first_product([unit])
+        for step in (squash, logarithm):
+            for k, n in second:
+                step(k, n)
+        finish(0, 1)
+        scatter_weighing(0, 1)
+        whole, all_entries = slice(0, S), slice(0, S // 16)
         finish(1, 1)
-        weigh(1, half(1))
+        weigh(rates[1, 1], half(1))
         for k in (2, 3):
             for n in range(HALVES):
                 finish(k, n)
-            weigh(k, whole)
-        scatter(1, half(1))
+            weigh(rates[k][:], whole)
+        scatter(1, rates[1, 1], entries(1))
         for k in (2, 3):
-            scatter(k, whole)
+            scatter(k, rates[k][:], all_entries)
         for k in range(PACK, TILES):
-            first_product(k)
-            squash(k)
-        for c in range(CHUNKS):
-            thin(0, range(c, c + 1))
-            thin(1, range(c, c + 1))
-            if c < CHUNKS - 1:
-                deplete(nc.gpsimd, 0, c)
-        for k in range(PACK, TILES):
-            logarithm(k)
             for n in range(HALVES):
-                finish(k, n)
-            weigh(k, whole)
-            if k == PACK:
-                deplete(nc.gpsimd, 0, CHUNKS - 1)
-        load_stock(3, placed([P, 2, T2], F32, "stock3", 18)[:])
+                first_product([(k, n)])
+                squash(k, n)
+        kept_late = placed([P, CHUNKS, PACK, BANK], F32, "kept_late", 0)
+        for k in (0, 1):
+            thin_early(k)
+            deplete_plane(k, slice(0, CHUNKS))
         for k in range(PACK, TILES):
-            scatter(k, whole)
-            thin(k - 2, range(CHUNKS))
+            for n in range(HALVES):
+                logarithm(k, n)
+                finish(k, n)
+            weigh(rates[k][:], whole)
+        thin_early(2)
+        thin_early(3)
+        deplete_plane(2, slice(0, CHUNKS))
+        for k in range(PACK, TILES):
+            scatter(k, rates[k][:], all_entries)
+        for k in (4, 5):
+            for c in range(CHUNKS):
+                thin_late(k, c)
         for c in range(CHUNKS):
-            deplete(nc.gpsimd, 1, c)
-            weave(nc.scalar.copy, U32, 0, c)
+            deplete_plane(3, slice(c, c + 1))
+            interleave(c)
             quantize_z(0, c)
-        pairs[1] = placed([P, CHUNKS, 2, 2 * BANK], BF16, "pairs1", 34)
-        for c in range(CHUNKS):
-            deplete(nc.gpsimd, 2, c)
-        thin(TILES - 2, range(CHUNKS))
-        for c in range(CHUNKS):
-            thin(TILES - 1, range(c, c + 1))
+        for k in (6, 7):
+            for c in range(CHUNKS):
+                thin_late(k, c)
         for c in range(2):
             for nt in range(N // P):
                 second_product(0, c, nt)
-        deplete(nc.vector, 3, 0)
         for c in range(CHUNKS):
-            weave(nc.vector.tensor_copy, F32, 1, c)
-            if c + 1 < CHUNKS:
-                deplete(nc.vector, 3, c + 1)
+            deplete_whole(c)
             quantize_z(1, c)
             for nt in range(N // P):
                 if c >= 2:

@@ -44,7 +44,7 @@ def tile_list_parts_depletion_kernel(tc, tab_words, tab_scales, offs, wf, wgs, o
         tab_s = keep.tile([P, T], U8, name="tab_s", align_bytes=64)
         v_w = {an: keep.tile([P, BANK], U32, name="v_w%d%d" % an, align_bytes=64) for an in ((0, 0), (0, 1), (1, 0))}
         v_s = {0: keep.tile([P, BANK], U8, name="v_s0", align_bytes=64)}
-        pages = [keep.tile([P, T2], F32, name="page%d" % i) for i in range(PAGES)]
+        pages = [keep.tile([P, T2], F32, name="page%d" % i) for i in range(2)]
         z_s = {(b, c): keep.tile([P, BANK], U8, name="z_s%d%d" % (b, c), align_bytes=64) for b in range(PASSES) for c in range(CHUNKS)}
         wc_w = keep.tile([P, PASSES, 2 * N], U8, name="wc_w", align_bytes=64)
         wc_s = keep.tile([P, PASSES, N], U8, name="wc_s", align_bytes=64)
@@ -64,15 +64,15 @@ def tile_list_parts_depletion_kernel(tc, tab_words, tab_scales, offs, wf, wgs, o
             return slice(BANK // 16 * n, BANK // 16 * (n + 1))
 
         nc.vector.memset(tab_s[:].bitcast(I32), 0)
-        for i, page in enumerate(pages):
-            (nc.vector if i < 2 else nc.gpsimd).memset(page[:], 0.0)
-        nc.gpsimd.memset(wc_s[:].rearrange("p a n -> p (a n)").bitcast(I32), 0)
+        for page in pages:
+            nc.vector.memset(page[:], 0.0)
+        nc.vector.memset(wc_s[:].rearrange("p a n -> p (a n)").bitcast(I32), 0)
 
         floor = keep.tile([P, 1], F32, name="floor")
         nc.scalar.activation(out=floor[:], in_=pages[0][:, 0:1], func=ACT.Sigmoid, bias=-CAP)
 
         tab_w = [placed([P, T], I32, "tab_w%d" % a, 8 * a) for a in range(PASSES)]
-        KEPT, SECOND, RATES, ZZ, LATE = 64, 80, 128, 160, 176
+        KEPT, SECOND, RATES, ZZ, LATE, PAGE = 64, 80, 128, 160, 176, 180
         raws = {ab: placed([P, PACK, KP], F32, "raw%d%d" % ab, kib) for ab, kib in (((0, 0), 16), ((1, 0), RATES + 8), ((0, 1), KEPT), ((1, 1), KEPT + 8))}
         wf_w = {(a, 0, 0): placed([P, 2 * P], U32, "wf_w%d00" % a, 24 + a) for a in range(PASSES)}
         wf_s = {(a, 0, 0): placed([P, 2 * P], U8, "wf_s%d00" % a, 26 + a) for a in range(PASSES)}
@@ -151,9 +151,9 @@ def tile_list_parts_depletion_kernel(tc, tab_words, tab_scales, offs, wf, wgs, o
         survival = {}
 
         def squash(k, n):
-            if k not in survival:
-                survival[k] = placed([P, S], F32, "survival%d" % k, 4 * k if k < PACK else SECOND + 4 * (k - PACK))
-            nc.scalar.activation(out=survival[k][:, half(n)], in_=bank(k, n)[:], func=ACT.Sigmoid, scale=-1.0)
+            kib = PAGE + 6 if (k, n) == (1, 0) else 4 * k + 2 * n if k < PACK else SECOND + 4 * (k - PACK) + 2 * n
+            survival[k, n] = placed([P, BANK], F32, "survival%d%d" % (k, n), kib)
+            nc.scalar.activation(out=survival[k, n][:], in_=bank(k, n)[:], func=ACT.Sigmoid, scale=-1.0)
 
         def logarithm(k, n):
             if k < 2:
@@ -161,7 +161,7 @@ def tile_list_parts_depletion_kernel(tc, tab_words, tab_scales, offs, wf, wgs, o
             elif n == 0:
                 rates[k] = placed([P, S], F32, "rates%d" % k, RATES + 4 * k)
                 rates[k, 0], rates[k, 1] = rates[k][:, half(0)], rates[k][:, half(1)]
-            nc.scalar.activation(out=rates[k, n], in_=survival[k][:, half(n)], func=ACT.Ln, bias=floor[:])
+            nc.scalar.activation(out=rates[k, n], in_=survival[k, n][:], func=ACT.Ln, bias=floor[:])
 
         def finish(k, n):
             nc.vector.scalar_tensor_tensor(out=rates[k, n], in0=rates[k, n], scalar=-1.0, in1=bank(k, n)[:], op0=ALU.mult, op1=ALU.max)
@@ -177,9 +177,11 @@ def tile_list_parts_depletion_kernel(tc, tab_words, tab_scales, offs, wf, wgs, o
 
         kept = {}
 
-        def thin_early(k):
-            kept[k] = placed([P, T2], F32, "kept%d" % k, KEPT + 8 * k)
-            nc.scalar.activation(out=kept[k][:], in_=pages[k][:], func=ACT.Exp, scale=-1.0)
+        def thin_early(k, chunks):
+            if k not in kept:
+                kept[k] = placed([P, T2], F32, "kept%d" % k, (KEPT, KEPT + 8, ZZ, SECOND)[k])
+            cols = slice(BANK * chunks.start, BANK * chunks.stop)
+            nc.scalar.activation(out=kept[k][:, cols], in_=pages[k][:, cols], func=ACT.Exp, scale=-1.0)
 
         def thin_late(k, c):
             nc.scalar.activation(out=kept_late[:, c, k - PACK, :], in_=pages[k % PAGES][:, half(c)], func=ACT.Exp, scale=-1.0)
@@ -204,7 +206,7 @@ def tile_list_parts_depletion_kernel(tc, tab_words, tab_scales, offs, wf, wgs, o
 
         def deplete_whole(c):
             nc.vector.tensor_tensor(
-                zz[:, c, :].rearrange("p (m i t) -> p m t i", i=RUN, t=PACK),
+                zz[:, (c + 1) % CHUNKS, :].rearrange("p (m i t) -> p m t i", i=RUN, t=PACK),
                 kept_late[:, c, :, :].rearrange("p t (m i) -> p m t i", i=RUN),
                 stocks[1][:, :, half(c)].rearrange("p t (m i) -> p m t i", i=RUN),
                 ALU.mult,
@@ -214,7 +216,7 @@ def tile_list_parts_depletion_kernel(tc, tab_words, tab_scales, offs, wf, wgs, o
 
         def quantize_z(b, c):
             z_w[b, c] = placed([P, BANK], U32, "z_w%d%d" % (b, c), KEPT + 8 * b + 2 * c)
-            nc.vector.quantize_mx(out=z_w[b, c][:].bitcast(FP8X4), scales=z_s[b, c][:], in_=zz[:, c, :])
+            nc.vector.quantize_mx(out=z_w[b, c][:].bitcast(FP8X4), scales=z_s[b, c][:], in_=zz[:, (c + b) % CHUNKS, :])
 
         def second_product(b, c, nt):
             nc.tensor.matmul_mx(
@@ -253,19 +255,22 @@ def tile_list_parts_depletion_kernel(tc, tab_words, tab_scales, offs, wf, wgs, o
         gather_words(1, 1)
         for a in range(PASSES):
             quantize_wf(a, 0, 2)
-        for a in range(PASSES):
-            round_wf(nc.vector.tensor_copy, a, 1, 0, PACK, ZZ + 8 + 4 * a)
-            quantize_wf(a, 1, 0)
-        zz = placed([P, CHUNKS, PACK * BANK], BF16, "zz", ZZ)
+        round_wf(nc.vector.tensor_copy, 0, 1, 0, PACK, ZZ + 8)
+        quantize_wf(0, 1, 0)
 
         opening = [(0, 0), (1, 0)]
         first_product(opening)
         for step in (squash, logarithm):
             for k, n in opening:
                 step(k, n)
+        round_wf(nc.scalar.copy, 1, 1, 0, PACK, PAGE + 6)
         for k, n in opening:
             finish(k, n)
             scatter_weighing(k, n)
+        quantize_wf(1, 1, 0)
+        for i in range(2):
+            pages.append(placed([P, T2], F32, "page%d" % (2 + i), PAGE + 8 * i))
+            nc.gpsimd.memset(pages[-1][:], 0.0)
         second = [(0, 1), (1, 1)] + [(k, n) for k in (2, 3) for n in range(HALVES)]
         for unit in second:
             first_product([unit])
@@ -289,18 +294,24 @@ def tile_list_parts_depletion_kernel(tc, tab_words, tab_scales, offs, wf, wgs, o
                 first_product([(k, n)])
                 squash(k, n)
         kept_late = placed([P, CHUNKS, PACK, BANK], F32, "kept_late", 0)
-        for k in (0, 1):
-            thin_early(k)
-            deplete_plane(k, slice(0, CHUNKS))
+        for k, chunks in ((0, slice(0, CHUNKS)), (1, slice(0, CHUNKS)), (2, slice(0, 2))):
+            thin_early(k, chunks)
+            deplete_plane(k, chunks)
         for k in range(PACK, TILES):
             for n in range(HALVES):
                 logarithm(k, n)
                 finish(k, n)
-            weigh(rates[k][:], whole)
-        thin_early(2)
-        thin_early(3)
-        deplete_plane(2, slice(0, CHUNKS))
-        for k in range(PACK, TILES):
+                if k == PACK:
+                    weigh(rates[k, n], half(n))
+            if k > PACK:
+                weigh(rates[k][:], whole)
+        thin_early(2, slice(2, CHUNKS))
+        thin_early(3, slice(0, CHUNKS))
+        deplete_plane(2, slice(2, CHUNKS))
+        zz = placed([P, CHUNKS, PACK * BANK], BF16, "zz", ZZ)
+        for n in range(HALVES):
+            scatter(PACK, rates[PACK, n], entries(n))
+        for k in range(PACK + 1, TILES):
             scatter(k, rates[k][:], all_entries)
         for k in (4, 5):
             for c in range(CHUNKS):

@@ -42,10 +42,10 @@ def tile_list_parts_depletion_kernel(tc, tab_words, tab_scales, offs, wf, wgs, o
         bins = keep.tile([P, S // 16], U16, name="bins")
         landing = keep.tile([P, T // 4], I32, name="landing")
         tab_s = keep.tile([P, T], U8, name="tab_s", align_bytes=64)
-        v_w = {an: keep.tile([P, BANK], U32, name="v_w%d%d" % an, align_bytes=64) for an in ((0, 0), (0, 1), (1, 0))}
-        v_s = {0: keep.tile([P, BANK], U8, name="v_s0", align_bytes=64)}
-        pages = [keep.tile([P, T2], F32, name="page%d" % i) for i in range(2)]
-        z_s = {(b, c): keep.tile([P, BANK], U8, name="z_s%d%d" % (b, c), align_bytes=64) for b in range(PASSES) for c in range(CHUNKS)}
+        v_w = {an: keep.tile([P, BANK], U32, name="v_w%d%d" % an, align_bytes=64) for an in ((0, 0), (0, 1), (1, 0), (1, 1))}
+        v_s = [keep.tile([P, BANK], U8, name="v_s%d" % n, align_bytes=64) for n in range(HALVES)]
+        pages = [keep.tile([P, T2], F32, name="page%d" % i) for i in range(1)]
+        z_s = {(1, c): keep.tile([P, BANK], U8, name="z_s1%d" % c, align_bytes=64) for c in range(CHUNKS)}
         wc_w = keep.tile([P, PASSES, 2 * N], U8, name="wc_w", align_bytes=64)
         wc_s = keep.tile([P, PASSES, N], U8, name="wc_s", align_bytes=64)
         weights = ring.tile([P, S], F32, name="weights", tag="weights", align_bytes=64)
@@ -72,7 +72,7 @@ def tile_list_parts_depletion_kernel(tc, tab_words, tab_scales, offs, wf, wgs, o
         nc.scalar.activation(out=floor[:], in_=pages[0][:, 0:1], func=ACT.Sigmoid, bias=-CAP)
 
         tab_w = [placed([P, T], I32, "tab_w%d" % a, 8 * a) for a in range(PASSES)]
-        KEPT, SECOND, RATES, ZZ, LATE, PAGE = 64, 80, 128, 160, 176, 180
+        KEPT, SECOND, RATES, ZZ, PAGE = 64, 80, 128, 160, 176
         raws = {ab: placed([P, PACK, KP], F32, "raw%d%d" % ab, kib) for ab, kib in (((0, 0), 16), ((1, 0), RATES + 8), ((0, 1), KEPT), ((1, 1), KEPT + 8))}
         wf_w = {(a, 0, 0): placed([P, 2 * P], U32, "wf_w%d00" % a, 24 + a) for a in range(PASSES)}
         wf_s = {(a, 0, 0): placed([P, 2 * P], U8, "wf_s%d00" % a, 26 + a) for a in range(PASSES)}
@@ -81,11 +81,9 @@ def tile_list_parts_depletion_kernel(tc, tab_words, tab_scales, offs, wf, wgs, o
         wf_s[0, 0, 2] = placed([P, 2 * P], U8, "wf_s002", RATES + 2)
         wf_s[1, 0, 2] = placed([P, 2 * P], U8, "wf_s102", RATES + 6)
         wf_w[0, 1, 0] = placed([P, KP], U32, "wf_w01", RATES + 16)
-        wf_w[1, 1, 0] = placed([P, KP], U32, "wf_w11", KEPT)
+        wf_w[1, 1, 0] = placed([P, KP], U32, "wf_w11", ZZ + 7)
         wf_s[0, 1, 0] = placed([P, KP], U8, "wf_s01", RATES + 20)
-        wf_s[1, 1, 0] = placed([P, KP], U8, "wf_s11", RATES + 24)
-        v_s[1] = placed([P, BANK], U8, "v_s1", LATE)
-        v_w[1, 1] = placed([P, BANK], U32, "v_w11", LATE + 0.5)
+        wf_s[1, 1, 0] = placed([P, KP], U8, "wf_s11", RATES + 27.75)
 
         def load_wf(a, b):
             nc.sync.dma_start(out=raws[a, b][:], in_=wf[KP * a : KP * (a + 1), KP * b : KP * (b + 1)].rearrange("(p j) c -> p j c", j=PACK))
@@ -100,11 +98,12 @@ def tile_list_parts_depletion_kernel(tc, tab_words, tab_scales, offs, wf, wgs, o
             nc.sync.dma_start(out=landing[32 * q : 32 * q + 4 * PASSES, :], in_=tab_scales[:, 4 * q : 4 * q + 4, :].bitcast(I32))
         for a in range(PASSES):
             nc.sync.dma_start(out=tab_w[a][:], in_=tab_words[a].rearrange("p t i -> p (t i)").bitcast(I32))
+        for a in range(PASSES):
             load_wf(a, 0)
         nc.sync.dma_start(bins[:], offs2)
         load_wf(0, 1)
-        load_wf(1, 1)
         nc.sync.dma_start(out=weights[:], in_=wgs)
+        load_wf(1, 1)
         nc.sync.dma_start(out=wc_w[:].bitcast(I32), in_=wc_words.rearrange("a p n -> p a n").bitcast(I32))
         for q in range(4):
             nc.sync.dma_start(out=wc_s[32 * q : 32 * q + 4, :, :].bitcast(I32), in_=wc_scales[:, 4 * q : 4 * q + 4, :].rearrange("a r n -> r a n").bitcast(I32))
@@ -131,8 +130,8 @@ def tile_list_parts_depletion_kernel(tc, tab_words, tab_scales, offs, wf, wgs, o
         def bank(k, n):
             return banks[(HALVES * k + n) % 8]
 
-        def first_product(units):
-            for a in range(PASSES):
+        def first_product(units, order):
+            for a in order:
                 for k, n in units:
                     b, t = divmod(k, PACK)
                     lo = 2 * (t // 2) if b == 0 else 0
@@ -143,21 +142,25 @@ def tile_list_parts_depletion_kernel(tc, tab_words, tab_scales, offs, wf, wgs, o
                         lhsT_scale=wf_s[a, b, lo][:, rows],
                         rhs=v_w[a, n][:].bitcast(FP8X4),
                         rhs_scale=v_s[n][4 * a : P, :],
-                        start=(a == 0),
-                        stop=(a == PASSES - 1),
+                        start=(a == order[0]),
+                        stop=(a == order[-1]),
                     )
+
+        def clear_page(i):
+            pages.append(placed([P, T2], F32, "page%d" % (1 + i), PAGE + 8 * i))
+            nc.gpsimd.memset(pages[-1][:], 0.0)
 
         rates = {}
         survival = {}
 
         def squash(k, n):
-            kib = PAGE + 6 if (k, n) == (1, 0) else 4 * k + 2 * n if k < PACK else SECOND + 4 * (k - PACK) + 2 * n
+            kib = PAGE + 16 * n if k == 0 else 4 * k + 2 * n if k < PACK else SECOND + 4 * (k - PACK) + 2 * n
             survival[k, n] = placed([P, BANK], F32, "survival%d%d" % (k, n), kib)
             nc.scalar.activation(out=survival[k, n][:], in_=bank(k, n)[:], func=ACT.Sigmoid, scale=-1.0)
 
         def logarithm(k, n):
             if k < 2:
-                rates[k, n] = placed([P, BANK], F32, "rates%d%d" % (k, n), RATES + 4 * k + 2 * n)[:]
+                rates[k, n] = placed([P, BANK], F32, "rates%d%d" % (k, n), RATES + 26 if (k, n) == (0, 0) else RATES + 4 * k + 2 * n)[:]
             elif n == 0:
                 rates[k] = placed([P, S], F32, "rates%d" % k, RATES + 4 * k)
                 rates[k, 0], rates[k, 1] = rates[k][:, half(0)], rates[k][:, half(1)]
@@ -166,8 +169,8 @@ def tile_list_parts_depletion_kernel(tc, tab_words, tab_scales, offs, wf, wgs, o
         def finish(k, n):
             nc.vector.scalar_tensor_tensor(out=rates[k, n], in0=rates[k, n], scalar=-1.0, in1=bank(k, n)[:], op0=ALU.mult, op1=ALU.max)
 
-        def weigh(part, cols):
-            nc.gpsimd.tensor_tensor(part, part, weights[:, cols], ALU.mult)
+        def weigh(part, cols, into=None):
+            nc.gpsimd.tensor_tensor(part if into is None else into, part, weights[:, cols], ALU.mult)
 
         def scatter_weighing(k, n):
             nc.vector.tensor_tensor(pages[k % PAGES][:].indirect(bins[:, entries(n)]), rates[k, n], weights[:, half(n)], ALU.mult)
@@ -176,47 +179,70 @@ def tile_list_parts_depletion_kernel(tc, tab_words, tab_scales, offs, wf, wgs, o
             nc.vector.tensor_copy(pages[k % PAGES][:].indirect(bins[:, names]), part)
 
         kept = {}
+        planes = {}
 
-        def thin_early(k, chunks):
+        def columns(chunks):
+            return slice(BANK * chunks.start, BANK * chunks.stop)
+
+        def thin(k, chunks):
             if k not in kept:
-                kept[k] = placed([P, T2], F32, "kept%d" % k, (KEPT, KEPT + 8, ZZ, SECOND)[k])
-            cols = slice(BANK * chunks.start, BANK * chunks.stop)
-            nc.scalar.activation(out=kept[k][:, cols], in_=pages[k][:, cols], func=ACT.Exp, scale=-1.0)
+                kept[k] = placed([P, T2], F32, "kept%d" % k, (KEPT, ZZ, ZZ + 8, SECOND, SECOND + 8, 0)[k])
+            nc.scalar.activation(out=kept[k][:, columns(chunks)], in_=pages[k % PAGES][:, columns(chunks)], func=ACT.Exp, scale=-1.0)
 
-        def thin_late(k, c):
-            nc.scalar.activation(out=kept_late[:, c, k - PACK, :], in_=pages[k % PAGES][:, half(c)], func=ACT.Exp, scale=-1.0)
+        def thin_last(k, c):
+            nc.scalar.activation(out=kept_last[c][:, k % 2, :], in_=pages[k % PAGES][:, half(c)], func=ACT.Exp, scale=-1.0)
 
-        def planes(chunks):
-            return kept_late[:, chunks, 2:4, :].rearrange("p c u m -> p c (u m)").bitcast(BF16).rearrange("p c (t m) -> p c t m", t=PACK)
-
-        def deplete_plane(t, chunks):
-            cols = slice(BANK * chunks.start, BANK * chunks.stop)
+        def deplete(k, chunks):
+            lo = 2 * (chunks.start // 2)
+            if lo not in planes:
+                planes[lo] = placed([P, 2, PACK, BANK], BF16, "planes%d" % lo, 4 * lo)
             nc.gpsimd.tensor_tensor(
-                planes(chunks)[:, :, t, :],
-                kept[t][:, cols].rearrange("p (c m) -> p c m", m=BANK),
-                stocks[0][:, t, cols].rearrange("p (c m) -> p c m", m=BANK),
+                planes[lo][:, chunks.start - lo : chunks.stop - lo, k, :],
+                kept[k][:, columns(chunks)].rearrange("p (c m) -> p c m", m=BANK),
+                stocks[0][:, k, columns(chunks)].rearrange("p (c m) -> p c m", m=BANK),
                 ALU.mult,
             )
 
         def interleave(c):
+            lo = 2 * (c // 2)
             nc.scalar.copy(
                 out=zz[:, c, :].rearrange("p (m i t) -> p m t i", i=RUN, t=PACK),
-                in_=planes(slice(c, c + 1))[:, 0, :, :].rearrange("p t (m i) -> p m t i", i=RUN),
+                in_=planes[lo][:, c - lo, :, :].rearrange("p t (m i) -> p m t i", i=RUN),
             )
 
-        def deplete_whole(c):
+        def late_planes(c):
+            return kept_last[c][:, 1, :].bitcast(BF16).rearrange("p (t m) -> p t m", t=2)
+
+        def deplete_late(t, c):
+            nc.gpsimd.tensor_tensor(late_planes(c)[:, t, :], kept[PACK + t][:, half(c)], stocks[1][:, t, half(c)], ALU.mult)
+
+        def in_pairs(c, u):
+            return pairs[:, c, u, :].rearrange("p (m i t) -> p m t i", i=RUN, t=2)
+
+        def pair_up(c):
+            nc.scalar.copy(out=in_pairs(c, 0), in_=late_planes(c).rearrange("p t (m i) -> p m t i", i=RUN))
+
+        def deplete_last(c):
             nc.vector.tensor_tensor(
-                zz[:, (c + 1) % CHUNKS, :].rearrange("p (m i t) -> p m t i", i=RUN, t=PACK),
-                kept_late[:, c, :, :].rearrange("p t (m i) -> p m t i", i=RUN),
-                stocks[1][:, :, half(c)].rearrange("p t (m i) -> p m t i", i=RUN),
+                in_pairs(c, 1),
+                kept_last[c][:].rearrange("p t (m i) -> p m t i", i=RUN),
+                stocks[1][:, 2:4, half(c)].rearrange("p t (m i) -> p m t i", i=RUN),
                 ALU.mult,
+            )
+
+        def weave(c):
+            nc.vector.tensor_copy(
+                out=zz[:, c, :].bitcast(F32).rearrange("p (m i u) -> p m u i", u=2, i=2),
+                in_=pairs[:, c, :, :].bitcast(F32).rearrange("p u (m i) -> p m u i", i=2),
             )
 
         z_w = {}
 
         def quantize_z(b, c):
-            z_w[b, c] = placed([P, BANK], U32, "z_w%d%d" % (b, c), KEPT + 8 * b + 2 * c)
-            nc.vector.quantize_mx(out=z_w[b, c][:].bitcast(FP8X4), scales=z_s[b, c][:], in_=zz[:, (c + b) % CHUNKS, :])
+            z_w[b, c] = placed([P, BANK], U32, "z_w%d%d" % (b, c), 28 + 4 * c if b == 0 and c > 0 else KEPT + 8 * b + 2 * c)
+            if b == 0:
+                z_s[b, c] = placed([P, BANK], U8, "z_s0%d" % c, SECOND + 4 + c)
+            nc.vector.quantize_mx(out=z_w[b, c][:].bitcast(FP8X4), scales=z_s[b, c][:], in_=zz[:, c, :])
 
         def second_product(b, c, nt):
             nc.tensor.matmul_mx(
@@ -231,7 +257,7 @@ def tile_list_parts_depletion_kernel(tc, tab_words, tab_scales, offs, wf, wgs, o
 
         def store(c, nt):
             i = N // P * c + nt
-            staged = rates[divmod(i, 2)]
+            staged = placed([P, BANK], F32, "staged%d" % i, RATES + 2 * i)[:]
             if c == CHUNKS - 1 and nt % 2 == 1:
                 nc.vector.tensor_copy(out=staged, in_=banks[i % 8][:])
             else:
@@ -241,42 +267,43 @@ def tile_list_parts_depletion_kernel(tc, tab_words, tab_scales, offs, wf, wgs, o
         for q in range(4):
             rows = slice(32 * q, 32 * q + 4 * PASSES)
             nc.vector.tensor_copy(out=tab_s[rows, :].bitcast(I32), in_=landing[rows, :])
-        gather_words(0, 0)
         gather_scales(0)
-        gather_words(0, 1)
+        gather_words(0, 0)
         gather_words(1, 0)
+        gather_scales(1)
+        gather_words(0, 1)
+        gather_words(1, 1)
         round_wf(nc.scalar.copy, 0, 0, 0, 2, ZZ)
         round_wf(nc.scalar.copy, 0, 0, 2, 4, ZZ + 2)
         quantize_wf(0, 0, 0)
-        round_wf(nc.vector.tensor_copy, 1, 0, 0, 2, LATE + 0.4375)
+        round_wf(nc.vector.tensor_copy, 1, 0, 0, 2, ZZ + 6)
         quantize_wf(1, 0, 0)
         round_wf(nc.scalar.copy, 1, 0, 2, 4, ZZ + 4)
-        gather_scales(1)
-        gather_words(1, 1)
         for a in range(PASSES):
             quantize_wf(a, 0, 2)
         round_wf(nc.vector.tensor_copy, 0, 1, 0, PACK, ZZ + 8)
         quantize_wf(0, 1, 0)
 
         opening = [(0, 0), (1, 0)]
-        first_product(opening)
+        first_product(opening, (0, 1))
         for step in (squash, logarithm):
             for k, n in opening:
                 step(k, n)
-        round_wf(nc.scalar.copy, 1, 1, 0, PACK, PAGE + 6)
-        for k, n in opening:
-            finish(k, n)
-            scatter_weighing(k, n)
+        clear_page(0)
+        finish(0, 0)
+        scatter_weighing(0, 0)
+        round_wf(nc.vector.tensor_copy, 1, 1, 0, PACK, PAGE + 8)
+        finish(1, 0)
         quantize_wf(1, 1, 0)
-        for i in range(2):
-            pages.append(placed([P, T2], F32, "page%d" % (2 + i), PAGE + 8 * i))
-            nc.gpsimd.memset(pages[-1][:], 0.0)
+        clear_page(1)
+        scatter_weighing(1, 0)
         second = [(0, 1), (1, 1)] + [(k, n) for k in (2, 3) for n in range(HALVES)]
         for unit in second:
-            first_product([unit])
+            first_product([unit], (1, 0))
         for step in (squash, logarithm):
             for k, n in second:
                 step(k, n)
+        clear_page(2)
         finish(0, 1)
         scatter_weighing(0, 1)
         whole, all_entries = slice(0, S), slice(0, S // 16)
@@ -289,48 +316,69 @@ def tile_list_parts_depletion_kernel(tc, tab_words, tab_scales, offs, wf, wgs, o
         scatter(1, rates[1, 1], entries(1))
         for k in (2, 3):
             scatter(k, rates[k][:], all_entries)
+        front, back, everything = slice(0, 2), slice(2, CHUNKS), slice(0, CHUNKS)
+        single = [slice(c, c + 1) for c in range(CHUNKS)]
+        thin(0, everything)
         for k in range(PACK, TILES):
             for n in range(HALVES):
-                first_product([(k, n)])
+                first_product([(k, n)], (1, 0))
                 squash(k, n)
-        kept_late = placed([P, CHUNKS, PACK, BANK], F32, "kept_late", 0)
-        for k, chunks in ((0, slice(0, CHUNKS)), (1, slice(0, CHUNKS)), (2, slice(0, 2))):
-            thin_early(k, chunks)
-            deplete_plane(k, chunks)
+        thin(1, everything)
+        thin(2, front)
+        for k, chunks in ((0, front), (0, back), (1, front), (1, back), (2, front)):
+            deplete(k, chunks)
         for k in range(PACK, TILES):
             for n in range(HALVES):
                 logarithm(k, n)
                 finish(k, n)
-                if k == PACK:
-                    weigh(rates[k, n], half(n))
-            if k > PACK:
-                weigh(rates[k][:], whole)
-        thin_early(2, slice(2, CHUNKS))
-        thin_early(3, slice(0, CHUNKS))
-        deplete_plane(2, slice(2, CHUNKS))
+        for n in range(HALVES):
+            weigh(rates[4, n], half(n))
+        weigh(rates[5][:], whole)
+        thin(2, back)
+        thin(3, everything)
+        deplete(2, back)
+        for c in range(CHUNKS):
+            deplete(3, single[c])
+        weighed = {k: placed([P, S], F32, "weighed%d" % k, SECOND + 4 * (k - 6)) for k in (6, 7)}
+        for k in (6, 7):
+            weigh(rates[k][:], whole, weighed[k][:])
         zz = placed([P, CHUNKS, PACK * BANK], BF16, "zz", ZZ)
         for n in range(HALVES):
-            scatter(PACK, rates[PACK, n], entries(n))
-        for k in range(PACK + 1, TILES):
-            scatter(k, rates[k][:], all_entries)
-        for k in (4, 5):
-            for c in range(CHUNKS):
-                thin_late(k, c)
-        for c in range(CHUNKS):
-            deplete_plane(3, slice(c, c + 1))
-            interleave(c)
-            quantize_z(0, c)
+            scatter(4, rates[4, n], entries(n))
+        scatter(5, rates[5][:], all_entries)
         for k in (6, 7):
-            for c in range(CHUNKS):
-                thin_late(k, c)
-        for c in range(2):
+            scatter(k, weighed[k][:], all_entries)
+        thin(4, everything)
+        for c in range(CHUNKS):
+            interleave(c)
+        thin(5, everything)
+        kept_last = [placed([P, 2, BANK], F32, "kept_last%d" % c, 32 + 4 * c) for c in range(CHUNKS)]
+        pairs = placed([P, CHUNKS, 2, 2 * BANK], BF16, "pairs", 48)
+        for c in range(CHUNKS):
+            for t in range(2):
+                deplete_late(t, c)
+        for c in range(CHUNKS):
+            thin_last(6, c)
+        pair_up(0)
+        for c in range(CHUNKS):
+            if c + 1 < CHUNKS:
+                pair_up(c + 1)
+            thin_last(7, c)
+        quantize_z(0, 0)
+        deplete_last(0)
+        for c in range(CHUNKS):
+            if 0 < c < CHUNKS - 1:
+                quantize_z(0, c + 1)
+            weave(c)
+            if c == 0:
+                quantize_z(0, 1)
+            elif c + 1 < CHUNKS:
+                deplete_last(c + 1)
+            quantize_z(1, c)
+            if c == 0:
+                deplete_last(1)
             for nt in range(N // P):
                 second_product(0, c, nt)
-        for c in range(CHUNKS):
-            deplete_whole(c)
-            quantize_z(1, c)
             for nt in range(N // P):
-                if c >= 2:
-                    second_product(0, c, nt)
                 second_product(1, c, nt)
                 store(c, nt)

@@ -73,17 +73,21 @@ def tile_list_parts_depletion_kernel(tc, tab_words, tab_scales, offs, wf, wgs, o
 
         tab_w = [placed([P, T], I32, "tab_w%d" % a, 8 * a) for a in range(PASSES)]
         KEPT, SECOND, RATES, ZZ, PAGE = 64, 80, 128, 160, 176
-        raws = {ab: placed([P, PACK, KP], F32, "raw%d%d" % ab, kib) for ab, kib in (((0, 0), 16), ((1, 0), RATES + 8), ((0, 1), KEPT), ((1, 1), KEPT + 8))}
-        wf_w = {(a, 0, 0): placed([P, 2 * P], U32, "wf_w%d00" % a, 24 + a) for a in range(PASSES)}
-        wf_s = {(a, 0, 0): placed([P, 2 * P], U8, "wf_s%d00" % a, 26 + a) for a in range(PASSES)}
-        wf_w[0, 0, 2] = placed([P, 2 * P], U32, "wf_w002", RATES + 12)
-        wf_w[1, 0, 2] = placed([P, 2 * P], U32, "wf_w102", RATES + 8)
-        wf_s[0, 0, 2] = placed([P, 2 * P], U8, "wf_s002", RATES + 2)
-        wf_s[1, 0, 2] = placed([P, 2 * P], U8, "wf_s102", RATES + 6)
-        wf_w[0, 1, 0] = placed([P, KP], U32, "wf_w01", RATES + 16)
+        raws = {ab: placed([P, PACK, KP], F32, "raw%d%d" % ab, kib) for ab, kib in (((0, 0), 16), ((1, 0), RATES + 20), ((0, 1), KEPT), ((1, 1), KEPT + 8))}
+        wf_w = {(0, 0, 0): placed([P, 2 * P], U32, "wf_w000", 24)}
+        wf_s = {(0, 0, 0): placed([P, 2 * P], U8, "wf_s000", 26)}
+        for t in range(2):
+            wf_w[1, 0, t] = placed([P, P], U32, "wf_w10%d" % t, 25 + 0.5 * t)
+        wf_s[1, 0, 0] = placed([P, P], U8, "wf_s100", RATES + 8)
+        wf_s[1, 0, 1] = placed([P, P], U8, "wf_s101", 27)
+        wf_w[0, 0, 2] = placed([P, 2 * P], U32, "wf_w002", RATES + 20)
+        wf_w[1, 0, 2] = placed([P, 2 * P], U32, "wf_w102", RATES + 2)
+        wf_s[0, 0, 2] = placed([P, 2 * P], U8, "wf_s002", RATES + 18)
+        wf_s[1, 0, 2] = placed([P, 2 * P], U8, "wf_s102", RATES + 11)
+        wf_w[0, 1, 0] = placed([P, KP], U32, "wf_w01", RATES)
         wf_w[1, 1, 0] = placed([P, KP], U32, "wf_w11", ZZ + 7)
-        wf_s[0, 1, 0] = placed([P, KP], U8, "wf_s01", RATES + 20)
-        wf_s[1, 1, 0] = placed([P, KP], U8, "wf_s11", RATES + 27.75)
+        wf_s[0, 1, 0] = placed([P, KP], U8, "wf_s01", RATES + 6)
+        wf_s[1, 1, 0] = placed([P, KP], U8, "wf_s11", RATES + 9.5)
 
         def load_wf(a, b):
             nc.sync.dma_start(out=raws[a, b][:], in_=wf[KP * a : KP * (a + 1), KP * b : KP * (b + 1)].rearrange("(p j) c -> p j c", j=PACK))
@@ -102,8 +106,9 @@ def tile_list_parts_depletion_kernel(tc, tab_words, tab_scales, offs, wf, wgs, o
             load_wf(a, 0)
         nc.sync.dma_start(bins[:], offs2)
         load_wf(0, 1)
-        nc.sync.dma_start(out=weights[:], in_=wgs)
         load_wf(1, 1)
+        for n in range(HALVES):
+            nc.sync.dma_start(out=weights[:, half(n)], in_=wgs[:, half(n)])
         nc.sync.dma_start(out=wc_w[:].bitcast(I32), in_=wc_words.rearrange("a p n -> p a n").bitcast(I32))
         for q in range(4):
             nc.sync.dma_start(out=wc_s[32 * q : 32 * q + 4, :, :].bitcast(I32), in_=wc_scales[:, 4 * q : 4 * q + 4, :].rearrange("a r n -> r a n").bitcast(I32))
@@ -134,7 +139,7 @@ def tile_list_parts_depletion_kernel(tc, tab_words, tab_scales, offs, wf, wgs, o
             for a in order:
                 for k, n in units:
                     b, t = divmod(k, PACK)
-                    lo = 2 * (t // 2) if b == 0 else 0
+                    lo = max(start for pass_, block, start in wf_w if (pass_, block) == (a, b) and start <= t)
                     rows = slice(P * (t - lo), P * (t - lo + 1))
                     nc.tensor.matmul_mx(
                         out=bank(k, n)[:],
@@ -154,26 +159,29 @@ def tile_list_parts_depletion_kernel(tc, tab_words, tab_scales, offs, wf, wgs, o
         survival = {}
 
         def squash(k, n):
-            kib = PAGE + 16 * n if k == 0 else 4 * k + 2 * n if k < PACK else SECOND + 4 * (k - PACK) + 2 * n
+            kib = PAGE + 16 * k if k < 2 and n == 0 else KEPT if (k, n) == (3, 0) else 4 * k + 2 * n if k < PACK else SECOND + 4 * (k - PACK) + 2 * n
             survival[k, n] = placed([P, BANK], F32, "survival%d%d" % (k, n), kib)
             nc.scalar.activation(out=survival[k, n][:], in_=bank(k, n)[:], func=ACT.Sigmoid, scale=-1.0)
 
-        def logarithm(k, n):
-            if k < 2:
-                rates[k, n] = placed([P, BANK], F32, "rates%d%d" % (k, n), RATES + 26 if (k, n) == (0, 0) else RATES + 4 * k + 2 * n)[:]
+        def logarithm(k, n, cols=slice(0, BANK)):
+            if (k, n) in rates:
+                pass
+            elif k < 2:
+                rates[k, n] = placed([P, BANK], F32, "rates%d%d" % (k, n), RATES + (8, 16, 18, 11)[2 * k + n])[:]
             elif n == 0:
-                rates[k] = placed([P, S], F32, "rates%d" % k, RATES + 4 * k)
+                rates[k] = placed([P, S], F32, "rates%d" % k, RATES + (2, 20, 0, 4, 8, 12)[k - 2])
                 rates[k, 0], rates[k, 1] = rates[k][:, half(0)], rates[k][:, half(1)]
-            nc.scalar.activation(out=rates[k, n], in_=survival[k, n][:], func=ACT.Ln, bias=floor[:])
+            nc.scalar.activation(out=rates[k, n][:, cols], in_=survival[k, n][:, cols], func=ACT.Ln, bias=floor[:])
 
-        def finish(k, n):
-            nc.vector.scalar_tensor_tensor(out=rates[k, n], in0=rates[k, n], scalar=-1.0, in1=bank(k, n)[:], op0=ALU.mult, op1=ALU.max)
+        def finish(k, n, cols=slice(0, BANK)):
+            nc.vector.scalar_tensor_tensor(out=rates[k, n][:, cols], in0=rates[k, n][:, cols], scalar=-1.0, in1=bank(k, n)[:, cols], op0=ALU.mult, op1=ALU.max)
 
         def weigh(part, cols, into=None):
             nc.gpsimd.tensor_tensor(part if into is None else into, part, weights[:, cols], ALU.mult)
 
-        def scatter_weighing(k, n):
-            nc.vector.tensor_tensor(pages[k % PAGES][:].indirect(bins[:, entries(n)]), rates[k, n], weights[:, half(n)], ALU.mult)
+        def scatter_weighing(k, n, cols=slice(0, BANK)):
+            lo, hi = BANK * n + cols.start, BANK * n + cols.stop
+            nc.vector.tensor_tensor(pages[k % PAGES][:].indirect(bins[:, lo // 16 : hi // 16]), rates[k, n][:, cols], weights[:, lo:hi], ALU.mult)
 
         def scatter(k, part, names):
             nc.vector.tensor_copy(pages[k % PAGES][:].indirect(bins[:, names]), part)
@@ -231,9 +239,10 @@ def tile_list_parts_depletion_kernel(tc, tab_words, tab_scales, offs, wf, wgs, o
             )
 
         def weave(c):
-            nc.vector.tensor_copy(
-                out=zz[:, c, :].bitcast(F32).rearrange("p (m i u) -> p m u i", u=2, i=2),
-                in_=pairs[:, c, :, :].bitcast(F32).rearrange("p u (m i) -> p m u i", i=2),
+            copy, word = (nc.scalar.copy, U32) if c < 2 else (nc.vector.tensor_copy, F32)
+            copy(
+                out=zz[:, c, :].bitcast(word).rearrange("p (m i u) -> p m u i", u=2, i=2),
+                in_=pairs[:, c, :, :].bitcast(word).rearrange("p u (m i) -> p m u i", i=2),
             )
 
         z_w = {}
@@ -258,7 +267,7 @@ def tile_list_parts_depletion_kernel(tc, tab_words, tab_scales, offs, wf, wgs, o
         def store(c, nt):
             i = N // P * c + nt
             staged = placed([P, BANK], F32, "staged%d" % i, RATES + 2 * i)[:]
-            if c == CHUNKS - 1 and nt % 2 == 1:
+            if c == CHUNKS - 1 and nt != 2:
                 nc.vector.tensor_copy(out=staged, in_=banks[i % 8][:])
             else:
                 nc.scalar.copy(out=staged, in_=banks[i % 8][:])
@@ -277,35 +286,42 @@ def tile_list_parts_depletion_kernel(tc, tab_words, tab_scales, offs, wf, wgs, o
         round_wf(nc.scalar.copy, 0, 0, 2, 4, ZZ + 2)
         quantize_wf(0, 0, 0)
         round_wf(nc.vector.tensor_copy, 1, 0, 0, 2, ZZ + 6)
-        quantize_wf(1, 0, 0)
+        grouped[1, 0, 1] = grouped[1, 0, 0][:, KP : 2 * KP]
+        grouped[1, 0, 0] = grouped[1, 0, 0][:, 0:KP]
+        for t in range(2):
+            quantize_wf(1, 0, t)
         round_wf(nc.scalar.copy, 1, 0, 2, 4, ZZ + 4)
         for a in range(PASSES):
             quantize_wf(a, 0, 2)
         round_wf(nc.vector.tensor_copy, 0, 1, 0, PACK, ZZ + 8)
         quantize_wf(0, 1, 0)
-
-        opening = [(0, 0), (1, 0)]
-        first_product(opening, (0, 1))
-        for step in (squash, logarithm):
-            for k, n in opening:
-                step(k, n)
-        clear_page(0)
-        finish(0, 0)
-        scatter_weighing(0, 0)
         round_wf(nc.vector.tensor_copy, 1, 1, 0, PACK, PAGE + 8)
-        finish(1, 0)
+
+        opening = [(0, 0), (0, 1)]
+        first_product(opening, (0, 1))
+        for k, n in opening:
+            squash(k, n)
+        pieces = [slice(0, P), slice(P, BANK)]
+        for cols in pieces:
+            logarithm(0, 0, cols)
+        logarithm(0, 1)
+        clear_page(0)
+        for cols in pieces:
+            finish(0, 0, cols)
+            scatter_weighing(0, 0, cols)
+        finish(0, 1)
         quantize_wf(1, 1, 0)
         clear_page(1)
-        scatter_weighing(1, 0)
-        second = [(0, 1), (1, 1)] + [(k, n) for k in (2, 3) for n in range(HALVES)]
+        scatter_weighing(0, 1)
+        second = [(k, n) for k in (1, 2, 3) for n in range(HALVES)]
         for unit in second:
             first_product([unit], (1, 0))
         for step in (squash, logarithm):
             for k, n in second:
                 step(k, n)
         clear_page(2)
-        finish(0, 1)
-        scatter_weighing(0, 1)
+        finish(1, 0)
+        scatter_weighing(1, 0)
         whole, all_entries = slice(0, S), slice(0, S // 16)
         finish(1, 1)
         weigh(rates[1, 1], half(1))
@@ -317,7 +333,6 @@ def tile_list_parts_depletion_kernel(tc, tab_words, tab_scales, offs, wf, wgs, o
         for k in (2, 3):
             scatter(k, rates[k][:], all_entries)
         front, back, everything = slice(0, 2), slice(2, CHUNKS), slice(0, CHUNKS)
-        single = [slice(c, c + 1) for c in range(CHUNKS)]
         thin(0, everything)
         for k in range(PACK, TILES):
             for n in range(HALVES):
@@ -337,8 +352,8 @@ def tile_list_parts_depletion_kernel(tc, tab_words, tab_scales, offs, wf, wgs, o
         thin(2, back)
         thin(3, everything)
         deplete(2, back)
-        for c in range(CHUNKS):
-            deplete(3, single[c])
+        for chunks in (front, back):
+            deplete(3, chunks)
         weighed = {k: placed([P, S], F32, "weighed%d" % k, SECOND + 4 * (k - 6)) for k in (6, 7)}
         for k in (6, 7):
             weigh(rates[k][:], whole, weighed[k][:])
@@ -359,10 +374,9 @@ def tile_list_parts_depletion_kernel(tc, tab_words, tab_scales, offs, wf, wgs, o
                 deplete_late(t, c)
         for c in range(CHUNKS):
             thin_last(6, c)
-        pair_up(0)
         for c in range(CHUNKS):
-            if c + 1 < CHUNKS:
-                pair_up(c + 1)
+            pair_up(c)
+        for c in range(CHUNKS):
             thin_last(7, c)
         quantize_z(0, 0)
         deplete_last(0)

@@ -102,7 +102,6 @@ def tile_list_parts_depletion_kernel(tc, tab_words, tab_scales, offs, wf, wgs, o
             nc.sync.dma_start(out=landing[32 * q : 32 * q + 4 * PASSES, :], in_=tab_scales[:, 4 * q : 4 * q + 4, :].bitcast(I32))
         for a in range(PASSES):
             nc.sync.dma_start(out=tab_w[a][:], in_=tab_words[a].rearrange("p t i -> p (t i)").bitcast(I32))
-        for a in range(PASSES):
             load_wf(a, 0)
         nc.sync.dma_start(bins[:], offs2)
         load_wf(0, 1)
@@ -277,14 +276,14 @@ def tile_list_parts_depletion_kernel(tc, tab_words, tab_scales, offs, wf, wgs, o
             rows = slice(32 * q, 32 * q + 4 * PASSES)
             nc.vector.tensor_copy(out=tab_s[rows, :].bitcast(I32), in_=landing[rows, :])
         gather_scales(0)
-        gather_words(0, 0)
-        gather_words(1, 0)
         gather_scales(1)
+        gather_words(0, 0)
         gather_words(0, 1)
-        gather_words(1, 1)
         round_wf(nc.scalar.copy, 0, 0, 0, 2, ZZ)
         round_wf(nc.scalar.copy, 0, 0, 2, 4, ZZ + 2)
         quantize_wf(0, 0, 0)
+        gather_words(1, 0)
+        gather_words(1, 1)
         round_wf(nc.vector.tensor_copy, 1, 0, 0, 2, ZZ + 6)
         grouped[1, 0, 1] = grouped[1, 0, 0][:, KP : 2 * KP]
         grouped[1, 0, 0] = grouped[1, 0, 0][:, 0:KP]
@@ -315,7 +314,7 @@ def tile_list_parts_depletion_kernel(tc, tab_words, tab_scales, offs, wf, wgs, o
         scatter_weighing(0, 1)
         second = [(k, n) for k in (1, 2, 3) for n in range(HALVES)]
         for unit in second:
-            first_product([unit], (1, 0))
+            first_product([unit], (0, 1) if unit[0] == 1 else (1, 0))
         for step in (squash, logarithm):
             for k, n in second:
                 step(k, n)
@@ -374,9 +373,11 @@ def tile_list_parts_depletion_kernel(tc, tab_words, tab_scales, offs, wf, wgs, o
                 deplete_late(t, c)
         for c in range(CHUNKS):
             thin_last(6, c)
-        for c in range(CHUNKS):
+        for c in range(CHUNKS - 1):
             pair_up(c)
         for c in range(CHUNKS):
+            if c == CHUNKS - 1:
+                pair_up(c)
             thin_last(7, c)
         quantize_z(0, 0)
         deplete_last(0)

@@ -197,7 +197,7 @@ def tile_list_parts_depletion_kernel(tc, tab_words, tab_scales, offs, wf, wgs, o
             nc.scalar.activation(out=kept[k][:, columns(chunks)], in_=pages[k % PAGES][:, columns(chunks)], func=ACT.Exp, scale=-1.0)
 
         def thin_last(k, c):
-            nc.scalar.activation(out=kept_last[c][:, k % 2, :], in_=pages[k % PAGES][:, half(c)], func=ACT.Exp, scale=-1.0)
+            nc.scalar.activation(out=kept_last[c][:, k - PACK if c == CHUNKS - 1 else k % 2, :], in_=pages[k % PAGES][:, half(c)], func=ACT.Exp, scale=-1.0)
 
         def deplete(k, chunks):
             lo = 2 * (chunks.start // 2)
@@ -218,6 +218,8 @@ def tile_list_parts_depletion_kernel(tc, tab_words, tab_scales, offs, wf, wgs, o
             )
 
         def late_planes(c):
+            if c == CHUNKS - 2:
+                return ending[:, 1 :: PACK, :].bitcast(BF16)[:, :, 0:BANK]
             return kept_last[c][:, 1, :].bitcast(BF16).rearrange("p (t m) -> p t m", t=2)
 
         def deplete_late(t, c):
@@ -237,6 +239,14 @@ def tile_list_parts_depletion_kernel(tc, tab_words, tab_scales, offs, wf, wgs, o
                 ALU.mult,
             )
 
+        def deplete_whole(c):
+            nc.vector.tensor_tensor(
+                zz[:, c, :].rearrange("p (m i t) -> p m t i", i=RUN, t=PACK),
+                kept_last[c][:].rearrange("p t (m i) -> p m t i", i=RUN),
+                stocks[1][:, :, half(c)].rearrange("p t (m i) -> p m t i", i=RUN),
+                ALU.mult,
+            )
+
         def weave(c):
             copy, word = (nc.scalar.copy, U32) if c < 2 else (nc.vector.tensor_copy, F32)
             copy(
@@ -247,7 +257,7 @@ def tile_list_parts_depletion_kernel(tc, tab_words, tab_scales, offs, wf, wgs, o
         z_w = {}
 
         def quantize_z(b, c):
-            z_w[b, c] = placed([P, BANK], U32, "z_w%d%d" % (b, c), 28 + 4 * c if b == 0 and c > 0 else KEPT + 8 * b + 2 * c)
+            z_w[b, c] = placed([P, BANK], U32, "z_w%d%d" % (b, c), (KEPT, 32, 36, 38)[c] if b == 0 else 16 + 2 * c)
             if b == 0:
                 z_s[b, c] = placed([P, BANK], U8, "z_s0%d" % c, SECOND + 4 + c)
             nc.vector.quantize_mx(out=z_w[b, c][:].bitcast(FP8X4), scales=z_s[b, c][:], in_=zz[:, c, :])
@@ -362,13 +372,19 @@ def tile_list_parts_depletion_kernel(tc, tab_words, tab_scales, offs, wf, wgs, o
         scatter(5, rates[5][:], all_entries)
         for k in (6, 7):
             scatter(k, weighed[k][:], all_entries)
-        thin(4, everything)
+        paired = slice(0, CHUNKS - 1)
+        ending = placed([P, 2 + PACK, BANK], F32, "ending", KEPT + 4)
+        kept_last = {CHUNKS - 2: ending[:, 0:2, :], CHUNKS - 1: ending[:, 2:, :]}
+        thin(4, paired)
+        thin_last(4, CHUNKS - 1)
         for c in range(CHUNKS):
             interleave(c)
-        thin(5, everything)
-        kept_last = [placed([P, 2, BANK], F32, "kept_last%d" % c, 32 + 4 * c) for c in range(CHUNKS)]
-        pairs = placed([P, CHUNKS, 2, 2 * BANK], BF16, "pairs", 48)
-        for c in range(CHUNKS):
+        thin(5, paired)
+        thin_last(5, CHUNKS - 1)
+        for c in range(CHUNKS - 2):
+            kept_last[c] = placed([P, 2, BANK], F32, "kept_last%d" % c, 32 + 4 * c)
+        pairs = placed([P, CHUNKS - 1, 2, 2 * BANK], BF16, "pairs", 48)
+        for c in range(CHUNKS - 1):
             for t in range(2):
                 deplete_late(t, c)
         for c in range(CHUNKS):
@@ -376,19 +392,20 @@ def tile_list_parts_depletion_kernel(tc, tab_words, tab_scales, offs, wf, wgs, o
         for c in range(CHUNKS - 1):
             pair_up(c)
         for c in range(CHUNKS):
-            if c == CHUNKS - 1:
-                pair_up(c)
             thin_last(7, c)
         quantize_z(0, 0)
         deplete_last(0)
         for c in range(CHUNKS):
             if 0 < c < CHUNKS - 1:
                 quantize_z(0, c + 1)
-            weave(c)
+            if c < CHUNKS - 1:
+                weave(c)
             if c == 0:
                 quantize_z(0, 1)
-            elif c + 1 < CHUNKS:
-                deplete_last(c + 1)
+            elif c == 1:
+                deplete_last(2)
+            elif c == 2:
+                deplete_whole(3)
             quantize_z(1, c)
             if c == 0:
                 deplete_last(1)

@@ -24,7 +24,7 @@ PASSES = K // KP
 TILES = H // P
 CHUNKS = T2 // BANK
 HALVES = S // BANK
-PAGES = 4
+PAGES = 3
 CAP = 43.5
 KIB = 1024
 RUN = 4
@@ -44,7 +44,7 @@ def tile_list_parts_depletion_kernel(tc, tab_words, tab_scales, offs, wf, wgs, o
         tab_s = keep.tile([P, T], U8, name="tab_s", align_bytes=64)
         v_w = {an: keep.tile([P, BANK], U32, name="v_w%d%d" % an, align_bytes=64) for an in ((0, 0), (0, 1), (1, 0), (1, 1))}
         v_s = [keep.tile([P, BANK], U8, name="v_s%d" % n, align_bytes=64) for n in range(HALVES)]
-        pages = [keep.tile([P, T2], F32, name="page%d" % i) for i in range(1)]
+        pages = [keep.tile([P, T2], F32, name="page%d" % i) for i in range(2)]
         z_s = {(1, c): keep.tile([P, BANK], U8, name="z_s1%d" % c, align_bytes=64) for c in range(CHUNKS)}
         wc_w = keep.tile([P, PASSES, 2 * N], U8, name="wc_w", align_bytes=64)
         wc_s = keep.tile([P, PASSES, N], U8, name="wc_s", align_bytes=64)
@@ -65,7 +65,7 @@ def tile_list_parts_depletion_kernel(tc, tab_words, tab_scales, offs, wf, wgs, o
 
         nc.vector.memset(tab_s[:].bitcast(I32), 0)
         for page in pages:
-            nc.vector.memset(page[:], 0.0)
+            nc.vector.memset(page[:].bitcast(I32), 0)
         nc.vector.memset(wc_s[:].rearrange("p a n -> p (a n)").bitcast(I32), 0)
 
         floor = keep.tile([P, 1], F32, name="floor")
@@ -150,15 +150,11 @@ def tile_list_parts_depletion_kernel(tc, tab_words, tab_scales, offs, wf, wgs, o
                         stop=(a == order[-1]),
                     )
 
-        def clear_page(i):
-            pages.append(placed([P, T2], F32, "page%d" % (1 + i), PAGE + 8 * i))
-            nc.gpsimd.memset(pages[-1][:], 0.0)
-
         rates = {}
         survival = {}
 
         def squash(k, n):
-            kib = PAGE + 16 * k if k < 2 and n == 0 else KEPT if (k, n) == (3, 0) else 4 * k + 2 * n if k < PACK else SECOND + 4 * (k - PACK) + 2 * n
+            kib = KEPT if (k, n) == (3, 0) else 4 * k + 2 * n if k < PACK else SECOND + 4 * (k - PACK) + 2 * n
             survival[k, n] = placed([P, BANK], F32, "survival%d%d" % (k, n), kib)
             nc.scalar.activation(out=survival[k, n][:], in_=bank(k, n)[:], func=ACT.Sigmoid, scale=-1.0)
 
@@ -302,9 +298,11 @@ def tile_list_parts_depletion_kernel(tc, tab_words, tab_scales, offs, wf, wgs, o
         round_wf(nc.scalar.copy, 1, 0, 2, 4, ZZ + 4)
         for a in range(PASSES):
             quantize_wf(a, 0, 2)
-        round_wf(nc.vector.tensor_copy, 0, 1, 0, PACK, ZZ + 8)
+        round_wf(nc.vector.tensor_copy, 0, 1, 0, PACK, PAGE)
         quantize_wf(0, 1, 0)
-        round_wf(nc.vector.tensor_copy, 1, 1, 0, PACK, PAGE + 8)
+        round_wf(nc.vector.tensor_copy, 1, 1, 0, PACK, ZZ + 12)
+        pages.append(placed([P, T2], F32, "page2", PAGE))
+        nc.vector.memset(pages[2][:].bitcast(I32), 0)
 
         opening = [(0, 0), (0, 1)]
         first_product(opening, (0, 1))
@@ -314,13 +312,11 @@ def tile_list_parts_depletion_kernel(tc, tab_words, tab_scales, offs, wf, wgs, o
         for cols in pieces:
             logarithm(0, 0, cols)
         logarithm(0, 1)
-        clear_page(0)
         for cols in pieces:
             finish(0, 0, cols)
             scatter_weighing(0, 0, cols)
         finish(0, 1)
         quantize_wf(1, 1, 0)
-        clear_page(1)
         scatter_weighing(0, 1)
         second = [(k, n) for k in (1, 2, 3) for n in range(HALVES)]
         for unit in second:
@@ -328,7 +324,6 @@ def tile_list_parts_depletion_kernel(tc, tab_words, tab_scales, offs, wf, wgs, o
         for step in (squash, logarithm):
             for k, n in second:
                 step(k, n)
-        clear_page(2)
         finish(1, 0)
         scatter_weighing(1, 0)
         whole, all_entries = slice(0, S), slice(0, S // 16)
@@ -338,11 +333,11 @@ def tile_list_parts_depletion_kernel(tc, tab_words, tab_scales, offs, wf, wgs, o
             for n in range(HALVES):
                 finish(k, n)
             weigh(rates[k][:], whole)
+        front, back, everything = slice(0, 2), slice(2, CHUNKS), slice(0, CHUNKS)
+        thin(0, everything)
         scatter(1, rates[1, 1], entries(1))
         for k in (2, 3):
             scatter(k, rates[k][:], all_entries)
-        front, back, everything = slice(0, 2), slice(2, CHUNKS), slice(0, CHUNKS)
-        thin(0, everything)
         for k in range(PACK, TILES):
             for n in range(HALVES):
                 first_product([(k, n)], (1, 0))
@@ -370,13 +365,13 @@ def tile_list_parts_depletion_kernel(tc, tab_words, tab_scales, offs, wf, wgs, o
         for n in range(HALVES):
             scatter(4, rates[4, n], entries(n))
         scatter(5, rates[5][:], all_entries)
-        for k in (6, 7):
-            scatter(k, weighed[k][:], all_entries)
+        scatter(6, weighed[6][:], all_entries)
         paired = slice(0, CHUNKS - 1)
         ending = placed([P, 2 + PACK, BANK], F32, "ending", KEPT + 4)
         kept_last = {CHUNKS - 2: ending[:, 0:2, :], CHUNKS - 1: ending[:, 2:, :]}
         thin(4, paired)
         thin_last(4, CHUNKS - 1)
+        scatter(7, weighed[7][:], all_entries)
         for c in range(CHUNKS):
             interleave(c)
         thin(5, paired)

@@ -154,7 +154,7 @@ def tile_list_parts_depletion_kernel(tc, tab_words, tab_scales, offs, wf, wgs, o
         survival = {}
 
         def squash(k, n):
-            kib = KEPT if (k, n) == (3, 0) else 4 * k + 2 * n if k < PACK else SECOND + 4 * (k - PACK) + 2 * n
+            kib = KEPT if (k, n) == (3, 0) else 4 * k + 2 * n if k < PACK else SECOND + (0, 2, 4, 6, 8, 14, 10, 12)[2 * (k - PACK) + n]
             survival[k, n] = placed([P, BANK], F32, "survival%d%d" % (k, n), kib)
             nc.scalar.activation(out=survival[k, n][:], in_=bank(k, n)[:], func=ACT.Sigmoid, scale=-1.0)
 
@@ -187,10 +187,15 @@ def tile_list_parts_depletion_kernel(tc, tab_words, tab_scales, offs, wf, wgs, o
         def columns(chunks):
             return slice(BANK * chunks.start, BANK * chunks.stop)
 
+        def left(k, chunks):
+            return kept[k, chunks.start][:] if k == 3 else kept[k][:, columns(chunks)]
+
         def thin(k, chunks):
-            if k not in kept:
-                kept[k] = placed([P, T2], F32, "kept%d" % k, (KEPT, ZZ, ZZ + 8, SECOND, SECOND + 8, 0)[k])
-            nc.scalar.activation(out=kept[k][:, columns(chunks)], in_=pages[k % PAGES][:, columns(chunks)], func=ACT.Exp, scale=-1.0)
+            if k == 3:
+                kept[k, chunks.start] = placed([P, T2 // 2], F32, "kept3%d" % chunks.start, SECOND + 2 * chunks.start)
+            elif k not in kept:
+                kept[k] = placed([P, T2], F32, "kept%d" % k, (KEPT, ZZ, ZZ + 8, SECOND, PAGE + 8, 0)[k])
+            nc.scalar.activation(out=left(k, chunks), in_=pages[k % PAGES][:, columns(chunks)], func=ACT.Exp, scale=-1.0)
 
         def thin_last(k, c):
             nc.scalar.activation(out=kept_last[c][:, k - PACK if c == CHUNKS - 1 else k % 2, :], in_=pages[k % PAGES][:, half(c)], func=ACT.Exp, scale=-1.0)
@@ -201,7 +206,7 @@ def tile_list_parts_depletion_kernel(tc, tab_words, tab_scales, offs, wf, wgs, o
                 planes[lo] = placed([P, 2, PACK, BANK], BF16, "planes%d" % lo, 4 * lo)
             nc.gpsimd.tensor_tensor(
                 planes[lo][:, chunks.start - lo : chunks.stop - lo, k, :],
-                kept[k][:, columns(chunks)].rearrange("p (c m) -> p c m", m=BANK),
+                left(k, chunks).rearrange("p (c m) -> p c m", m=BANK),
                 stocks[0][:, k, columns(chunks)].rearrange("p (c m) -> p c m", m=BANK),
                 ALU.mult,
             )
@@ -350,22 +355,21 @@ def tile_list_parts_depletion_kernel(tc, tab_words, tab_scales, offs, wf, wgs, o
             for n in range(HALVES):
                 logarithm(k, n)
                 finish(k, n)
-        for n in range(HALVES):
-            weigh(rates[4, n], half(n))
-        weigh(rates[5][:], whole)
+        weighed = {}
+        for k in (4, 5):
+            weighed[k] = placed([P, S], F32, "weighed%d" % k, SECOND + 4 * (k - 2))
+            weigh(rates[k][:], whole, weighed[k][:])
         thin(2, back)
-        thin(3, everything)
-        deplete(2, back)
         for chunks in (front, back):
+            thin(3, chunks)
+        deplete(2, back)
+        for k, chunks in ((6, front), (7, back)):
             deplete(3, chunks)
-        weighed = {k: placed([P, S], F32, "weighed%d" % k, SECOND + 4 * (k - 6)) for k in (6, 7)}
-        for k in (6, 7):
+            weighed[k] = placed([P, S], F32, "weighed%d" % k, SECOND + 4 * (k - 6))
             weigh(rates[k][:], whole, weighed[k][:])
         zz = placed([P, CHUNKS, PACK * BANK], BF16, "zz", ZZ)
-        for n in range(HALVES):
-            scatter(4, rates[4, n], entries(n))
-        scatter(5, rates[5][:], all_entries)
-        scatter(6, weighed[6][:], all_entries)
+        for k in (4, 5, 6):
+            scatter(k, weighed[k][:], all_entries)
         paired = slice(0, CHUNKS - 1)
         ending = placed([P, 2 + PACK, BANK], F32, "ending", KEPT + 4)
         kept_last = {CHUNKS - 2: ending[:, 0:2, :], CHUNKS - 1: ending[:, 2:, :]}

@@ -105,9 +105,8 @@ def tile_list_parts_depletion_kernel(tc, tab_words, tab_scales, offs, wf, wgs, o
             load_wf(a, 0)
         nc.sync.dma_start(bins[:], offs2)
         load_wf(0, 1)
+        nc.sync.dma_start(out=weights[:], in_=wgs)
         load_wf(1, 1)
-        for n in range(HALVES):
-            nc.sync.dma_start(out=weights[:, half(n)], in_=wgs[:, half(n)])
         nc.sync.dma_start(out=wc_w[:].bitcast(I32), in_=wc_words.rearrange("a p n -> p a n").bitcast(I32))
         for q in range(4):
             nc.sync.dma_start(out=wc_s[32 * q : 32 * q + 4, :, :].bitcast(I32), in_=wc_scales[:, 4 * q : 4 * q + 4, :].rearrange("a r n -> r a n").bitcast(I32))
@@ -127,6 +126,9 @@ def tile_list_parts_depletion_kernel(tc, tab_words, tab_scales, offs, wf, wgs, o
             grouped[a, b, lo] = placed([P, (hi - lo) * KP], BF16, "grouped%d%d%d" % (a, b, lo), kib)
             src = raws[a, b][:].rearrange("p j (m t) -> p m j t", t=PACK)
             copy(out=grouped[a, b, lo][:].rearrange("p (t m j) -> p m j t", t=hi - lo, j=PACK), in_=src[:, :, :, lo:hi])
+
+        def gpsimd_round(out, in_):
+            nc.gpsimd.tensor_scalar(out, in_, 1.0, 0.0, ALU.mult, ALU.add)
 
         def quantize_wf(a, b, lo):
             nc.vector.quantize_mx(out=wf_w[a, b, lo][:].bitcast(FP8X4), scales=wf_s[a, b, lo][:], in_=grouped[a, b, lo][:])
@@ -295,7 +297,7 @@ def tile_list_parts_depletion_kernel(tc, tab_words, tab_scales, offs, wf, wgs, o
         quantize_wf(0, 0, 0)
         gather_words(1, 0)
         gather_words(1, 1)
-        round_wf(nc.vector.tensor_copy, 1, 0, 0, 2, ZZ + 6)
+        round_wf(nc.vector.tensor_copy, 1, 0, 0, 2, PAGE)
         grouped[1, 0, 1] = grouped[1, 0, 0][:, KP : 2 * KP]
         grouped[1, 0, 0] = grouped[1, 0, 0][:, 0:KP]
         for t in range(2):
@@ -303,11 +305,10 @@ def tile_list_parts_depletion_kernel(tc, tab_words, tab_scales, offs, wf, wgs, o
         round_wf(nc.scalar.copy, 1, 0, 2, 4, ZZ + 4)
         for a in range(PASSES):
             quantize_wf(a, 0, 2)
-        round_wf(nc.vector.tensor_copy, 0, 1, 0, PACK, PAGE)
-        quantize_wf(0, 1, 0)
-        round_wf(nc.vector.tensor_copy, 1, 1, 0, PACK, ZZ + 12)
         pages.append(placed([P, T2], F32, "page2", PAGE))
         nc.vector.memset(pages[2][:].bitcast(I32), 0)
+        round_wf(nc.vector.tensor_copy, 0, 1, 0, PACK, PAGE + 8)
+        quantize_wf(0, 1, 0)
 
         opening = [(0, 0), (0, 1)]
         first_product(opening, (0, 1))
@@ -319,10 +320,19 @@ def tile_list_parts_depletion_kernel(tc, tab_words, tab_scales, offs, wf, wgs, o
         logarithm(0, 1)
         for cols in pieces:
             finish(0, 0, cols)
-            scatter_weighing(0, 0, cols)
+            weigh(rates[0, 0][:, cols], cols)
         finish(0, 1)
+        weighed01 = placed([P, BANK], F32, "weighed01", ZZ + 7)
+        weigh(rates[0, 1], half(1), weighed01[:])
+        for cols in pieces:
+            scatter(0, rates[0, 0][:, cols], slice(cols.start // 16, cols.stop // 16))
+        scatter(0, weighed01[:], entries(1))
+        grouped[1, 1, 0] = placed([P, PACK * KP], BF16, "grouped110", RATES + 14)
+        gpsimd_round(
+            grouped[1, 1, 0][:].rearrange("p (t m j) -> p t m j", t=PACK, j=PACK),
+            raws[1, 1][:].rearrange("p j (m t) -> p t m j", t=PACK),
+        )
         quantize_wf(1, 1, 0)
-        scatter_weighing(0, 1)
         second = [(k, n) for k in (1, 2, 3) for n in range(HALVES)]
         for unit in second:
             first_product([unit], (0, 1) if unit[0] == 1 else (1, 0))

@@ -244,7 +244,7 @@ def tile_list_parts_depletion_kernel(tc, tab_words, tab_scales, offs, wf, wgs, o
 
         def deplete_whole(c):
             nc.vector.tensor_tensor(
-                zz[:, c, :].rearrange("p (m i t) -> p m t i", i=RUN, t=PACK),
+                zz[:, c - 1, :].rearrange("p (m i t) -> p m t i", i=RUN, t=PACK),
                 kept_last[c][:].rearrange("p t (m i) -> p m t i", i=RUN),
                 stocks[1][:, :, half(c)].rearrange("p t (m i) -> p m t i", i=RUN),
                 ALU.mult,
@@ -260,10 +260,10 @@ def tile_list_parts_depletion_kernel(tc, tab_words, tab_scales, offs, wf, wgs, o
         z_w = {}
 
         def quantize_z(b, c):
-            z_w[b, c] = placed([P, BANK], U32, "z_w%d%d" % (b, c), (KEPT, 32, 36, 38)[c] if b == 0 else 16 + 2 * c)
+            z_w[b, c] = placed([P, BANK], U32, "z_w%d%d" % (b, c), (KEPT, 32, 36, 38)[c] if b == 0 else ZZ + 2 * c)
             if b == 0:
                 z_s[b, c] = placed([P, BANK], U8, "z_s0%d" % c, SECOND + 4 + c)
-            nc.vector.quantize_mx(out=z_w[b, c][:].bitcast(FP8X4), scales=z_s[b, c][:], in_=zz[:, c, :])
+            nc.vector.quantize_mx(out=z_w[b, c][:].bitcast(FP8X4), scales=z_s[b, c][:], in_=zz[:, c - 1 if (b, c) == (1, CHUNKS - 1) else c, :])
 
         def second_product(b, c, nt):
             nc.tensor.matmul_mx(
@@ -279,7 +279,7 @@ def tile_list_parts_depletion_kernel(tc, tab_words, tab_scales, offs, wf, wgs, o
         def store(c, nt):
             i = N // P * c + nt
             staged = placed([P, BANK], F32, "staged%d" % i, RATES + 2 * i)[:]
-            if c == CHUNKS - 1 and nt != 2:
+            if c == CHUNKS - 1 and nt % 2 == 0:
                 nc.vector.tensor_copy(out=staged, in_=banks[i % 8][:])
             else:
                 nc.scalar.copy(out=staged, in_=banks[i % 8][:])
@@ -369,24 +369,25 @@ def tile_list_parts_depletion_kernel(tc, tab_words, tab_scales, offs, wf, wgs, o
         for k in (4, 5):
             weighed[k] = placed([P, S], F32, "weighed%d" % k, SECOND + 4 * (k - 2))
             weigh(rates[k][:], whole, weighed[k][:])
-        thin(2, back)
-        for chunks in (front, back):
-            thin(3, chunks)
-        deplete(2, back)
-        for k, chunks in ((6, front), (7, back)):
-            deplete(3, chunks)
+        for k, chunks in ((3, front), (2, back), (3, back)):
+            thin(k, chunks)
+        for k, chunks in ((3, front), (2, back), (3, back)):
+            deplete(k, chunks)
+        for k in (6, 7):
             weighed[k] = placed([P, S], F32, "weighed%d" % k, SECOND + 4 * (k - 6))
             weigh(rates[k][:], whole, weighed[k][:])
-        zz = placed([P, CHUNKS, PACK * BANK], BF16, "zz", ZZ)
+        zz = placed([P, CHUNKS, PACK * BANK], BF16, "zz", 16)
         for k in (4, 5, 6):
             scatter(k, weighed[k][:], all_entries)
         paired = slice(0, CHUNKS - 1)
         ending = placed([P, 2 + PACK, BANK], F32, "ending", KEPT + 4)
         kept_last = {CHUNKS - 2: ending[:, 0:2, :], CHUNKS - 1: ending[:, 2:, :]}
+        for c in range(2):
+            interleave(c)
         thin(4, paired)
         thin_last(4, CHUNKS - 1)
         scatter(7, weighed[7][:], all_entries)
-        for c in range(CHUNKS):
+        for c in range(2, CHUNKS):
             interleave(c)
         thin(5, paired)
         thin_last(5, CHUNKS - 1)
@@ -413,9 +414,9 @@ def tile_list_parts_depletion_kernel(tc, tab_words, tab_scales, offs, wf, wgs, o
                 quantize_z(0, 1)
             elif c == 1:
                 deplete_last(2)
-            elif c == 2:
-                deplete_whole(3)
             quantize_z(1, c)
+            if c == 2:
+                deplete_whole(3)
             if c == 0:
                 deplete_last(1)
             for nt in range(N // P):

@@ -1,6 +1,7 @@
 from contextlib import ExitStack
 
 import concourse.mybir as mybir
+from concourse.masks import make_identity
 
 K, H, N, T, S, T2 = 1024, 1024, 512, 2048, 1024, 2048
 FLOPS = 2 * K * H * S + 2 * H * N * T2
@@ -20,12 +21,12 @@ P = 128
 PACK = 4
 KP = P * PACK
 BANK = 512
+HALF = BANK // 2
 PASSES = K // KP
-TILES = H // P
 CHUNKS = T2 // BANK
-HALVES = S // BANK
 PAGES = 3
 CAP = 43.5
+SHIFT = 16.0
 KIB = 1024
 RUN = 4
 
@@ -34,68 +35,46 @@ def tile_list_parts_depletion_kernel(tc, tab_words, tab_scales, offs, wf, wgs, o
     nc = tc.nc
     with ExitStack() as ctx:
         keep = ctx.enter_context(tc.tile_pool(name="keep", bufs=1))
-        ring = ctx.enter_context(tc.tile_pool(name="ring", bufs=1))
         arena = ctx.enter_context(tc.tile_pool(name="arena", bufs=1))
         psum = ctx.enter_context(tc.psum_pool(name="psum", bufs=1))
 
-        parts = keep.tile([P, S // 16], U16, name="parts")
-        bins = keep.tile([P, S // 16], U16, name="bins")
-        landing = keep.tile([P, T // 4], I32, name="landing")
-        tab_s = keep.tile([P, T], U8, name="tab_s", align_bytes=64)
-        v_w = {an: keep.tile([P, BANK], U32, name="v_w%d%d" % an, align_bytes=64) for an in ((0, 0), (0, 1), (1, 0), (1, 1))}
-        v_s = [keep.tile([P, BANK], U8, name="v_s%d" % n, align_bytes=64) for n in range(HALVES)]
-        pages = [keep.tile([P, T2], F32, name="page%d" % i) for i in range(2)]
-        z_s = {(1, c): keep.tile([P, BANK], U8, name="z_s1%d" % c, align_bytes=64) for c in range(CHUNKS)}
-        wc_w = keep.tile([P, PASSES, 2 * N], U8, name="wc_w", align_bytes=64)
-        wc_s = keep.tile([P, PASSES, N], U8, name="wc_s", align_bytes=64)
-        weights = ring.tile([P, S], F32, name="weights", tag="weights", align_bytes=64)
-        banks = [psum.tile([P, BANK], F32, name="bank%d" % i) for i in range(8)]
+        def held(shape, dtype, name):
+            return keep.tile(shape, dtype, name=name, align_bytes=64)
 
         def placed(shape, dtype, name, kib):
             return arena.tile(shape, dtype, name=name, offset=int(kib * KIB), align_bytes=64)
 
-        def slot(shape, dtype, name, tag):
-            return ring.tile(shape, dtype, name=name, tag=tag, align_bytes=64)
+        def span(i, width=BANK, count=1):
+            return slice(width * i, width * (i + count))
 
-        def half(n):
-            return slice(BANK * n, BANK * (n + 1))
+        def entries(cols):
+            return slice(cols.start // 16, cols.stop // 16)
 
-        def entries(n):
-            return slice(BANK // 16 * n, BANK // 16 * (n + 1))
+        parts = keep.tile([P, S // 16], U16, name="parts")
+        bins = keep.tile([P, S // 16], U16, name="bins")
+        tab_s = held([P, T], U8, "tab_s")
+        v_w = {(a, n): held([P, BANK], U32, "v_w%d%d" % (a, n)) for a in range(PASSES) for n in range(2)}
+        v_s = [held([P, BANK], U8, "v_s%d" % n) for n in range(2)]
+        pages = [held([P, T2], F32, "page%d" % i) for i in range(2)]
+        wc_w = held([P, PASSES, 2 * N], U8, "wc_w")
+        wc_s = held([P, PASSES, N], U8, "wc_s")
+        weights = held([P, S], F32, "weights")
+        floor = held([P, 1], F32, "floor")
+        banks = [psum.tile([P, BANK], F32, name="bank%d" % i) for i in range(8)]
 
         nc.vector.memset(tab_s[:].bitcast(I32), 0)
         for page in pages:
             nc.vector.memset(page[:].bitcast(I32), 0)
         nc.vector.memset(wc_s[:].rearrange("p a n -> p (a n)").bitcast(I32), 0)
-
-        floor = keep.tile([P, 1], F32, name="floor")
         nc.scalar.activation(out=floor[:], in_=pages[0][:, 0:1], func=ACT.Sigmoid, bias=-CAP)
 
+        landing = placed([P, T // 4], I32, "landing", 200)
         tab_w = [placed([P, T], I32, "tab_w%d" % a, 8 * a) for a in range(PASSES)]
-        KEPT, SECOND, RATES, ZZ, PAGE = 64, 80, 128, 160, 176
-        raws = {ab: placed([P, PACK, KP], F32, "raw%d%d" % ab, kib) for ab, kib in (((0, 0), 16), ((1, 0), RATES + 20), ((0, 1), KEPT), ((1, 1), KEPT + 8))}
-        wf_w = {(0, 0, 0): placed([P, 2 * P], U32, "wf_w000", 24)}
-        wf_s = {(0, 0, 0): placed([P, 2 * P], U8, "wf_s000", 26)}
-        for t in range(2):
-            wf_w[1, 0, t] = placed([P, P], U32, "wf_w10%d" % t, 25 + 0.5 * t)
-        wf_s[1, 0, 0] = placed([P, P], U8, "wf_s100", RATES + 8)
-        wf_s[1, 0, 1] = placed([P, P], U8, "wf_s101", 27)
-        wf_w[0, 0, 2] = placed([P, 2 * P], U32, "wf_w002", RATES + 20)
-        wf_w[1, 0, 2] = placed([P, 2 * P], U32, "wf_w102", RATES + 2)
-        wf_s[0, 0, 2] = placed([P, 2 * P], U8, "wf_s002", RATES + 18)
-        wf_s[1, 0, 2] = placed([P, 2 * P], U8, "wf_s102", RATES + 11)
-        wf_w[0, 1, 0] = placed([P, KP], U32, "wf_w01", RATES)
-        wf_w[1, 1, 0] = placed([P, KP], U32, "wf_w11", ZZ + 7)
-        wf_s[0, 1, 0] = placed([P, KP], U8, "wf_s01", RATES + 6)
-        wf_s[1, 1, 0] = placed([P, KP], U8, "wf_s11", RATES + 9.5)
+        raws = {(a, b): placed([P, PACK, KP], F32, "raw%d%d" % (a, b), 16 + 8 * a + 16 * b) for a in range(PASSES) for b in range(PASSES)}
+        stocks = [placed([P, PACK, T2], F32, "stock%d" % b, 76 + 32 * b) for b in range(PASSES)]
 
         def load_wf(a, b):
-            nc.sync.dma_start(out=raws[a, b][:], in_=wf[KP * a : KP * (a + 1), KP * b : KP * (b + 1)].rearrange("(p j) c -> p j c", j=PACK))
-
-        stocks = [placed([P, PACK, T2], F32, "stock%d" % b, 32 + 64 * b) for b in range(PASSES)]
-
-        def load_stock(b, ts):
-            nc.sync.dma_start(out=stocks[b][:, ts, :], in_=stock[KP * b : KP * (b + 1), :].rearrange("(p t) m -> p t m", t=PACK)[:, ts, :])
+            nc.sync.dma_start(out=raws[a, b][:], in_=wf[span(a, KP), span(b, KP)].rearrange("(p j) c -> p j c", j=PACK))
 
         nc.sync.dma_start(parts[:], offs)
         for q in range(4):
@@ -111,316 +90,417 @@ def tile_list_parts_depletion_kernel(tc, tab_words, tab_scales, offs, wf, wgs, o
         for q in range(4):
             nc.sync.dma_start(out=wc_s[32 * q : 32 * q + 4, :, :].bitcast(I32), in_=wc_scales[:, 4 * q : 4 * q + 4, :].rearrange("a r n -> r a n").bitcast(I32))
         for b in range(PASSES):
-            load_stock(b, slice(0, 2))
-            load_stock(b, slice(2, 4))
+            for u in range(2):
+                nc.sync.dma_start(out=stocks[b][:, span(u, 2), :], in_=stock[span(b, KP), :].rearrange("(p t) m -> p t m", t=PACK)[:, span(u, 2), :])
 
-        def gather_words(a, n):
-            nc.vector.tensor_copy(v_w[a, n][:], tab_w[a][:].bitcast(U32).indirect(parts[:, entries(n)]))
+        for q in range(4):
+            rows = slice(32 * q, 32 * q + 4 * PASSES)
+            nc.vector.tensor_copy(out=tab_s[rows, :].bitcast(I32), in_=landing[rows, :])
+        identity = placed([P, P], F32, "identity", 200)
+        make_identity(nc, identity[:])
 
-        def gather_scales(n):
-            nc.vector.tensor_copy(v_s[n][:], tab_s[:].indirect(parts[:, entries(n)]))
+        def gather_words(a):
+            for n in range(2):
+                nc.vector.tensor_copy(v_w[a, n][:], tab_w[a][:].bitcast(U32).indirect(parts[:, entries(span(n))]))
 
-        grouped = {}
+        grouped, wf_w, wf_s = {}, {}, {}
 
         def round_wf(copy, a, b, lo, hi, kib):
-            grouped[a, b, lo] = placed([P, (hi - lo) * KP], BF16, "grouped%d%d%d" % (a, b, lo), kib)
+            whole = placed([P, (hi - lo) * KP], BF16, "grouped%d%d%d" % (a, b, lo), kib)
             src = raws[a, b][:].rearrange("p j (m t) -> p m j t", t=PACK)
-            copy(out=grouped[a, b, lo][:].rearrange("p (t m j) -> p m j t", t=hi - lo, j=PACK), in_=src[:, :, :, lo:hi])
+            copy(out=whole[:].rearrange("p (t m j) -> p m j t", t=hi - lo, j=PACK), in_=src[:, :, :, lo:hi])
+            grouped[a, b, lo] = whole
 
-        def gpsimd_round(out, in_):
-            nc.gpsimd.tensor_scalar(out, in_, 1.0, 0.0, ALU.mult, ALU.add)
+        def quantize_wf(a, b, t, count, source, codes_kib, scales_kib):
+            codes = placed([P, count * P], U32, "wf_w%d%d%d" % (a, b, t), codes_kib)
+            scales = placed([P, count * P], U8, "wf_s%d%d%d" % (a, b, t), scales_kib)
+            nc.vector.quantize_mx(out=codes[:].bitcast(FP8X4), scales=scales[:], in_=grouped[a, b, source][:, span(t - source, KP, count)])
+            for i in range(count):
+                wf_w[a, b, t + i], wf_s[a, b, t + i] = codes[:, span(i, P)], scales[:, span(i, P)]
+            wf_w[a, b, t, count], wf_s[a, b, t, count] = codes[:], scales[:]
 
-        def quantize_wf(a, b, lo):
-            nc.vector.quantize_mx(out=wf_w[a, b, lo][:].bitcast(FP8X4), scales=wf_s[a, b, lo][:], in_=grouped[a, b, lo][:])
+        for n in range(2):
+            nc.vector.tensor_copy(v_s[n][:], tab_s[:].indirect(parts[:, entries(span(n))]))
+        gather_words(0)
+        round_wf(nc.scalar.copy, 0, 0, 0, 2, 50)
+        round_wf(nc.scalar.copy, 0, 0, 2, 4, 52)
+        quantize_wf(0, 0, 0, 2, 0, 66, 73)
+        gather_words(1)
+        round_wf(nc.vector.tensor_copy, 1, 0, 0, 2, 54)
+        quantize_wf(1, 0, 0, 1, 0, 67, 140)
+        quantize_wf(1, 0, 1, 1, 0, 67.5, 73.25)
+        round_wf(nc.scalar.copy, 1, 0, 2, 4, 56)
+        quantize_wf(0, 0, 2, 2, 2, 24, 146)
+        quantize_wf(1, 0, 2, 2, 2, 68, 73.5)
+        pages.append(placed([P, T2], F32, "page2", 50))
+        nc.vector.memset(pages[2][:].bitcast(I32), 0)
+        round_wf(nc.vector.tensor_copy, 0, 1, 0, PACK, 58)
+        quantize_wf(0, 1, 0, 2, 0, 69, 62)
+        quantize_wf(0, 1, 2, 2, 0, 71, 74)
 
         def bank(k, n):
-            return banks[(HALVES * k + n) % 8]
+            return banks[(2 * k + n) % 8]
 
         def first_product(units, order):
             for a in order:
                 for k, n in units:
                     b, t = divmod(k, PACK)
-                    lo = max(start for pass_, block, start in wf_w if (pass_, block) == (a, b) and start <= t)
-                    rows = slice(P * (t - lo), P * (t - lo + 1))
                     nc.tensor.matmul_mx(
                         out=bank(k, n)[:],
-                        lhsT=wf_w[a, b, lo][:, rows].bitcast(FP8X4),
-                        lhsT_scale=wf_s[a, b, lo][:, rows],
+                        lhsT=wf_w[a, b, t].bitcast(FP8X4),
+                        lhsT_scale=wf_s[a, b, t],
                         rhs=v_w[a, n][:].bitcast(FP8X4),
                         rhs_scale=v_s[n][4 * a : P, :],
                         start=(a == order[0]),
                         stop=(a == order[-1]),
                     )
 
-        rates = {}
-        survival = {}
+        survival, rates = {}, {}
+        every = slice(0, BANK)
 
         def squash(k, n):
-            kib = KEPT if (k, n) == (3, 0) else 4 * k + 2 * n if k < PACK else SECOND + (0, 2, 4, 6, 8, 14, 10, 12)[2 * (k - PACK) + n]
-            survival[k, n] = placed([P, BANK], F32, "survival%d%d" % (k, n), kib)
+            survival[k, n] = placed([P, BANK], F32, "survival%d%d" % (k, n), 4 * k + 2 * n)
             nc.scalar.activation(out=survival[k, n][:], in_=bank(k, n)[:], func=ACT.Sigmoid, scale=-1.0)
 
-        def logarithm(k, n, cols=slice(0, BANK)):
-            if (k, n) in rates:
-                pass
-            elif k < 2:
-                rates[k, n] = placed([P, BANK], F32, "rates%d%d" % (k, n), RATES + (8, 16, 18, 11)[2 * k + n])[:]
-            elif n == 0:
-                rates[k] = placed([P, S], F32, "rates%d" % k, RATES + (2, 20, 0, 4, 8, 12)[k - 2])
-                rates[k, 0], rates[k, 1] = rates[k][:, half(0)], rates[k][:, half(1)]
+        def rate_tile(k, kibs):
+            if len(kibs) == 2:
+                for n in range(2):
+                    rates[k, n] = placed([P, BANK], F32, "rates%d%d" % (k, n), kibs[n])[:]
+            else:
+                rates[k] = placed([P, S], F32, "rates%d" % k, kibs[0])[:]
+                rates[k, 0], rates[k, 1] = rates[k][:, span(0)], rates[k][:, span(1)]
+
+        def logarithm(k, n, cols=every):
             nc.scalar.activation(out=rates[k, n][:, cols], in_=survival[k, n][:, cols], func=ACT.Ln, bias=floor[:])
 
-        def finish(k, n, cols=slice(0, BANK)):
+        def finish(k, n, cols=every):
             nc.vector.scalar_tensor_tensor(out=rates[k, n][:, cols], in0=rates[k, n][:, cols], scalar=-1.0, in1=bank(k, n)[:, cols], op0=ALU.mult, op1=ALU.max)
 
-        def weigh(part, cols, into=None):
-            nc.gpsimd.tensor_tensor(part if into is None else into, part, weights[:, cols], ALU.mult)
+        def weigh(into, part, cols):
+            nc.gpsimd.tensor_tensor(into, part, weights[:, cols], ALU.mult)
 
-        def scatter_weighing(k, n, cols=slice(0, BANK)):
-            lo, hi = BANK * n + cols.start, BANK * n + cols.stop
-            nc.vector.tensor_tensor(pages[k % PAGES][:].indirect(bins[:, lo // 16 : hi // 16]), rates[k, n][:, cols], weights[:, lo:hi], ALU.mult)
+        def scatter(k, part, cols):
+            nc.vector.tensor_copy(pages[k % PAGES][:].indirect(bins[:, entries(cols)]), part)
 
-        def scatter(k, part, names):
-            nc.vector.tensor_copy(pages[k % PAGES][:].indirect(bins[:, names]), part)
-
-        kept = {}
-        planes = {}
-
-        def columns(chunks):
-            return slice(BANK * chunks.start, BANK * chunks.stop)
-
-        def left(k, chunks):
-            return kept[k, chunks.start][:] if k == 3 else kept[k][:, columns(chunks)]
-
-        def thin(k, chunks):
-            if k == 3:
-                kept[k, chunks.start] = placed([P, T2 // 2], F32, "kept3%d" % chunks.start, SECOND + 2 * chunks.start)
-            elif k not in kept:
-                kept[k] = placed([P, T2], F32, "kept%d" % k, (KEPT, ZZ, ZZ + 8, SECOND, PAGE + 8, 0)[k])
-            nc.scalar.activation(out=left(k, chunks), in_=pages[k % PAGES][:, columns(chunks)], func=ACT.Exp, scale=-1.0)
-
-        def thin_last(k, c):
-            nc.scalar.activation(out=kept_last[c][:, k - PACK if c == CHUNKS - 1 else k % 2, :], in_=pages[k % PAGES][:, half(c)], func=ACT.Exp, scale=-1.0)
-
-        def deplete(k, chunks):
-            lo = 2 * (chunks.start // 2)
-            if lo not in planes:
-                planes[lo] = placed([P, 2, PACK, BANK], BF16, "planes%d" % lo, 4 * lo)
-            nc.gpsimd.tensor_tensor(
-                planes[lo][:, chunks.start - lo : chunks.stop - lo, k, :],
-                left(k, chunks).rearrange("p (c m) -> p c m", m=BANK),
-                stocks[0][:, k, columns(chunks)].rearrange("p (c m) -> p c m", m=BANK),
-                ALU.mult,
-            )
-
-        def interleave(c):
-            lo = 2 * (c // 2)
-            nc.scalar.copy(
-                out=zz[:, c, :].rearrange("p (m i t) -> p m t i", i=RUN, t=PACK),
-                in_=planes[lo][:, c - lo, :, :].rearrange("p t (m i) -> p m t i", i=RUN),
-            )
-
-        def late_planes(c):
-            if c == CHUNKS - 2:
-                return ending[:, 1 :: PACK, :].bitcast(BF16)[:, :, 0:BANK]
-            return kept_last[c][:, 1, :].bitcast(BF16).rearrange("p (t m) -> p t m", t=2)
-
-        def deplete_late(t, c):
-            nc.gpsimd.tensor_tensor(late_planes(c)[:, t, :], kept[PACK + t][:, half(c)], stocks[1][:, t, half(c)], ALU.mult)
-
-        def in_pairs(c, u):
-            return pairs[:, c, u, :].rearrange("p (m i t) -> p m t i", i=RUN, t=2)
-
-        def pair_up(c):
-            nc.scalar.copy(out=in_pairs(c, 0), in_=late_planes(c).rearrange("p t (m i) -> p m t i", i=RUN))
-
-        def deplete_last(c):
-            nc.vector.tensor_tensor(
-                in_pairs(c, 1),
-                kept_last[c][:].rearrange("p t (m i) -> p m t i", i=RUN),
-                stocks[1][:, 2:4, half(c)].rearrange("p t (m i) -> p m t i", i=RUN),
-                ALU.mult,
-            )
-
-        def deplete_whole(c):
-            nc.vector.tensor_tensor(
-                zz[:, c - 1, :].rearrange("p (m i t) -> p m t i", i=RUN, t=PACK),
-                kept_last[c][:].rearrange("p t (m i) -> p m t i", i=RUN),
-                stocks[1][:, :, half(c)].rearrange("p t (m i) -> p m t i", i=RUN),
-                ALU.mult,
-            )
-
-        def weave(c):
-            copy, word = (nc.scalar.copy, U32) if c < 2 else (nc.vector.tensor_copy, F32)
-            copy(
-                out=zz[:, c, :].bitcast(word).rearrange("p (m i u) -> p m u i", u=2, i=2),
-                in_=pairs[:, c, :, :].bitcast(word).rearrange("p u (m i) -> p m u i", i=2),
-            )
-
-        z_w = {}
-
-        def quantize_z(b, c):
-            z_w[b, c] = placed([P, BANK], U32, "z_w%d%d" % (b, c), (KEPT, 32, 36, 38)[c] if b == 0 else ZZ + 2 * c)
-            if b == 0:
-                z_s[b, c] = placed([P, BANK], U8, "z_s0%d" % c, SECOND + 4 + c)
-            nc.vector.quantize_mx(out=z_w[b, c][:].bitcast(FP8X4), scales=z_s[b, c][:], in_=zz[:, c - 1 if (b, c) == (1, CHUNKS - 1) else c, :])
-
-        def second_product(b, c, nt):
-            nc.tensor.matmul_mx(
-                out=banks[(N // P * c + nt) % 8][:],
-                lhsT=wc_w[:, b, 2 * P * nt : 2 * P * (nt + 1)].bitcast(FP4X4),
-                lhsT_scale=wc_s[:, b, P * nt : P * (nt + 1)],
-                rhs=z_w[b, c][:].bitcast(FP8X4),
-                rhs_scale=z_s[b, c][:],
-                start=(b == 0),
-                stop=(b == PASSES - 1),
-            )
-
-        def store(c, nt):
-            i = N // P * c + nt
-            staged = placed([P, BANK], F32, "staged%d" % i, RATES + 2 * i)[:]
-            if c == CHUNKS - 1 and nt % 2 == 0:
-                nc.vector.tensor_copy(out=staged, in_=banks[i % 8][:])
-            else:
-                nc.scalar.copy(out=staged, in_=banks[i % 8][:])
-            nc.sync.dma_start(out=out[P * nt : P * (nt + 1), half(c)], in_=staged)
-
-        for q in range(4):
-            rows = slice(32 * q, 32 * q + 4 * PASSES)
-            nc.vector.tensor_copy(out=tab_s[rows, :].bitcast(I32), in_=landing[rows, :])
-        gather_scales(0)
-        gather_scales(1)
-        gather_words(0, 0)
-        gather_words(0, 1)
-        round_wf(nc.scalar.copy, 0, 0, 0, 2, ZZ)
-        round_wf(nc.scalar.copy, 0, 0, 2, 4, ZZ + 2)
-        quantize_wf(0, 0, 0)
-        gather_words(1, 0)
-        gather_words(1, 1)
-        round_wf(nc.vector.tensor_copy, 1, 0, 0, 2, PAGE)
-        grouped[1, 0, 1] = grouped[1, 0, 0][:, KP : 2 * KP]
-        grouped[1, 0, 0] = grouped[1, 0, 0][:, 0:KP]
-        for t in range(2):
-            quantize_wf(1, 0, t)
-        round_wf(nc.scalar.copy, 1, 0, 2, 4, ZZ + 4)
-        for a in range(PASSES):
-            quantize_wf(a, 0, 2)
-        pages.append(placed([P, T2], F32, "page2", PAGE))
-        nc.vector.memset(pages[2][:].bitcast(I32), 0)
-        round_wf(nc.vector.tensor_copy, 0, 1, 0, PACK, PAGE + 8)
-        quantize_wf(0, 1, 0)
-
+        whole_list = slice(0, S)
         opening = [(0, 0), (0, 1)]
         first_product(opening, (0, 1))
         for k, n in opening:
             squash(k, n)
+        rate_tile(0, (140, 144))
         pieces = [slice(0, P), slice(P, BANK)]
         for cols in pieces:
             logarithm(0, 0, cols)
         logarithm(0, 1)
         for cols in pieces:
             finish(0, 0, cols)
-            weigh(rates[0, 0][:, cols], cols)
+            weigh(rates[0, 0][:, cols], rates[0, 0][:, cols], cols)
         finish(0, 1)
-        weighed01 = placed([P, BANK], F32, "weighed01", ZZ + 7)
-        weigh(rates[0, 1], half(1), weighed01[:])
+        weighed01 = placed([P, BANK], F32, "weighed01", 166)
+        weigh(weighed01[:], rates[0, 1], span(1))
         for cols in pieces:
-            scatter(0, rates[0, 0][:, cols], slice(cols.start // 16, cols.stop // 16))
-        scatter(0, weighed01[:], entries(1))
-        grouped[1, 1, 0] = placed([P, PACK * KP], BF16, "grouped110", RATES + 14)
-        gpsimd_round(
+            scatter(0, rates[0, 0][:, cols], cols)
+        scatter(0, weighed01[:], span(1))
+        grouped[1, 1, 0] = placed([P, PACK * KP], BF16, "grouped110", 142)
+        nc.gpsimd.tensor_scalar(
             grouped[1, 1, 0][:].rearrange("p (t m j) -> p t m j", t=PACK, j=PACK),
             raws[1, 1][:].rearrange("p j (m t) -> p t m j", t=PACK),
+            1.0,
+            0.0,
+            ALU.mult,
+            ALU.add,
         )
-        quantize_wf(1, 1, 0)
-        second = [(k, n) for k in (1, 2, 3) for n in range(HALVES)]
+        quantize_wf(1, 1, 0, 2, 0, 70, 73.75)
+        quantize_wf(1, 1, 2, 2, 0, 72, 74.25)
+
+        second = [(k, n) for k in (1, 2, 3) for n in range(2)]
         for unit in second:
             first_product([unit], (0, 1) if unit[0] == 1 else (1, 0))
-        for step in (squash, logarithm):
-            for k, n in second:
-                step(k, n)
+        for k, n in second:
+            squash(k, n)
+        rate_tile(1, (146, 148))
+        rate_tile(2, (150,))
+        rate_tile(3, (154,))
+        for k, n in second:
+            logarithm(k, n)
         finish(1, 0)
-        scatter_weighing(1, 0)
-        whole, all_entries = slice(0, S), slice(0, S // 16)
+        nc.vector.tensor_tensor(pages[1][:].indirect(bins[:, entries(span(0))]), rates[1, 0], weights[:, span(0)], ALU.mult)
         finish(1, 1)
-        weigh(rates[1, 1], half(1))
+        weigh(rates[1, 1], rates[1, 1], span(1))
         for k in (2, 3):
-            for n in range(HALVES):
+            for n in range(2):
                 finish(k, n)
-            weigh(rates[k][:], whole)
-        front, back, everything = slice(0, 2), slice(2, CHUNKS), slice(0, CHUNKS)
-        thin(0, everything)
-        scatter(1, rates[1, 1], entries(1))
-        for k in (2, 3):
-            scatter(k, rates[k][:], all_entries)
-        for k in range(PACK, TILES):
-            for n in range(HALVES):
-                first_product([(k, n)], (1, 0))
-                squash(k, n)
-        thin(1, everything)
-        thin(2, front)
-        for k, chunks in ((0, front), (0, back), (1, front), (1, back), (2, front)):
-            deplete(k, chunks)
-        for k in range(PACK, TILES):
-            for n in range(HALVES):
-                logarithm(k, n)
-                finish(k, n)
-        weighed = {}
-        for k in (4, 5):
-            weighed[k] = placed([P, S], F32, "weighed%d" % k, SECOND + 4 * (k - 2))
-            weigh(rates[k][:], whole, weighed[k][:])
-        for k, chunks in ((3, front), (2, back), (3, back)):
-            thin(k, chunks)
-        for k, chunks in ((3, front), (2, back), (3, back)):
-            deplete(k, chunks)
-        for k in (6, 7):
-            weighed[k] = placed([P, S], F32, "weighed%d" % k, SECOND + 4 * (k - 6))
-            weigh(rates[k][:], whole, weighed[k][:])
-        zz = placed([P, CHUNKS, PACK * BANK], BF16, "zz", 16)
-        for k in (4, 5, 6):
-            scatter(k, weighed[k][:], all_entries)
-        paired = slice(0, CHUNKS - 1)
-        ending = placed([P, 2 + PACK, BANK], F32, "ending", KEPT + 4)
-        kept_last = {CHUNKS - 2: ending[:, 0:2, :], CHUNKS - 1: ending[:, 2:, :]}
-        for c in range(2):
-            interleave(c)
-        thin(4, paired)
-        thin_last(4, CHUNKS - 1)
-        scatter(7, weighed[7][:], all_entries)
-        for c in range(2, CHUNKS):
-            interleave(c)
-        thin(5, paired)
-        thin_last(5, CHUNKS - 1)
-        for c in range(CHUNKS - 2):
-            kept_last[c] = placed([P, 2, BANK], F32, "kept_last%d" % c, 32 + 4 * c)
-        pairs = placed([P, CHUNKS - 1, 2, 2 * BANK], BF16, "pairs", 48)
-        for c in range(CHUNKS - 1):
-            for t in range(2):
-                deplete_late(t, c)
+            weigh(rates[k], rates[k], whole_list)
+        scatter(1, rates[1, 1], span(1))
+        scatter(2, rates[2], whole_list)
+
+        third = [(k, n) for k in (4, 5) for n in range(2)]
+        for unit in third:
+            first_product([unit], (1, 0))
+            squash(*unit)
+
+        def thin(k, into, cols):
+            nc.scalar.activation(out=into, in_=pages[k % PAGES][:, cols], func=ACT.Exp, scale=-1.0)
+
+        def by_chunk(ap):
+            return ap.rearrange("p (c m) -> p c m", m=BANK)
+
+        front, back, page_wide = span(1, 2 * BANK), span(0, 2 * BANK), slice(0, T2)
+        planes = {2: placed([P, 2, PACK, BANK], BF16, "planes_front", 168), 0: placed([P, 2, PACK, BANK], BF16, "planes_back", 176)}
+
+        def deplete(t, left, cols):
+            first, count = cols.start // BANK, (cols.stop - cols.start) // BANK
+            lo = 2 * (first // 2)
+            nc.gpsimd.tensor_tensor(planes[lo][:, first - lo : first - lo + count, t, :], by_chunk(left), by_chunk(stocks[0][:, t, cols]), ALU.mult)
+
+        kept0 = placed([P, T2], F32, "kept0", 58)
+        thin(0, kept0[:], page_wide)
+
+        lifted, decay, excess = [], [], []
+        for g in range(4):
+            for i in range(2):
+                n, q = divmod(2 * g + i, PACK)
+                for a in (1, 0):
+                    nc.tensor.matmul_mx(
+                        out=banks[4 + g][:, span(i, HALF)],
+                        lhsT=v_w[a, n][:, span(q, P)].bitcast(FP8X4),
+                        lhsT_scale=v_s[n][4 * a : P, span(q, P)],
+                        rhs=wf_w[a, 1, 2, 2].bitcast(FP8X4),
+                        rhs_scale=wf_s[a, 1, 2, 2],
+                        start=(a == 1),
+                        stop=(a == 0),
+                    )
+            lifted.append(placed([P, BANK], F32, "lifted%d" % g, 24 + 2 * g))
+            nc.scalar.activation(out=lifted[g][:], in_=banks[4 + g][:], func=ACT.Relu, bias=SHIFT)
+        for g in range(4):
+            decay.append(placed([P, BANK], F32, "decay%d" % g, 32 + 2 * g))
+            nc.scalar.activation(out=decay[g][:], in_=lifted[g][:], func=ACT.Exp, scale=-1.0, bias=SHIFT)
+
+        kept1 = placed([P, T2], F32, "kept1", 0)
+        thin(1, kept1[:], page_wide)
+        kept2a = placed([P, BANK], F32, "kept2a", 8)
+        thin(2, kept2a[:], span(3))
+        scatter(3, rates[3], whole_list)
+        for t, left in ((0, kept0), (1, kept1)):
+            for cols in (front, back):
+                deplete(t, left[:, cols], cols)
+        deplete(2, kept2a[:], span(3))
+
+        rate_tile(4, (158, 160))
+        rate_tile(5, (162,))
+        for k, n in third:
+            logarithm(k, n)
+        for g in range(4):
+            excess.append(placed([P, BANK], F32, "excess%d" % g, 188 + 2 * g))
+            nc.scalar.activation(out=excess[g][:], in_=decay[g][:], func=ACT.Ln, bias=1.0)
+        for k, n in third:
+            finish(k, n)
+        for n in range(2):
+            weighed = placed([P, BANK], F32, "weighed4%d" % n, 20 + 2 * n)
+            weigh(weighed[:], rates[4, n], span(n))
+            scatter(4, weighed[:], span(n))
+        weigh(rates[5], rates[5], whole_list)
+        for t in range(2):
+            for jt in range(2 * PACK):
+                n, q = divmod(jt, PACK)
+                g, i = divmod(jt, 2)
+                for term in (lifted, excess):
+                    nc.tensor.matmul(
+                        banks[4 + 2 * t + n][:, span(q, P)],
+                        lhsT=term[g][:, span(2 * i + t, P)],
+                        rhs=identity[:],
+                        is_transpose=True,
+                        start=(term is lifted),
+                        stop=(term is excess),
+                    )
+
+        kept3f = placed([P, 2 * BANK], F32, "kept3f", 184)
+        thin(3, kept3f[:], front)
+
+        def lower(t, kib):
+            rate_tile(6 + t, (kib,))
+            for n in range(2):
+                nc.scalar.activation(out=rates[6 + t, n], in_=banks[4 + 2 * t + n][:], func=ACT.Copy, bias=-SHIFT)
+
+        lower(0, 16)
+        kept2r = placed([P, 3 * BANK], F32, "kept2r", 10)
+        thin(2, kept2r[:], span(0, 3 * BANK))
+        kept3b = placed([P, 2 * BANK], F32, "kept3b", 40)
+        thin(3, kept3b[:], back)
+        scatter(5, rates[5], whole_list)
+        lower(1, 150)
+        deplete(3, kept3f[:], front)
+        weigh(rates[6], rates[6], whole_list)
+        deplete(2, kept2r[:, span(2)], span(2))
+        deplete(2, kept2r[:, back], back)
+        deplete(3, kept3b[:], back)
+        weigh(rates[7], rates[7], whole_list)
+        scatter(6, rates[6], whole_list)
+
+        zz = {}
+
+        def interleave(c, kib):
+            zz[0, c] = placed([P, PACK * BANK], BF16, "zz0%d" % c, kib)
+            nc.scalar.copy(
+                out=zz[0, c][:].rearrange("p (m i t) -> p m t i", i=RUN, t=PACK),
+                in_=planes[2 * (c // 2)][:, c % 2, :, :].rearrange("p t (m i) -> p m t i", i=RUN),
+            )
+
+        paired = span(1, BANK, 3)
+        kept4 = placed([P, 3 * BANK], F32, "kept4", 0)
+        thin(4, kept4[:], paired)
+        interleave(3, 58)
+        interleave(2, 62)
+        kept5 = placed([P, 3 * BANK], F32, "kept5", 168)
+        thin(5, kept5[:], paired)
+        ending = placed([P, 10 * BANK], F32, "ending", 29)
+        for t in range(2):
+            thin(4 + t, ending[:, span(t)], span(0))
+        scatter(7, rates[7], whole_list)
+        interleave(1, 140)
+
+        def late_planes(c):
+            rows = ending[:].bitcast(BF16).rearrange("p (r x) -> p r x", x=2 * BANK)
+            return rows[:, 5:8:2, span(0)] if c == 3 else rows[:, 3::6, span(c - 1)]
+
+        def by_half(ap):
+            return ap.rearrange("p (h m) -> p h m", h=2)
+
+        descending = (3, 2, 1)
+        for c in descending:
+            for t, left in ((0, kept4), (1, kept5)):
+                nc.gpsimd.tensor_tensor(late_planes(c)[:, t, :], left[:, span(c - 1)], stocks[1][:, t, span(c)], ALU.mult)
         for c in range(CHUNKS):
-            thin_last(6, c)
-        for c in range(CHUNKS - 1):
-            pair_up(c)
-        for c in range(CHUNKS):
-            thin_last(7, c)
-        quantize_z(0, 0)
-        deplete_last(0)
-        for c in range(CHUNKS):
-            if 0 < c < CHUNKS - 1:
-                quantize_z(0, c + 1)
-            if c < CHUNKS - 1:
-                weave(c)
-            if c == 0:
-                quantize_z(0, 1)
-            elif c == 1:
-                deplete_last(2)
-            quantize_z(1, c)
-            if c == 2:
-                deplete_whole(3)
-            if c == 0:
-                deplete_last(1)
+            thin(6, ending[:, span(2 + 2 * c)], span(c))
+        pairs = {}
+        for c, kib in zip(descending, (160, 164, 184)):
+            pairs[c] = placed([P, 2, 2 * BANK], BF16, "pairs%d" % c, kib)
+            nc.scalar.copy(
+                out=pairs[c][:, 0, :].rearrange("p (m i t) -> p m t i", i=RUN, t=2),
+                in_=late_planes(c).rearrange("p t (m i) -> p m t i", i=RUN),
+            )
+        zz[0, 0] = placed([P, PACK * BANK], BF16, "zz00", 168)
+        nc.gpsimd.tensor_scalar(zz[0, 0][:].rearrange("p (m t) -> p m t", t=PACK), planes[0][:, 0, :, :].rearrange("p t m -> p m t"), 1.0, 0.0, ALU.mult, ALU.add)
+
+        halves = [span(0, HALF), span(1, HALF)]
+
+        def within(c, cols):
+            return slice(BANK * c + cols.start, BANK * c + cols.stop)
+
+        def times(cols, factor):
+            return slice(cols.start * factor, cols.stop * factor)
+
+        def thin_last(c, cols=every):
+            thin(7, ending[:, within(3 + 2 * c, cols)], within(c, cols))
+
+        def deplete_pair(c, cols=every):
+            nc.vector.tensor_tensor(
+                pairs[c][:, 1, times(cols, 2)].rearrange("p (m i t) -> p m t i", i=RUN, t=2),
+                by_chunk(ending[:, span(1 + c, 2 * BANK)])[:, :, cols].rearrange("p t (m i) -> p m t i", i=RUN),
+                stocks[1][:, 2:4, within(c, cols)].rearrange("p t (m i) -> p m t i", i=RUN),
+                ALU.mult,
+            )
+
+        def weave(copy, word, c, cols=every):
+            copy(
+                out=zz[1, c][:].bitcast(word)[:, times(cols, 2)].rearrange("p (m i u) -> p m u i", u=2, i=2),
+                in_=pairs[c][:].bitcast(word)[:, :, cols].rearrange("p u (m i) -> p m u i", i=2),
+            )
+
+        def deplete_whole(h, kib):
+            zz[1, 0, h] = placed([P, PACK * HALF], BF16, "zz10%d" % h, kib)
+            nc.vector.tensor_tensor(
+                zz[1, 0, h][:].rearrange("p (m i t) -> p m t i", i=RUN, t=PACK),
+                by_chunk(ending[:, span(0, PACK * BANK)])[:, :, halves[h]].rearrange("p t (m i) -> p m t i", i=RUN),
+                stocks[1][:, :, halves[h]].rearrange("p t (m i) -> p m t i", i=RUN),
+                ALU.mult,
+            )
+
+        z_w, z_s = {}, {}
+
+        def quantize_z(key, source, kib):
+            width = source.shape[1] // PACK
+            z_w[key] = placed([P, width], U32, "z_w" + "".join(str(i) for i in key), kib)
+            z_s[key] = placed([P, width], U8, "z_s" + "".join(str(i) for i in key), 66 + 0.5 * len(z_s))
+            nc.vector.quantize_mx(out=z_w[key][:].bitcast(FP8X4), scales=z_s[key][:], in_=source)
+
+        def second_product(into, key, nt, start, stop):
+            b = key[0]
+            nc.tensor.matmul_mx(
+                out=into,
+                lhsT=wc_w[:, b, span(nt, 2 * P)].bitcast(FP4X4),
+                lhsT_scale=wc_s[:, b, span(nt, P)],
+                rhs=z_w[key][:].bitcast(FP8X4),
+                rhs_scale=z_s[key][:],
+                start=start,
+                stop=stop,
+            )
+
+        staged = []
+
+        def leave(copy, source, rows):
+            staged.append(placed([P, BANK], F32, "staged%d" % len(staged), 76 + 2 * len(staged)))
+            copy(out=staged[-1][:], in_=source[:])
+            nc.sync.dma_start(out=rows, in_=staged[-1][:] if len(rows.shape) == 2 else by_half(staged[-1][:]))
+
+        def open_chunk(c):
             for nt in range(N // P):
-                second_product(0, c, nt)
+                second_product(banks[4 * (1 - c % 2) + nt][:], (0, c), nt, True, False)
+
+        def close_chunk(c):
             for nt in range(N // P):
-                second_product(1, c, nt)
-                store(c, nt)
+                second_product(banks[4 * (1 - c % 2) + nt][:], (1, c), nt, False, True)
+                leave(nc.scalar.copy, banks[4 * (1 - c % 2) + nt], out[span(nt, P), span(c)])
+
+        def half_product(b, h, g):
+            for i in range(2):
+                second_product(banks[4 + 2 * h + g][:, span(i, HALF)], (b, 0, h), 2 * g + i, (b, i) == (0, 0), (b, i) == (1, 1))
+
+        def leave_half(copy, h, g):
+            leave(copy, banks[4 + 2 * h + g], out[span(g, 2 * P), halves[h]].rearrange("(i p) m -> p i m", p=P))
+
+        for cols in halves:
+            thin_last(3, cols)
+        thin_last(2)
+        quantize_z((0, 3), zz[0, 3][:], 150)
+        open_chunk(3)
+        zz[1, 3] = placed([P, PACK * BANK], BF16, "zz13", 154)
+        for cols in halves:
+            deplete_pair(3, cols)
+            weave(nc.scalar.copy, U32, 3, cols)
+        thin_last(1)
+        thin_last(0)
+        deplete_pair(2)
+        quantize_z((1, 3), zz[1, 3][:], 12)
+        close_chunk(3)
+        zz[1, 2] = placed([P, PACK * BANK], BF16, "zz12", 144)
+        weave(nc.vector.tensor_copy, F32, 2)
+        quantize_z((0, 2), zz[0, 2][:], 154)
+        open_chunk(2)
+        quantize_z((1, 2), zz[1, 2][:], 14)
+        close_chunk(2)
+        deplete_pair(1)
+        quantize_z((0, 1), zz[0, 1][:], 144)
+        open_chunk(1)
+        zz[1, 1] = placed([P, PACK * BANK], BF16, "zz11", 196)
+        weave(nc.vector.tensor_copy, F32, 1)
+        quantize_z((0, 0, 0), zz[0, 0][:, times(halves[0], PACK)], 140)
+        quantize_z((1, 1), zz[1, 1][:], 0)
+        close_chunk(1)
+        for g in range(2):
+            half_product(0, 0, g)
+        deplete_whole(0, 8)
+        quantize_z((0, 0, 1), zz[0, 0][:, times(halves[1], PACK)], 196)
+        quantize_z((1, 0, 0), zz[1, 0, 0][:], 2)
+        for g in range(2):
+            half_product(1, 0, g)
+        for g in range(2):
+            half_product(0, 1, g)
+        deplete_whole(1, 10)
+        leave_half(nc.scalar.copy, 0, 0)
+        leave_half(nc.vector.tensor_copy, 0, 1)
+        quantize_z((1, 0, 1), zz[1, 0, 1][:], 3)
+        for g in range(2):
+            half_product(1, 1, g)
+        leave_half(nc.scalar.copy, 1, 0)
+        leave_half(nc.vector.tensor_copy, 1, 1)

@@ -1,3 +1,4 @@
+import math
 from contextlib import ExitStack
 
 import concourse.mybir as mybir
@@ -234,11 +235,6 @@ def tile_list_parts_depletion_kernel(tc, tab_words, tab_scales, offs, wf, wgs, o
         scatter(1, rates[1, 1], span(1))
         scatter(2, rates[2], whole_list)
 
-        third = [(k, n) for k in (4, 5) for n in range(2)]
-        for unit in third:
-            first_product([unit], (1, 0))
-            squash(*unit)
-
         def thin(k, into, cols):
             nc.scalar.activation(out=into, in_=pages[k % PAGES][:, cols], func=ACT.Exp, scale=-1.0)
 
@@ -253,88 +249,98 @@ def tile_list_parts_depletion_kernel(tc, tab_words, tab_scales, offs, wf, wgs, o
             lo = 2 * (first // 2)
             nc.gpsimd.tensor_tensor(planes[lo][:, first - lo : first - lo + count, t, :], by_chunk(left), by_chunk(stocks[0][:, t, cols]), ALU.mult)
 
-        kept0 = placed([P, T2], F32, "kept0", 58)
+        kept0 = placed([P, T2], F32, "kept0", 8)
         thin(0, kept0[:], page_wide)
 
-        lifted, decay, excess = [], [], []
-        for g in range(4):
-            for i in range(2):
-                n, q = divmod(2 * g + i, PACK)
-                for a in (1, 0):
-                    nc.tensor.matmul_mx(
-                        out=banks[4 + g][:, span(i, HALF)],
-                        lhsT=v_w[a, n][:, span(q, P)].bitcast(FP8X4),
-                        lhsT_scale=v_s[n][4 * a : P, span(q, P)],
-                        rhs=wf_w[a, 1, 2, 2].bitcast(FP8X4),
-                        rhs_scale=wf_s[a, 1, 2, 2],
-                        start=(a == 1),
-                        stop=(a == 0),
-                    )
-            lifted.append(placed([P, BANK], F32, "lifted%d" % g, 24 + 2 * g))
-            nc.scalar.activation(out=lifted[g][:], in_=banks[4 + g][:], func=ACT.Relu, bias=SHIFT)
-        for g in range(4):
-            decay.append(placed([P, BANK], F32, "decay%d" % g, 32 + 2 * g))
-            nc.scalar.activation(out=decay[g][:], in_=lifted[g][:], func=ACT.Exp, scale=-1.0, bias=SHIFT)
+        def turned_product(into, jt, t, count):
+            n, q = divmod(jt, PACK)
+            for a in (1, 0):
+                nc.tensor.matmul_mx(
+                    out=into,
+                    lhsT=v_w[a, n][:, span(q, P)].bitcast(FP8X4),
+                    lhsT_scale=v_s[n][4 * a : P, span(q, P)],
+                    rhs=(wf_w[a, 1, t] if count == 1 else wf_w[a, 1, t, count]).bitcast(FP8X4),
+                    rhs_scale=wf_s[a, 1, t] if count == 1 else wf_s[a, 1, t, count],
+                    start=(a == 1),
+                    stop=(a == 0),
+                )
 
+        lifted, decay, excess = {}, {}, {}
+
+        def lift(g):
+            lifted[g] = placed([P, BANK], F32, "lifted%d" % g, 16 + 2 * g)
+            nc.scalar.activation(out=lifted[g][:], in_=banks[g][:], func=ACT.Relu, bias=SHIFT)
+
+        for n in range(2):
+            for q in range(PACK):
+                turned_product(banks[n][:, span(q, P)], PACK * n + q, 0, 1)
+            lift(n)
+        for n in range(2):
+            first_product([(5, n)], (1, 0))
+            lift(2 + n)
         kept1 = placed([P, T2], F32, "kept1", 0)
-        thin(1, kept1[:], page_wide)
-        kept2a = placed([P, BANK], F32, "kept2a", 8)
-        thin(2, kept2a[:], span(3))
+        for g in range(4, 8):
+            for i in range(2):
+                turned_product(banks[g][:, span(i, HALF)], 2 * (g - 4) + i, 2, 2)
+            lift(g)
+        for g in range(8):
+            decay[g] = placed([P, BANK], F32, "decay%d" % g, 158 + 2 * g if g < 4 else 24 + 2 * g)
+            nc.scalar.activation(out=decay[g][:], in_=lifted[g][:], func=ACT.Exp, scale=-1.0, bias=SHIFT)
+            if g == 1:
+                thin(1, kept1[:], page_wide)
+        kept2f = placed([P, 2 * BANK], F32, "kept2f", 58)
+        thin(2, kept2f[:], front)
         scatter(3, rates[3], whole_list)
         for t, left in ((0, kept0), (1, kept1)):
             for cols in (front, back):
                 deplete(t, left[:, cols], cols)
-        deplete(2, kept2a[:], span(3))
+        deplete(2, kept2f[:], front)
+
+        for g in range(8):
+            excess[g] = placed([P, BANK], F32, "excess%d" % g, 40 + 2 * g if g < 4 else 180 + 2 * g)
+            lowered = math.e**-SHIFT if g in (2, 3) else 1.0
+            nc.scalar.activation(out=excess[g][:], in_=decay[g][:], func=ACT.Ln, scale=lowered, bias=lowered)
+
+        def turn_back(into, g, block):
+            for term in (lifted, excess):
+                nc.tensor.matmul(into, lhsT=term[g][:, span(block, P)], rhs=identity[:], is_transpose=True, start=(term is lifted), stop=(term is excess))
 
         rate_tile(4, (158, 160))
-        rate_tile(5, (162,))
-        for k, n in third:
-            logarithm(k, n)
-        for g in range(4):
-            excess.append(placed([P, BANK], F32, "excess%d" % g, 188 + 2 * g))
-            nc.scalar.activation(out=excess[g][:], in_=decay[g][:], func=ACT.Ln, bias=1.0)
-        for k, n in third:
-            finish(k, n)
         for n in range(2):
-            weighed = placed([P, BANK], F32, "weighed4%d" % n, 20 + 2 * n)
-            weigh(weighed[:], rates[4, n], span(n))
-            scatter(4, weighed[:], span(n))
+            for q in range(PACK):
+                turn_back(banks[n][:, span(q, P)], n, q)
+            nc.vector.scalar_tensor_tensor(out=rates[4, n], in0=banks[n][:], scalar=-SHIFT, in1=weights[:, span(n)], op0=ALU.add, op1=ALU.mult)
+        for n in range(2):
+            scatter(4, rates[4, n], span(n))
+        rate_tile(5, (162,))
+        for n in range(2):
+            nc.gpsimd.tensor_tensor(rates[5, n], lifted[2 + n][:], excess[2 + n][:], ALU.add)
         weigh(rates[5], rates[5], whole_list)
         for t in range(2):
             for jt in range(2 * PACK):
                 n, q = divmod(jt, PACK)
                 g, i = divmod(jt, 2)
-                for term in (lifted, excess):
-                    nc.tensor.matmul(
-                        banks[4 + 2 * t + n][:, span(q, P)],
-                        lhsT=term[g][:, span(2 * i + t, P)],
-                        rhs=identity[:],
-                        is_transpose=True,
-                        start=(term is lifted),
-                        stop=(term is excess),
-                    )
-
-        kept3f = placed([P, 2 * BANK], F32, "kept3f", 184)
-        thin(3, kept3f[:], front)
+                turn_back(banks[4 + 2 * t + n][:, span(q, P)], 4 + g, 2 * i + t)
 
         def lower(t, kib):
             rate_tile(6 + t, (kib,))
             for n in range(2):
                 nc.scalar.activation(out=rates[6 + t, n], in_=banks[4 + 2 * t + n][:], func=ACT.Copy, bias=-SHIFT)
 
+        kept3f = placed([P, 2 * BANK], F32, "kept3f", 184)
+        thin(3, kept3f[:], front)
         lower(0, 16)
-        kept2r = placed([P, 3 * BANK], F32, "kept2r", 10)
-        thin(2, kept2r[:], span(0, 3 * BANK))
-        kept3b = placed([P, 2 * BANK], F32, "kept3b", 40)
-        thin(3, kept3b[:], back)
+        kept2b = placed([P, 2 * BANK], F32, "kept2b", 62)
+        thin(2, kept2b[:], back)
         scatter(5, rates[5], whole_list)
         lower(1, 150)
+        kept3b = placed([P, 2 * BANK], F32, "kept3b", 40)
+        thin(3, kept3b[:], back)
         deplete(3, kept3f[:], front)
         weigh(rates[6], rates[6], whole_list)
-        deplete(2, kept2r[:, span(2)], span(2))
-        deplete(2, kept2r[:, back], back)
-        deplete(3, kept3b[:], back)
+        deplete(2, kept2b[:], back)
         weigh(rates[7], rates[7], whole_list)
+        deplete(3, kept3b[:], back)
         scatter(6, rates[6], whole_list)
 
         zz = {}
@@ -349,8 +355,8 @@ def tile_list_parts_depletion_kernel(tc, tab_words, tab_scales, offs, wf, wgs, o
         paired = span(1, BANK, 3)
         kept4 = placed([P, 3 * BANK], F32, "kept4", 0)
         thin(4, kept4[:], paired)
-        interleave(3, 58)
-        interleave(2, 62)
+        interleave(3, 8)
+        interleave(2, 12)
         kept5 = placed([P, 3 * BANK], F32, "kept5", 168)
         thin(5, kept5[:], paired)
         ending = placed([P, 10 * BANK], F32, "ending", 29)
@@ -367,8 +373,8 @@ def tile_list_parts_depletion_kernel(tc, tab_words, tab_scales, offs, wf, wgs, o
             return ap.rearrange("p (h m) -> p h m", h=2)
 
         descending = (3, 2, 1)
-        for c in descending:
-            for t, left in ((0, kept4), (1, kept5)):
+        for t, left in ((0, kept4), (1, kept5)):
+            for c in descending:
                 nc.gpsimd.tensor_tensor(late_planes(c)[:, t, :], left[:, span(c - 1)], stocks[1][:, t, span(c)], ALU.mult)
         for c in range(CHUNKS):
             thin(6, ending[:, span(2 + 2 * c)], span(c))
@@ -471,13 +477,13 @@ def tile_list_parts_depletion_kernel(tc, tab_words, tab_scales, offs, wf, wgs, o
         thin_last(1)
         thin_last(0)
         deplete_pair(2)
-        quantize_z((1, 3), zz[1, 3][:], 12)
+        quantize_z((1, 3), zz[1, 3][:], 58)
         close_chunk(3)
         zz[1, 2] = placed([P, PACK * BANK], BF16, "zz12", 144)
         weave(nc.vector.tensor_copy, F32, 2)
         quantize_z((0, 2), zz[0, 2][:], 154)
         open_chunk(2)
-        quantize_z((1, 2), zz[1, 2][:], 14)
+        quantize_z((1, 2), zz[1, 2][:], 60)
         close_chunk(2)
         deplete_pair(1)
         quantize_z((0, 1), zz[0, 1][:], 144)

@@ -365,9 +365,11 @@ def tile_list_parts_depletion_kernel(tc, tab_words, tab_scales, offs, wf, wgs, o
         scatter(7, rates[7], whole_list)
         interleave(1, 140)
 
+        ending_rows = ending[:].bitcast(BF16).rearrange("p (r x) -> p r x", x=2 * BANK)
+        late3 = placed([P, 2, BANK], BF16, "late3", 160)
+
         def late_planes(c):
-            rows = ending[:].bitcast(BF16).rearrange("p (r x) -> p r x", x=2 * BANK)
-            return rows[:, 5:8:2, span(0)] if c == 3 else rows[:, 3::6, span(c - 1)]
+            return late3[:] if c == 3 else ending_rows[:, 7::2, span(2 - c)]
 
         def by_half(ap):
             return ap.rearrange("p (h m) -> p h m", h=2)
@@ -378,12 +380,13 @@ def tile_list_parts_depletion_kernel(tc, tab_words, tab_scales, offs, wf, wgs, o
                 nc.gpsimd.tensor_tensor(late_planes(c)[:, t, :], left[:, span(c - 1)], stocks[1][:, t, span(c)], ALU.mult)
         for c in range(CHUNKS):
             thin(6, ending[:, span(2 + 2 * c)], span(c))
-        pairs = {}
-        for c, kib in zip(descending, (160, 164, 184)):
-            pairs[c] = placed([P, 2, 2 * BANK], BF16, "pairs%d" % c, kib)
+        pairs = {3: ending_rows[:, 3:6:2, :].rearrange("p h (u x) -> p h u x", u=2)}
+        for c, kib in ((2, 164), (1, 184)):
+            pairs[c] = placed([P, 2, 2, BANK], BF16, "pairs%d" % c, kib)[:]
+        for c in descending:
             nc.scalar.copy(
-                out=pairs[c][:, 0, :].rearrange("p (m i t) -> p m t i", i=RUN, t=2),
-                in_=late_planes(c).rearrange("p t (m i) -> p m t i", i=RUN),
+                out=pairs[c][:, :, 0, :].rearrange("p h (m i t) -> p h m t i", i=RUN, t=2),
+                in_=late_planes(c).rearrange("p t (h m i) -> p h m t i", h=2, i=RUN),
             )
         zz[0, 0] = placed([P, PACK * BANK], BF16, "zz00", 168)
         nc.gpsimd.tensor_scalar(zz[0, 0][:].rearrange("p (m t) -> p m t", t=PACK), planes[0][:, 0, :, :].rearrange("p t m -> p m t"), 1.0, 0.0, ALU.mult, ALU.add)
@@ -399,18 +402,19 @@ def tile_list_parts_depletion_kernel(tc, tab_words, tab_scales, offs, wf, wgs, o
         def thin_last(c, cols=every):
             thin(7, ending[:, within(3 + 2 * c, cols)], within(c, cols))
 
-        def deplete_pair(c, cols=every):
+        def deplete_pair(c, h):
+            cols = halves[h]
             nc.vector.tensor_tensor(
-                pairs[c][:, 1, times(cols, 2)].rearrange("p (m i t) -> p m t i", i=RUN, t=2),
+                pairs[c][:, h, 1, :].rearrange("p (m i t) -> p m t i", i=RUN, t=2),
                 by_chunk(ending[:, span(1 + c, 2 * BANK)])[:, :, cols].rearrange("p t (m i) -> p m t i", i=RUN),
                 stocks[1][:, 2:4, within(c, cols)].rearrange("p t (m i) -> p m t i", i=RUN),
                 ALU.mult,
             )
 
-        def weave(copy, word, c, cols=every):
+        def weave(copy, word, c, hs=slice(0, 2)):
             copy(
-                out=zz[1, c][:].bitcast(word)[:, times(cols, 2)].rearrange("p (m i u) -> p m u i", u=2, i=2),
-                in_=pairs[c][:].bitcast(word)[:, :, cols].rearrange("p u (m i) -> p m u i", i=2),
+                out=zz[1, c][:].bitcast(word).rearrange("p (h m i u) -> p h m u i", h=2, u=2, i=2)[:, hs],
+                in_=pairs[c].bitcast(word).rearrange("p h u (m i) -> p h m u i", i=2)[:, hs],
             )
 
         def deplete_whole(h, kib):
@@ -436,16 +440,16 @@ def tile_list_parts_depletion_kernel(tc, tab_words, tab_scales, offs, wf, wgs, o
                 out=into,
                 lhsT=wc_w[:, b, span(nt, 2 * P)].bitcast(FP4X4),
                 lhsT_scale=wc_s[:, b, span(nt, P)],
-                rhs=z_w[key][:].bitcast(FP8X4),
-                rhs_scale=z_s[key][:],
+                rhs=z_w[key][:, :].bitcast(FP8X4),
+                rhs_scale=z_s[key][:, :],
                 start=start,
                 stop=stop,
             )
 
         staged = []
 
-        def leave(copy, source, rows):
-            staged.append(placed([P, BANK], F32, "staged%d" % len(staged), 76 + 2 * len(staged)))
+        def leave(copy, source, rows, kib=None):
+            staged.append(placed([P, BANK], F32, "staged%d" % len(staged), 76 + 2 * len(staged) if kib is None else kib))
             copy(out=staged[-1][:], in_=source[:])
             nc.sync.dma_start(out=rows, in_=staged[-1][:] if len(rows.shape) == 2 else by_half(staged[-1][:]))
 
@@ -458,34 +462,49 @@ def tile_list_parts_depletion_kernel(tc, tab_words, tab_scales, offs, wf, wgs, o
                 second_product(banks[4 * (1 - c % 2) + nt][:], (1, c), nt, False, True)
                 leave(nc.scalar.copy, banks[4 * (1 - c % 2) + nt], out[span(nt, P), span(c)])
 
-        def half_product(b, h, g):
-            for i in range(2):
-                second_product(banks[4 + 2 * h + g][:, span(i, HALF)], (b, 0, h), 2 * g + i, (b, i) == (0, 0), (b, i) == (1, 1))
+        def half_bank(c, h, g):
+            return banks[4 * (1 - c % 2) + 2 * h + g]
 
-        def leave_half(copy, h, g):
-            leave(copy, banks[4 + 2 * h + g], out[span(g, 2 * P), halves[h]].rearrange("(i p) m -> p i m", p=P))
+        def half_product(b, c, h, g, first=0):
+            for i in range(2):
+                second_product(half_bank(c, h, g)[:, span(i, HALF)], (b, c, h), 2 * g + i, (b, i) == (first, 0), (b, i) == (1 - first, 1))
+
+        def leave_half(copy, c, h, g, kib=None):
+            leave(copy, half_bank(c, h, g), out[span(g, 2 * P), within(c, halves[h])].rearrange("(i p) m -> p i m", p=P), kib)
 
         for cols in halves:
             thin_last(3, cols)
         thin_last(2)
         quantize_z((0, 3), zz[0, 3][:], 150)
-        open_chunk(3)
+        for h in range(2):
+            z_w[0, 3, h], z_s[0, 3, h] = z_w[0, 3][:, halves[h]], z_s[0, 3][:, halves[h]]
+        for g in range(2):
+            half_product(0, 3, 0, g)
         zz[1, 3] = placed([P, PACK * BANK], BF16, "zz13", 154)
-        for cols in halves:
-            deplete_pair(3, cols)
-            weave(nc.scalar.copy, U32, 3, cols)
+        for h in range(2):
+            deplete_pair(3, h)
+            weave(nc.scalar.copy, U32, 3, span(h, 1))
         thin_last(1)
+        deplete_pair(2, 0)
+        quantize_z((1, 3, 0), zz[1, 3][:, times(halves[0], PACK)], 58)
+        for g in range(2):
+            half_product(1, 3, 0, g)
+            leave_half(nc.scalar.copy, 3, 0, g)
         thin_last(0)
-        deplete_pair(2)
-        quantize_z((1, 3), zz[1, 3][:], 58)
-        close_chunk(3)
+        deplete_pair(2, 1)
+        quantize_z((1, 3, 1), zz[1, 3][:, times(halves[1], PACK)], 59)
+        for g in range(2):
+            for b in (1, 0):
+                half_product(b, 3, 1, g, first=1)
+            leave_half(nc.scalar.copy, 3, 1, g)
         zz[1, 2] = placed([P, PACK * BANK], BF16, "zz12", 144)
         weave(nc.vector.tensor_copy, F32, 2)
         quantize_z((0, 2), zz[0, 2][:], 154)
         open_chunk(2)
         quantize_z((1, 2), zz[1, 2][:], 60)
         close_chunk(2)
-        deplete_pair(1)
+        for h in range(2):
+            deplete_pair(1, h)
         quantize_z((0, 1), zz[0, 1][:], 144)
         open_chunk(1)
         zz[1, 1] = placed([P, PACK * BANK], BF16, "zz11", 196)
@@ -494,19 +513,19 @@ def tile_list_parts_depletion_kernel(tc, tab_words, tab_scales, offs, wf, wgs, o
         quantize_z((1, 1), zz[1, 1][:], 0)
         close_chunk(1)
         for g in range(2):
-            half_product(0, 0, g)
+            half_product(0, 0, 0, g)
         deplete_whole(0, 8)
         quantize_z((0, 0, 1), zz[0, 0][:, times(halves[1], PACK)], 196)
         quantize_z((1, 0, 0), zz[1, 0, 0][:], 2)
         for g in range(2):
-            half_product(1, 0, g)
+            half_product(1, 0, 0, g)
         for g in range(2):
-            half_product(0, 1, g)
+            half_product(0, 0, 1, g)
         deplete_whole(1, 10)
-        leave_half(nc.scalar.copy, 0, 0)
-        leave_half(nc.vector.tensor_copy, 0, 1)
+        leave_half(nc.scalar.copy, 0, 0, 0)
         quantize_z((1, 0, 1), zz[1, 0, 1][:], 3)
+        leave_half(nc.vector.tensor_copy, 0, 0, 1, 10)
         for g in range(2):
-            half_product(1, 1, g)
-        leave_half(nc.scalar.copy, 1, 0)
-        leave_half(nc.vector.tensor_copy, 1, 1)
+            half_product(1, 0, 1, g)
+        leave_half(nc.scalar.copy, 0, 1, 0)
+        leave_half(nc.vector.tensor_copy, 0, 1, 1)

@@ -159,9 +159,10 @@ def tile_list_parts_depletion_kernel(tc, tab_words, tab_scales, offs, wf, wgs, o
         survival, rates = {}, {}
         every = slice(0, BANK)
 
-        def squash(k, n):
-            survival[k, n] = placed([P, BANK], F32, "survival%d%d" % (k, n), 4 * k + 2 * n)
-            nc.scalar.activation(out=survival[k, n][:], in_=bank(k, n)[:], func=ACT.Sigmoid, scale=-1.0)
+        def squash(k, n, cols=every):
+            if (k, n) not in survival:
+                survival[k, n] = placed([P, BANK], F32, "survival%d%d" % (k, n), 4 * k + 2 * n)
+            nc.scalar.activation(out=survival[k, n][:, cols], in_=bank(k, n)[:, cols], func=ACT.Sigmoid, scale=-1.0)
 
         def rate_tile(k, kibs):
             if len(kibs) == 2:
@@ -186,19 +187,25 @@ def tile_list_parts_depletion_kernel(tc, tab_words, tab_scales, offs, wf, wgs, o
         whole_list = slice(0, S)
         opening = [(0, 0), (0, 1)]
         first_product(opening, (0, 1))
+        first_product([(1, 0)], (0, 1))
+        pieces = [slice(0, P), slice(P, BANK)]
         for k, n in opening:
             squash(k, n)
+        squash(1, 0, pieces[0])
         rate_tile(0, (140, 144))
-        pieces = [slice(0, P), slice(P, BANK)]
+        rate_tile(1, (146, 148))
         for cols in pieces:
             logarithm(0, 0, cols)
         logarithm(0, 1)
+        logarithm(1, 0, pieces[0])
         for cols in pieces:
             finish(0, 0, cols)
             weigh(rates[0, 0][:, cols], rates[0, 0][:, cols], cols)
         finish(0, 1)
         weighed01 = placed([P, BANK], F32, "weighed01", 166)
         weigh(weighed01[:], rates[0, 1], span(1))
+        finish(1, 0, pieces[0])
+        weigh(rates[1, 0][:, pieces[0]], rates[1, 0][:, pieces[0]], pieces[0])
         for cols in pieces:
             scatter(0, rates[0, 0][:, cols], cols)
         scatter(0, weighed01[:], span(1))
@@ -214,18 +221,19 @@ def tile_list_parts_depletion_kernel(tc, tab_words, tab_scales, offs, wf, wgs, o
         quantize_wf(1, 1, 0, 2, 0, 70, 73.75)
         quantize_wf(1, 1, 2, 2, 0, 72, 74.25)
 
+        scatter(1, rates[1, 0][:, pieces[0]], pieces[0])
+
         second = [(k, n) for k in (1, 2, 3) for n in range(2)]
-        for unit in second:
+        for unit in second[1:]:
             first_product([unit], (0, 1) if unit[0] == 1 else (1, 0))
         for k, n in second:
-            squash(k, n)
-        rate_tile(1, (146, 148))
+            squash(k, n, pieces[1] if (k, n) == (1, 0) else every)
         rate_tile(2, (150,))
         rate_tile(3, (154,))
         for k, n in second:
-            logarithm(k, n)
-        finish(1, 0)
-        nc.vector.tensor_tensor(pages[1][:].indirect(bins[:, entries(span(0))]), rates[1, 0], weights[:, span(0)], ALU.mult)
+            logarithm(k, n, pieces[1] if (k, n) == (1, 0) else every)
+        finish(1, 0, pieces[1])
+        nc.vector.tensor_tensor(pages[1][:].indirect(bins[:, entries(pieces[1])]), rates[1, 0][:, pieces[1]], weights[:, pieces[1]], ALU.mult)
         finish(1, 1)
         weigh(rates[1, 1], rates[1, 1], span(1))
         for k in (2, 3):

@@ -56,7 +56,7 @@ def tile_list_parts_depletion_kernel(tc, tab_words, tab_scales, offs, wf, wgs, o
         tab_s = held([P, T], U8, "tab_s")
         v_w = {(a, n): held([P, BANK], U32, "v_w%d%d" % (a, n)) for a in range(PASSES) for n in range(2)}
         v_s = [held([P, BANK], U8, "v_s%d" % n) for n in range(2)]
-        pages = [held([P, T2], F32, "page%d" % i) for i in range(2)]
+        pages = [held([P, T2], F32, "page0")]
         wc_w = held([P, PASSES, 2 * N], U8, "wc_w")
         wc_s = held([P, PASSES, N], U8, "wc_s")
         weights = held([P, S], F32, "weights")
@@ -64,12 +64,11 @@ def tile_list_parts_depletion_kernel(tc, tab_words, tab_scales, offs, wf, wgs, o
         banks = [psum.tile([P, BANK], F32, name="bank%d" % i) for i in range(8)]
 
         nc.vector.memset(tab_s[:].bitcast(I32), 0)
-        for page in pages:
-            nc.vector.memset(page[:].bitcast(I32), 0)
+        nc.vector.memset(pages[0][:].bitcast(I32), 0)
         nc.vector.memset(wc_s[:].rearrange("p a n -> p (a n)").bitcast(I32), 0)
         nc.scalar.activation(out=floor[:], in_=pages[0][:, 0:1], func=ACT.Sigmoid, bias=-CAP)
 
-        landing = placed([P, T // 4], I32, "landing", 200)
+        landing = placed([P, T // 4], I32, "landing", 204)
         tab_w = [placed([P, T], I32, "tab_w%d" % a, 8 * a) for a in range(PASSES)]
         raws = {(a, b): placed([P, PACK, KP], F32, "raw%d%d" % (a, b), 16 + 8 * a + 16 * b) for a in range(PASSES) for b in range(PASSES)}
         stocks = [placed([P, PACK, T2], F32, "stock%d" % b, 76 + 32 * b) for b in range(PASSES)]
@@ -78,8 +77,11 @@ def tile_list_parts_depletion_kernel(tc, tab_words, tab_scales, offs, wf, wgs, o
             nc.sync.dma_start(out=raws[a, b][:], in_=wf[span(a, KP), span(b, KP)].rearrange("(p j) c -> p j c", j=PACK))
 
         nc.sync.dma_start(parts[:], offs)
-        for q in range(4):
+        for q in range(2):
             nc.sync.dma_start(out=landing[32 * q : 32 * q + 4 * PASSES, :], in_=tab_scales[:, 4 * q : 4 * q + 4, :].bitcast(I32))
+        for q in range(2, 4):
+            for a in range(PASSES):
+                nc.sync.dma_start(out=landing[32 * q + 4 * a : 32 * q + 4 * a + 4, :], in_=tab_scales[a, 4 * q : 4 * q + 4, :].bitcast(I32))
         for a in range(PASSES):
             nc.sync.dma_start(out=tab_w[a][:], in_=tab_words[a].rearrange("p t i -> p (t i)").bitcast(I32))
             load_wf(a, 0)
@@ -97,7 +99,10 @@ def tile_list_parts_depletion_kernel(tc, tab_words, tab_scales, offs, wf, wgs, o
         for q in range(4):
             rows = slice(32 * q, 32 * q + 4 * PASSES)
             nc.vector.tensor_copy(out=tab_s[rows, :].bitcast(I32), in_=landing[rows, :])
-        identity = placed([P, P], F32, "identity", 200)
+        for kib in (197, 205):
+            pages.append(placed([P, T2], F32, "page%d" % len(pages), kib))
+            nc.gpsimd.memset(pages[-1][:].bitcast(I32), 0)
+        identity = placed([P, P], F32, "identity", 49)
         make_identity(nc, identity[:])
 
         def gather_words(a):
@@ -123,18 +128,16 @@ def tile_list_parts_depletion_kernel(tc, tab_words, tab_scales, offs, wf, wgs, o
         for n in range(2):
             nc.vector.tensor_copy(v_s[n][:], tab_s[:].indirect(parts[:, entries(span(n))]))
         gather_words(0)
-        round_wf(nc.scalar.copy, 0, 0, 0, 2, 50)
-        round_wf(nc.scalar.copy, 0, 0, 2, 4, 52)
+        round_wf(nc.scalar.copy, 0, 0, 0, 2, 168)
+        round_wf(nc.scalar.copy, 0, 0, 2, 4, 170)
         quantize_wf(0, 0, 0, 2, 0, 66, 73)
         gather_words(1)
-        round_wf(nc.vector.tensor_copy, 1, 0, 0, 2, 54)
+        round_wf(nc.vector.tensor_copy, 1, 0, 0, 2, 172)
         quantize_wf(1, 0, 0, 1, 0, 67, 140)
         quantize_wf(1, 0, 1, 1, 0, 67.5, 73.25)
-        round_wf(nc.scalar.copy, 1, 0, 2, 4, 56)
+        round_wf(nc.scalar.copy, 1, 0, 2, 4, 174)
         quantize_wf(0, 0, 2, 2, 2, 24, 146)
         quantize_wf(1, 0, 2, 2, 2, 68, 73.5)
-        pages.append(placed([P, T2], F32, "page2", 50))
-        nc.vector.memset(pages[2][:].bitcast(I32), 0)
         round_wf(nc.vector.tensor_copy, 0, 1, 0, PACK, 58)
         quantize_wf(0, 1, 0, 2, 0, 69, 62)
         quantize_wf(0, 1, 2, 2, 0, 71, 74)
@@ -515,7 +518,7 @@ def tile_list_parts_depletion_kernel(tc, tab_words, tab_scales, offs, wf, wgs, o
             deplete_pair(1, h)
         quantize_z((0, 1), zz[0, 1][:], 144)
         open_chunk(1)
-        zz[1, 1] = placed([P, PACK * BANK], BF16, "zz11", 196)
+        zz[1, 1] = placed([P, PACK * BANK], BF16, "zz11", 50)
         weave(nc.vector.tensor_copy, F32, 1)
         quantize_z((0, 0, 0), zz[0, 0][:, times(halves[0], PACK)], 140)
         quantize_z((1, 1), zz[1, 1][:], 0)
@@ -523,7 +526,7 @@ def tile_list_parts_depletion_kernel(tc, tab_words, tab_scales, offs, wf, wgs, o
         for g in range(2):
             half_product(0, 0, 0, g)
         deplete_whole(0, 8)
-        quantize_z((0, 0, 1), zz[0, 0][:, times(halves[1], PACK)], 196)
+        quantize_z((0, 0, 1), zz[0, 0][:, times(halves[1], PACK)], 50)
         quantize_z((1, 0, 0), zz[1, 0, 0][:], 2)
         for g in range(2):
             half_product(1, 0, 0, g)

@@ -278,9 +278,11 @@ def tile_list_parts_depletion_kernel(tc, tab_words, tab_scales, offs, wf, wgs, o
 
         lifted, decay, excess = {}, {}, {}
 
+        lifted5 = placed([P, S], F32, "lifted_tile5", 20)
+
         def lift(g):
-            lifted[g] = placed([P, BANK], F32, "lifted%d" % g, 16 + 2 * g)
-            nc.scalar.activation(out=lifted[g][:], in_=banks[g][:], func=ACT.Relu, bias=SHIFT)
+            lifted[g] = lifted5[:, span(g - 2)] if g in (2, 3) else placed([P, BANK], F32, "lifted%d" % g, 16 + 2 * g)[:]
+            nc.scalar.activation(out=lifted[g], in_=banks[g][:], func=ACT.Relu, bias=SHIFT)
 
         for n in range(2):
             for q in range(PACK):
@@ -296,7 +298,7 @@ def tile_list_parts_depletion_kernel(tc, tab_words, tab_scales, offs, wf, wgs, o
             lift(g)
         for g in range(8):
             decay[g] = placed([P, BANK], F32, "decay%d" % g, 158 + 2 * g if g < 4 else 24 + 2 * g)
-            nc.scalar.activation(out=decay[g][:], in_=lifted[g][:], func=ACT.Exp, scale=-1.0, bias=SHIFT)
+            nc.scalar.activation(out=decay[g][:], in_=lifted[g], func=ACT.Exp, scale=-1.0, bias=SHIFT)
             if g == 1:
                 thin(1, kept1[:], page_wide)
         kept2f = placed([P, 2 * BANK], F32, "kept2f", 58)
@@ -307,10 +309,11 @@ def tile_list_parts_depletion_kernel(tc, tab_words, tab_scales, offs, wf, wgs, o
                 deplete(t, left[:, cols], cols)
         deplete(2, kept2f[:], front)
 
+        excess5 = placed([P, S], F32, "excess_tile5", 44)
         for g in range(8):
-            excess[g] = placed([P, BANK], F32, "excess%d" % g, 40 + 2 * g if g < 4 else 180 + 2 * g)
+            excess[g] = excess5[:, span(g - 2)] if g in (2, 3) else placed([P, BANK], F32, "excess%d" % g, 40 + 2 * g if g < 4 else 180 + 2 * g)[:]
             lowered = math.e**-SHIFT if g in (2, 3) else 1.0
-            nc.scalar.activation(out=excess[g][:], in_=decay[g][:], func=ACT.Ln, scale=lowered, bias=lowered)
+            nc.scalar.activation(out=excess[g], in_=decay[g][:], func=ACT.Ln, scale=lowered, bias=lowered)
 
         def turn_back(into, g, block):
             for term in (lifted, excess):
@@ -324,8 +327,7 @@ def tile_list_parts_depletion_kernel(tc, tab_words, tab_scales, offs, wf, wgs, o
         for n in range(2):
             scatter(4, rates[4, n], span(n))
         rate_tile(5, (162,))
-        for n in range(2):
-            nc.gpsimd.tensor_tensor(rates[5, n], lifted[2 + n][:], excess[2 + n][:], ALU.add)
+        nc.gpsimd.tensor_tensor(rates[5], lifted5[:], excess5[:], ALU.add)
         weigh(rates[5], rates[5], whole_list)
         for t in range(2):
             for jt in range(2 * PACK):
@@ -350,8 +352,8 @@ def tile_list_parts_depletion_kernel(tc, tab_words, tab_scales, offs, wf, wgs, o
         deplete(3, kept3f[:], front)
         weigh(rates[6], rates[6], whole_list)
         deplete(2, kept2b[:], back)
-        weigh(rates[7], rates[7], whole_list)
         deplete(3, kept3b[:], back)
+        weigh(rates[7], rates[7], whole_list)
         scatter(6, rates[6], whole_list)
 
         zz = {}
@@ -365,8 +367,8 @@ def tile_list_parts_depletion_kernel(tc, tab_words, tab_scales, offs, wf, wgs, o
 
         paired = span(1, BANK, 3)
         kept4 = placed([P, 3 * BANK], F32, "kept4", 0)
-        thin(4, kept4[:], paired)
         interleave(3, 8)
+        thin(4, kept4[:], paired)
         interleave(2, 12)
         kept5 = placed([P, 3 * BANK], F32, "kept5", 168)
         thin(5, kept5[:], paired)

@@ -343,16 +343,19 @@ def tile_list_parts_depletion_kernel(tc, tab_words, tab_scales, offs, wf, wgs, o
         kept3f = placed([P, 2 * BANK], F32, "kept3f", 184)
         thin(3, kept3f[:], front)
         lower(0, 16)
-        kept2b = placed([P, 2 * BANK], F32, "kept2b", 62)
-        thin(2, kept2b[:], back)
+        kept_back = placed([P, 2, 2 * BANK], F32, "kept_back", 40)
+        thin(2, kept_back[:, 0, :], back)
         scatter(5, rates[5], whole_list)
         lower(1, 150)
-        kept3b = placed([P, 2 * BANK], F32, "kept3b", 40)
-        thin(3, kept3b[:], back)
+        thin(3, kept_back[:, 1, :], back)
         deplete(3, kept3f[:], front)
         weigh(rates[6], rates[6], whole_list)
-        deplete(2, kept2b[:], back)
-        deplete(3, kept3b[:], back)
+        nc.gpsimd.tensor_tensor(
+            planes[0][:, :, 2:4, :].rearrange("p c t m -> p t c m"),
+            kept_back[:].rearrange("p t (c m) -> p t c m", m=BANK),
+            stocks[0][:, 2:4, back].rearrange("p t (c m) -> p t c m", m=BANK),
+            ALU.mult,
+        )
         weigh(rates[7], rates[7], whole_list)
         scatter(6, rates[6], whole_list)
 
@@ -372,31 +375,32 @@ def tile_list_parts_depletion_kernel(tc, tab_words, tab_scales, offs, wf, wgs, o
         interleave(2, 12)
         kept5 = placed([P, 3 * BANK], F32, "kept5", 168)
         thin(5, kept5[:], paired)
-        ending = placed([P, 10 * BANK], F32, "ending", 29)
+        ending_tile = placed([P, 12 * BANK], F32, "ending", 25)
+        ending = ending_tile[:, 2 * BANK :]
         for t in range(2):
             thin(4 + t, ending[:, span(t)], span(0))
         scatter(7, rates[7], whole_list)
         interleave(1, 140)
 
-        ending_rows = ending[:].bitcast(BF16).rearrange("p (r x) -> p r x", x=2 * BANK)
-        late3 = placed([P, 2, BANK], BF16, "late3", 160)
+        ending_rows = ending.bitcast(BF16).rearrange("p (r x) -> p r x", x=2 * BANK)
+        late_rows = ending_tile[:].bitcast(BF16).rearrange("p (r x) -> p r x", x=BANK)
+        second_row = {3: 18, 1: 22, 2: 23}
 
         def late_planes(c):
-            return late3[:] if c == 3 else ending_rows[:, 7::2, span(2 - c)]
+            return late_rows[:, c - 1 : second_row[c] + 1 : second_row[c] - c + 1, :]
 
         def by_half(ap):
             return ap.rearrange("p (h m) -> p h m", h=2)
 
-        descending = (3, 2, 1)
-        for t, left in ((0, kept4), (1, kept5)):
-            for c in descending:
-                nc.gpsimd.tensor_tensor(late_planes(c)[:, t, :], left[:, span(c - 1)], stocks[1][:, t, span(c)], ALU.mult)
+        nc.gpsimd.tensor_tensor(ending_tile[:].bitcast(BF16)[:, span(0, 3 * BANK)], kept4[:], stocks[1][:, 0, paired], ALU.mult)
+        nc.gpsimd.tensor_tensor(late_planes(3)[:, 1, :], kept5[:, span(2)], stocks[1][:, 1, span(3)], ALU.mult)
+        nc.gpsimd.tensor_tensor(ending_rows[:, 9, :], kept5[:, span(0, BANK, 2)], stocks[1][:, 1, span(1, BANK, 2)], ALU.mult)
         for c in range(CHUNKS):
             thin(6, ending[:, span(2 + 2 * c)], span(c))
         pairs = {3: ending_rows[:, 3:6:2, :].rearrange("p h (u x) -> p h u x", u=2)}
         for c, kib in ((2, 164), (1, 184)):
             pairs[c] = placed([P, 2, 2, BANK], BF16, "pairs%d" % c, kib)[:]
-        for c in descending:
+        for c in (3, 1, 2):
             nc.scalar.copy(
                 out=pairs[c][:, :, 0, :].rearrange("p h (m i t) -> p h m t i", i=RUN, t=2),
                 in_=late_planes(c).rearrange("p t (h m i) -> p h m t i", h=2, i=RUN),

@@ -27,7 +27,7 @@ PASSES = K // KP
 CHUNKS = T2 // BANK
 PAGES = 3
 CAP = 43.5
-SHIFT = 16.0
+SHIFT = 24.0
 KIB = 1024
 RUN = 4
 

@@ -1,4 +1,3 @@
-import math
 from contextlib import ExitStack
 
 import concourse.mybir as mybir
@@ -25,11 +24,12 @@ BANK = 512
 HALF = BANK // 2
 PASSES = K // KP
 CHUNKS = T2 // BANK
-PAGES = 3
+PAGES = 4
 CAP = 43.5
 SHIFT = 24.0
 KIB = 1024
 RUN = 4
+EARLY = 256
 
 
 def tile_list_parts_depletion_kernel(tc, tab_words, tab_scales, offs, wf, wgs, offs2, stock, wc_words, wc_scales, out):
@@ -54,27 +54,32 @@ def tile_list_parts_depletion_kernel(tc, tab_words, tab_scales, offs, wf, wgs, o
         parts = keep.tile([P, S // 16], U16, name="parts")
         bins = keep.tile([P, S // 16], U16, name="bins")
         tab_s = held([P, T], U8, "tab_s")
-        v_w = {(a, n): held([P, BANK], U32, "v_w%d%d" % (a, n)) for a in range(PASSES) for n in range(2)}
+        v_w = {(a, n): placed([P, BANK], U32, "v_w%d%d" % (a, n), 162 + 8 * n + 4 * a) for a in range(PASSES) for n in range(2)}
         v_s = [held([P, BANK], U8, "v_s%d" % n) for n in range(2)]
         pages = [held([P, T2], F32, "page0")]
         wc_w = held([P, PASSES, 2 * N], U8, "wc_w")
         wc_s = held([P, PASSES, N], U8, "wc_s")
         weights = held([P, S], F32, "weights")
         floor = held([P, 1], F32, "floor")
+        identity = held([P, P], F32, "identity")
         banks = [psum.tile([P, BANK], F32, name="bank%d" % i) for i in range(8)]
 
         nc.vector.memset(tab_s[:].bitcast(I32), 0)
         nc.vector.memset(pages[0][:].bitcast(I32), 0)
         nc.vector.memset(wc_s[:].rearrange("p a n -> p (a n)").bitcast(I32), 0)
         nc.scalar.activation(out=floor[:], in_=pages[0][:, 0:1], func=ACT.Sigmoid, bias=-CAP)
+        make_identity(nc, identity[:])
 
-        landing = placed([P, T // 4], I32, "landing", 204)
+        landing = placed([P, T // 4], I32, "landing", 145)
         tab_w = [placed([P, T], I32, "tab_w%d" % a, 8 * a) for a in range(PASSES)]
         raws = {(a, b): placed([P, PACK, KP], F32, "raw%d%d" % (a, b), 16 + 8 * a + 16 * b) for a in range(PASSES) for b in range(PASSES)}
-        stocks = [placed([P, PACK, T2], F32, "stock%d" % b, 76 + 32 * b) for b in range(PASSES)]
+        stocks = [placed([P, PACK, T2], F32, "stock%d" % b, 74 + 32 * b) for b in range(PASSES)]
 
         def load_wf(a, b):
             nc.sync.dma_start(out=raws[a, b][:], in_=wf[span(a, KP), span(b, KP)].rearrange("(p j) c -> p j c", j=PACK))
+
+        def load_stock(b, rows):
+            nc.sync.dma_start(out=stocks[b][:, rows, :], in_=stock[span(b, KP), :].rearrange("(p t) m -> p t m", t=PACK)[:, rows, :])
 
         nc.sync.dma_start(parts[:], offs)
         for q in range(2):
@@ -86,24 +91,22 @@ def tile_list_parts_depletion_kernel(tc, tab_words, tab_scales, offs, wf, wgs, o
             nc.sync.dma_start(out=tab_w[a][:], in_=tab_words[a].rearrange("p t i -> p (t i)").bitcast(I32))
             load_wf(a, 0)
         nc.sync.dma_start(bins[:], offs2)
-        load_wf(0, 1)
+        for a in range(PASSES):
+            load_wf(a, 1)
         nc.sync.dma_start(out=weights[:], in_=wgs)
-        load_wf(1, 1)
+        for b in range(PASSES):
+            for u in range(2):
+                load_stock(b, span(u, 2))
         nc.sync.dma_start(out=wc_w[:].bitcast(I32), in_=wc_words.rearrange("a p n -> p a n").bitcast(I32))
         for q in range(4):
             nc.sync.dma_start(out=wc_s[32 * q : 32 * q + 4, :, :].bitcast(I32), in_=wc_scales[:, 4 * q : 4 * q + 4, :].rearrange("a r n -> r a n").bitcast(I32))
-        for b in range(PASSES):
-            for u in range(2):
-                nc.sync.dma_start(out=stocks[b][:, span(u, 2), :], in_=stock[span(b, KP), :].rearrange("(p t) m -> p t m", t=PACK)[:, span(u, 2), :])
 
         for q in range(4):
             rows = slice(32 * q, 32 * q + 4 * PASSES)
             nc.vector.tensor_copy(out=tab_s[rows, :].bitcast(I32), in_=landing[rows, :])
-        for kib in (197, 205):
+        for kib in (138, 146):
             pages.append(placed([P, T2], F32, "page%d" % len(pages), kib))
             nc.gpsimd.memset(pages[-1][:].bitcast(I32), 0)
-        identity = placed([P, P], F32, "identity", 49)
-        make_identity(nc, identity[:])
 
         def gather_words(a):
             for n in range(2):
@@ -111,140 +114,84 @@ def tile_list_parts_depletion_kernel(tc, tab_words, tab_scales, offs, wf, wgs, o
 
         grouped, wf_w, wf_s = {}, {}, {}
 
-        def round_wf(copy, a, b, lo, hi, kib):
-            whole = placed([P, (hi - lo) * KP], BF16, "grouped%d%d%d" % (a, b, lo), kib)
+        def round_wf(copy, a, b, lo, hi):
+            whole = placed([P, (hi - lo) * KP], BF16, "grouped%d%d%d" % (a, b, lo), 48 + 4 * a + 8 * b + lo)
             src = raws[a, b][:].rearrange("p j (m t) -> p m j t", t=PACK)
             copy(out=whole[:].rearrange("p (t m j) -> p m j t", t=hi - lo, j=PACK), in_=src[:, :, :, lo:hi])
             grouped[a, b, lo] = whole
 
-        def quantize_wf(a, b, t, count, source, codes_kib, scales_kib):
-            codes = placed([P, count * P], U32, "wf_w%d%d%d" % (a, b, t), codes_kib)
-            scales = placed([P, count * P], U8, "wf_s%d%d%d" % (a, b, t), scales_kib)
+        def quantize_wf(a, b, t, count, source):
+            place = 2 * a + 4 * b + t / 2
+            codes = placed([P, count * P], U32, "wf_w%d%d%d" % (a, b, t), 64 + place)
+            scales = placed([P, count * P], U8, "wf_s%d%d%d" % (a, b, t), 72 + place / 4)
             nc.vector.quantize_mx(out=codes[:].bitcast(FP8X4), scales=scales[:], in_=grouped[a, b, source][:, span(t - source, KP, count)])
             for i in range(count):
                 wf_w[a, b, t + i], wf_s[a, b, t + i] = codes[:, span(i, P)], scales[:, span(i, P)]
-            wf_w[a, b, t, count], wf_s[a, b, t, count] = codes[:], scales[:]
+            wf_w[a, b], wf_s[a, b] = codes[:], scales[:]
 
         for n in range(2):
             nc.vector.tensor_copy(v_s[n][:], tab_s[:].indirect(parts[:, entries(span(n))]))
         gather_words(0)
-        round_wf(nc.scalar.copy, 0, 0, 0, 2, 168)
-        round_wf(nc.scalar.copy, 0, 0, 2, 4, 170)
-        quantize_wf(0, 0, 0, 2, 0, 66, 73)
+        round_wf(nc.scalar.copy, 0, 0, 0, 2)
+        round_wf(nc.scalar.copy, 0, 0, 2, 4)
+        quantize_wf(0, 0, 0, 2, 0)
         gather_words(1)
-        round_wf(nc.vector.tensor_copy, 1, 0, 0, 2, 172)
-        quantize_wf(1, 0, 0, 1, 0, 67, 140)
-        quantize_wf(1, 0, 1, 1, 0, 67.5, 73.25)
-        round_wf(nc.scalar.copy, 1, 0, 2, 4, 174)
-        quantize_wf(0, 0, 2, 2, 2, 24, 146)
-        quantize_wf(1, 0, 2, 2, 2, 68, 73.5)
-        round_wf(nc.vector.tensor_copy, 0, 1, 0, PACK, 58)
-        quantize_wf(0, 1, 0, 2, 0, 69, 62)
-        quantize_wf(0, 1, 2, 2, 0, 71, 74)
+        quantize_wf(0, 0, 2, 2, 2)
+        round_wf(nc.vector.tensor_copy, 1, 0, 0, 2)
+        round_wf(nc.scalar.copy, 1, 0, 2, 4)
+        quantize_wf(1, 0, 0, 1, 0)
+        quantize_wf(1, 0, 1, 1, 0)
+        quantize_wf(1, 0, 2, 2, 2)
+        for a in range(PASSES):
+            round_wf(nc.vector.tensor_copy, a, 1, 0, PACK)
+            quantize_wf(a, 1, 0, PACK, 0)
 
-        def bank(k, n):
-            return banks[(2 * k + n) % 8]
+        first = [(k, span(n)) for k in range(3) for n in range(2)] + [(3, span(0, EARLY))]
+        for a in range(PASSES):
+            for g, (k, cols) in enumerate(first):
+                n, width = cols.start // BANK, cols.stop - cols.start
+                nc.tensor.matmul_mx(
+                    out=banks[g][:, :width],
+                    lhsT=wf_w[a, 0, k].bitcast(FP8X4),
+                    lhsT_scale=wf_s[a, 0, k],
+                    rhs=v_w[a, n][:, :width].bitcast(FP8X4),
+                    rhs_scale=v_s[n][4 * a : P, :width],
+                    start=(a == 0),
+                    stop=(a == PASSES - 1),
+                )
 
-        def first_product(units, order):
-            for a in order:
-                for k, n in units:
-                    b, t = divmod(k, PACK)
-                    nc.tensor.matmul_mx(
-                        out=bank(k, n)[:],
-                        lhsT=wf_w[a, b, t].bitcast(FP8X4),
-                        lhsT_scale=wf_s[a, b, t],
-                        rhs=v_w[a, n][:].bitcast(FP8X4),
-                        rhs_scale=v_s[n][4 * a : P, :],
-                        start=(a == order[0]),
-                        stop=(a == order[-1]),
-                    )
+        places = {0: 8, 1: 0, 2: 4, 3: 154}
+        logs = {k: placed([P, S if k < 3 else EARLY], F32, "logs%d" % k, places[k]) for k in range(4)}
+        rates = {k: placed([P, S], F32, "rates%d" % k, places[k - 1] if k else 60) for k in range(4)}
 
-        survival, rates = {}, {}
-        every = slice(0, BANK)
+        def in_bank(g, cols):
+            return banks[g][:, cols.start % BANK : (cols.stop - 1) % BANK + 1]
 
-        def squash(k, n, cols=every):
-            if (k, n) not in survival:
-                survival[k, n] = placed([P, BANK], F32, "survival%d%d" % (k, n), 4 * k + 2 * n)
-            nc.scalar.activation(out=survival[k, n][:, cols], in_=bank(k, n)[:, cols], func=ACT.Sigmoid, scale=-1.0)
+        def weigh(k, cols):
+            nc.gpsimd.tensor_tensor(rates[k][:, cols], rates[k][:, cols], weights[:, cols], ALU.mult)
 
-        def rate_tile(k, kibs):
-            if len(kibs) == 2:
-                for n in range(2):
-                    rates[k, n] = placed([P, BANK], F32, "rates%d%d" % (k, n), kibs[n])[:]
-            else:
-                rates[k] = placed([P, S], F32, "rates%d" % k, kibs[0])[:]
-                rates[k, 0], rates[k, 1] = rates[k][:, span(0)], rates[k][:, span(1)]
-
-        def logarithm(k, n, cols=every):
-            nc.scalar.activation(out=rates[k, n][:, cols], in_=survival[k, n][:, cols], func=ACT.Ln, bias=floor[:])
-
-        def finish(k, n, cols=every):
-            nc.vector.scalar_tensor_tensor(out=rates[k, n][:, cols], in0=rates[k, n][:, cols], scalar=-1.0, in1=bank(k, n)[:, cols], op0=ALU.mult, op1=ALU.max)
-
-        def weigh(into, part, cols):
-            nc.gpsimd.tensor_tensor(into, part, weights[:, cols], ALU.mult)
-
-        def scatter(k, part, cols):
-            nc.vector.tensor_copy(pages[k % PAGES][:].indirect(bins[:, entries(cols)]), part)
+        def scatter(k, cols):
+            nc.vector.tensor_copy(pages[k % PAGES][:].indirect(bins[:, entries(cols)]), rates[k][:, cols])
 
         whole_list = slice(0, S)
-        opening = [(0, 0), (0, 1)]
-        first_product(opening, (0, 1))
-        first_product([(1, 0)], (0, 1))
-        pieces = [slice(0, P), slice(P, BANK)]
-        for k, n in opening:
-            squash(k, n)
-        squash(1, 0, pieces[0])
-        rate_tile(0, (140, 144))
-        rate_tile(1, (146, 148))
-        for cols in pieces:
-            logarithm(0, 0, cols)
-        logarithm(0, 1)
-        logarithm(1, 0, pieces[0])
-        for cols in pieces:
-            finish(0, 0, cols)
-            weigh(rates[0, 0][:, cols], rates[0, 0][:, cols], cols)
-        finish(0, 1)
-        weighed01 = placed([P, BANK], F32, "weighed01", 166)
-        weigh(weighed01[:], rates[0, 1], span(1))
-        finish(1, 0, pieces[0])
-        weigh(rates[1, 0][:, pieces[0]], rates[1, 0][:, pieces[0]], pieces[0])
-        for cols in pieces:
-            scatter(0, rates[0, 0][:, cols], cols)
-        scatter(0, weighed01[:], span(1))
-        grouped[1, 1, 0] = placed([P, PACK * KP], BF16, "grouped110", 142)
-        nc.gpsimd.tensor_scalar(
-            grouped[1, 1, 0][:].rearrange("p (t m j) -> p t m j", t=PACK, j=PACK),
-            raws[1, 1][:].rearrange("p j (m t) -> p t m j", t=PACK),
-            1.0,
-            0.0,
-            ALU.mult,
-            ALU.add,
-        )
-        quantize_wf(1, 1, 0, 2, 0, 70, 73.75)
-        quantize_wf(1, 1, 2, 2, 0, 72, 74.25)
-
-        scatter(1, rates[1, 0][:, pieces[0]], pieces[0])
-
-        second = [(k, n) for k in (1, 2, 3) for n in range(2)]
-        for unit in second[1:]:
-            first_product([unit], (0, 1) if unit[0] == 1 else (1, 0))
-        for k, n in second:
-            squash(k, n, pieces[1] if (k, n) == (1, 0) else every)
-        rate_tile(2, (150,))
-        rate_tile(3, (154,))
-        for k, n in second:
-            logarithm(k, n, pieces[1] if (k, n) == (1, 0) else every)
-        finish(1, 0, pieces[1])
-        nc.vector.tensor_tensor(pages[1][:].indirect(bins[:, entries(pieces[1])]), rates[1, 0][:, pieces[1]], weights[:, pieces[1]], ALU.mult)
-        finish(1, 1)
-        weigh(rates[1, 1], rates[1, 1], span(1))
-        for k in (2, 3):
-            for n in range(2):
-                finish(k, n)
-            weigh(rates[k], rates[k], whole_list)
-        scatter(1, rates[1, 1], span(1))
-        scatter(2, rates[2], whole_list)
+        for g, (k, cols) in enumerate(first):
+            nc.scalar.activation(out=logs[k][:, cols], in_=in_bank(g, cols), func=ACT.Sigmoid, scale=-1.0)
+        pieces = [(0, 0, slice(0, P)), (0, 0, slice(P, BANK))] + [(g, k, cols) for g, (k, cols) in enumerate(first) if g > 0]
+        for g, k, cols in pieces:
+            nc.scalar.activation(out=logs[k][:, cols], in_=logs[k][:, cols], func=ACT.Ln, bias=floor[:])
+        for g, k, cols in pieces:
+            nc.vector.scalar_tensor_tensor(out=rates[k][:, cols], in0=logs[k][:, cols], scalar=-1.0, in1=in_bank(g, cols), op0=ALU.mult, op1=ALU.max)
+            if k in (0, 3):
+                weigh(k, cols)
+            elif cols.stop == S:
+                weigh(k, whole_list)
+        for g, k, cols in pieces[:3]:
+            scatter(k, cols)
+        pages.append(placed([P, T2], F32, "page3", 154))
+        nc.gpsimd.memset(pages[-1][:].bitcast(I32), 0)
+        scatter(1, whole_list)
+        scatter(2, whole_list)
+        scatter(3, span(0, EARLY))
 
         def thin(k, into, cols):
             nc.scalar.activation(out=into, in_=pages[k % PAGES][:, cols], func=ACT.Exp, scale=-1.0)
@@ -253,111 +200,127 @@ def tile_list_parts_depletion_kernel(tc, tab_words, tab_scales, offs, wf, wgs, o
             return ap.rearrange("p (c m) -> p c m", m=BANK)
 
         front, back, page_wide = span(1, 2 * BANK), span(0, 2 * BANK), slice(0, T2)
-        planes = {2: placed([P, 2, PACK, BANK], BF16, "planes_front", 168), 0: placed([P, 2, PACK, BANK], BF16, "planes_back", 176)}
+        planes = {2: placed([P, 2, PACK, BANK], BF16, "planes_front", 178), 0: placed([P, 2, PACK, BANK], BF16, "planes_back", 186)}
 
         def deplete(t, left, cols):
-            first, count = cols.start // BANK, (cols.stop - cols.start) // BANK
-            lo = 2 * (first // 2)
-            nc.gpsimd.tensor_tensor(planes[lo][:, first - lo : first - lo + count, t, :], by_chunk(left), by_chunk(stocks[0][:, t, cols]), ALU.mult)
+            lo = cols.start // BANK
+            nc.gpsimd.tensor_tensor(planes[lo][:, :, t, :], by_chunk(left), by_chunk(stocks[0][:, t, cols]), ALU.mult)
 
-        kept0 = placed([P, T2], F32, "kept0", 8)
-        thin(0, kept0[:], page_wide)
+        def thin_early(t):
+            kept = placed([P, T2], F32, "kept%d" % t, 162 + 8 * t)
+            for cols in (front, back):
+                thin(t, kept[:, cols], cols)
+                deplete(t, kept[:, cols], cols)
 
-        def turned_product(into, jt, t, count):
+        terms = placed([P, PACK, 2, S], F32, "terms", 16)
+        terms3 = placed([P, 2, S - EARLY], F32, "terms3", 48)
+        blocks = S // P
+        skipped = EARLY // P
+
+        def turned_product(into, jt, codes, scales):
             n, q = divmod(jt, PACK)
-            for a in (1, 0):
+            for a in range(PASSES):
                 nc.tensor.matmul_mx(
                     out=into,
                     lhsT=v_w[a, n][:, span(q, P)].bitcast(FP8X4),
                     lhsT_scale=v_s[n][4 * a : P, span(q, P)],
-                    rhs=(wf_w[a, 1, t] if count == 1 else wf_w[a, 1, t, count]).bitcast(FP8X4),
-                    rhs_scale=wf_s[a, 1, t] if count == 1 else wf_s[a, 1, t, count],
-                    start=(a == 1),
-                    stop=(a == 0),
+                    rhs=codes[a].bitcast(FP8X4),
+                    rhs_scale=scales[a],
+                    start=(a == 0),
+                    stop=(a == PASSES - 1),
                 )
 
-        lifted, decay, excess = {}, {}, {}
-
-        lifted5 = placed([P, S], F32, "lifted_tile5", 20)
+        groups = []
+        for lo in range(0, blocks - skipped, PACK):
+            count = min(PACK, blocks - skipped - lo)
+            groups.append((range(lo, lo + count), terms3[:, 0, span(lo, P, count)], terms3[:, 1, span(lo, P, count)]))
+        for jt in (0, 1, 2, 4, 3, 5, 6, 7):
+            groups.append((jt, terms[:, :, 0, span(jt, P)], terms[:, :, 1, span(jt, P)]))
 
         def lift(g):
-            lifted[g] = lifted5[:, span(g - 2)] if g in (2, 3) else placed([P, BANK], F32, "lifted%d" % g, 16 + 2 * g)[:]
-            nc.scalar.activation(out=lifted[g], in_=banks[g][:], func=ACT.Relu, bias=SHIFT)
+            which, lifted, decay = groups[g]
+            source = banks[(g % 3 + len(first)) % 8]
+            if isinstance(which, int):
+                turned_product(source[:], which, [wf_w[a, 1] for a in range(PASSES)], [wf_s[a, 1] for a in range(PASSES)])
+                sums = source[:].rearrange("p (t m) -> p t m", t=PACK)
+            else:
+                for i, block in enumerate(which):
+                    turned_product(source[:, span(i, P)], skipped + block, [wf_w[a, 0, 3] for a in range(PASSES)], [wf_s[a, 0, 3] for a in range(PASSES)])
+                sums = source[:, span(0, P, len(which))]
+            nc.scalar.activation(out=lifted, in_=sums, func=ACT.Relu, bias=SHIFT)
 
-        for n in range(2):
-            for q in range(PACK):
-                turned_product(banks[n][:, span(q, P)], PACK * n + q, 0, 1)
-            lift(n)
-        for n in range(2):
-            first_product([(5, n)], (1, 0))
-            lift(2 + n)
-        kept1 = placed([P, T2], F32, "kept1", 0)
-        for g in range(4, 8):
-            for i in range(2):
-                turned_product(banks[g][:, span(i, HALF)], 2 * (g - 4) + i, 2, 2)
-            lift(g)
-        for g in range(8):
-            decay[g] = placed([P, BANK], F32, "decay%d" % g, 158 + 2 * g if g < 4 else 24 + 2 * g)
-            nc.scalar.activation(out=decay[g][:], in_=lifted[g], func=ACT.Exp, scale=-1.0, bias=SHIFT)
-            if g == 1:
-                thin(1, kept1[:], page_wide)
-        kept2f = placed([P, 2 * BANK], F32, "kept2f", 58)
-        thin(2, kept2f[:], front)
-        scatter(3, rates[3], whole_list)
-        for t, left in ((0, kept0), (1, kept1)):
-            for cols in (front, back):
-                deplete(t, left[:, cols], cols)
-        deplete(2, kept2f[:], front)
+        lift(0)
+        for g in range(len(groups)):
+            if g + 1 < len(groups):
+                lift(g + 1)
+            nc.scalar.activation(out=groups[g][2], in_=groups[g][1], func=ACT.Exp, scale=-1.0, bias=SHIFT)
+            if g == 4:
+                thin_early(0)
+            if g == len(groups) - 2:
+                thin_early(1)
 
-        excess5 = placed([P, S], F32, "excess_tile5", 44)
-        for g in range(8):
-            excess[g] = excess5[:, span(g - 2)] if g in (2, 3) else placed([P, BANK], F32, "excess%d" % g, 40 + 2 * g if g < 4 else 180 + 2 * g)[:]
-            lowered = math.e**-SHIFT if g in (2, 3) else 1.0
-            nc.scalar.activation(out=excess[g], in_=decay[g][:], func=ACT.Ln, scale=lowered, bias=lowered)
+        def both(k):
+            return terms3 if k == 3 else terms[:, k - PACK]
 
-        def turn_back(into, g, block):
-            for term in (lifted, excess):
-                nc.tensor.matmul(into, lhsT=term[g][:, span(block, P)], rhs=identity[:], is_transpose=True, start=(term is lifted), stop=(term is excess))
+        def shifted(k, cols):
+            return slice(cols.start - EARLY, cols.stop - EARLY) if k == 3 else cols
 
-        rate_tile(4, (158, 160))
-        for n in range(2):
-            for q in range(PACK):
-                turn_back(banks[n][:, span(q, P)], n, q)
-            nc.vector.scalar_tensor_tensor(out=rates[4, n], in0=banks[n][:], scalar=-SHIFT, in1=weights[:, span(n)], op0=ALU.add, op1=ALU.mult)
-        for n in range(2):
-            scatter(4, rates[4, n], span(n))
-        rate_tile(5, (162,))
-        nc.gpsimd.tensor_tensor(rates[5], lifted5[:], excess5[:], ALU.add)
-        weigh(rates[5], rates[5], whole_list)
-        for t in range(2):
-            for jt in range(2 * PACK):
-                n, q = divmod(jt, PACK)
-                g, i = divmod(jt, 2)
-                turn_back(banks[4 + 2 * t + n][:, span(q, P)], 4 + g, 2 * i + t)
+        def logarithm(k, cols):
+            part = both(k)[:, 1, shifted(k, cols)]
+            nc.scalar.activation(out=part, in_=part, func=ACT.Ln, bias=1.0)
 
-        def lower(t, kib):
-            rate_tile(6 + t, (kib,))
+        def turn_back(k, cols, g):
+            lo = shifted(k, cols).start // P
+            for q in range((cols.stop - cols.start) // P):
+                for term in range(2):
+                    nc.tensor.matmul(banks[g][:, span(q, P)], lhsT=both(k)[:, term, span(lo + q, P)], rhs=identity[:], is_transpose=True, start=(term == 0), stop=(term == 1))
+
+        def lower(k, cols, g):
+            nc.scalar.activation(out=rates[k][:, cols], in_=banks[g][:, : cols.stop - cols.start], func=ACT.Copy, bias=-SHIFT)
+
+        def turn_tile(k):
+            logarithm(k, whole_list)
             for n in range(2):
-                nc.scalar.activation(out=rates[6 + t, n], in_=banks[4 + 2 * t + n][:], func=ACT.Copy, bias=-SHIFT)
+                turn_back(k, span(n), (2 * k + 3 + n) % 8)
 
-        kept3f = placed([P, 2 * BANK], F32, "kept3f", 184)
-        thin(3, kept3f[:], front)
-        lower(0, 16)
-        kept_back = placed([P, 2, 2 * BANK], F32, "kept_back", 40)
-        thin(2, kept_back[:, 0, :], back)
-        scatter(5, rates[5], whole_list)
-        lower(1, 150)
-        thin(3, kept_back[:, 1, :], back)
-        deplete(3, kept3f[:], front)
-        weigh(rates[6], rates[6], whole_list)
+        def lower_tile(k):
+            rates[k] = placed([P, S], F32, "rates%d" % k, places[k - 5] if k > 4 else 12)
+            for n in range(2):
+                lower(k, span(n), (2 * k + 3 + n) % 8)
+
+        rest = [slice(EARLY, BANK), span(1)]
+        for g, cols in enumerate(rest):
+            logarithm(3, cols)
+            turn_back(3, cols, 1 + g)
+        lower(3, rest[0], 1)
+        weigh(3, rest[0])
+        scatter(3, rest[0])
+        turn_tile(4)
+        lower(3, rest[1], 2)
+        weigh(3, rest[1])
+        scatter(3, rest[1])
+        for k in range(4, 7):
+            turn_tile(k + 1)
+            lower_tile(k)
+            weigh(k, whole_list)
+        for k in (4, 5):
+            scatter(k, whole_list)
+
+        kept_front = placed([P, 2, 2 * BANK], F32, "kept_front", 30)
+        kept_back = placed([P, 2, 2 * BANK], F32, "kept_back", 38)
+        for t in range(2):
+            thin(2 + t, kept_front[:, t, :], front)
+            thin(2 + t, kept_back[:, t, :], back)
+            deplete(2 + t, kept_front[:, t, :], front)
         nc.gpsimd.tensor_tensor(
             planes[0][:, :, 2:4, :].rearrange("p c t m -> p t c m"),
             kept_back[:].rearrange("p t (c m) -> p t c m", m=BANK),
             stocks[0][:, 2:4, back].rearrange("p t (c m) -> p t c m", m=BANK),
             ALU.mult,
         )
-        weigh(rates[7], rates[7], whole_list)
-        scatter(6, rates[6], whole_list)
+        scatter(6, whole_list)
+        lower_tile(7)
+        weigh(7, whole_list)
 
         zz = {}
 
@@ -369,18 +332,18 @@ def tile_list_parts_depletion_kernel(tc, tab_words, tab_scales, offs, wf, wgs, o
             )
 
         paired = span(1, BANK, 3)
-        kept4 = placed([P, 3 * BANK], F32, "kept4", 0)
-        interleave(3, 8)
+        kept4 = placed([P, 3 * BANK], F32, "kept4", 16)
         thin(4, kept4[:], paired)
-        interleave(2, 12)
-        kept5 = placed([P, 3 * BANK], F32, "kept5", 168)
+        interleave(3, 162)
+        interleave(2, 166)
+        kept5 = placed([P, 3 * BANK], F32, "kept5", 178)
         thin(5, kept5[:], paired)
-        ending_tile = placed([P, 12 * BANK], F32, "ending", 25)
+        ending_tile = placed([P, 12 * BANK], F32, "ending", 38)
         ending = ending_tile[:, 2 * BANK :]
         for t in range(2):
             thin(4 + t, ending[:, span(t)], span(0))
-        scatter(7, rates[7], whole_list)
-        interleave(1, 140)
+        scatter(7, whole_list)
+        interleave(1, 170)
 
         ending_rows = ending.bitcast(BF16).rearrange("p (r x) -> p r x", x=2 * BANK)
         late_rows = ending_tile[:].bitcast(BF16).rearrange("p (r x) -> p r x", x=BANK)
@@ -395,20 +358,20 @@ def tile_list_parts_depletion_kernel(tc, tab_words, tab_scales, offs, wf, wgs, o
         nc.gpsimd.tensor_tensor(ending_tile[:].bitcast(BF16)[:, span(0, 3 * BANK)], kept4[:], stocks[1][:, 0, paired], ALU.mult)
         nc.gpsimd.tensor_tensor(late_planes(3)[:, 1, :], kept5[:, span(2)], stocks[1][:, 1, span(3)], ALU.mult)
         nc.gpsimd.tensor_tensor(ending_rows[:, 9, :], kept5[:, span(0, BANK, 2)], stocks[1][:, 1, span(1, BANK, 2)], ALU.mult)
-        for c in range(CHUNKS):
-            thin(6, ending[:, span(2 + 2 * c)], span(c))
+        nc.scalar.activation(out=by_chunk(ending)[:, 2 : 2 + 2 * CHUNKS : 2, :], in_=by_chunk(pages[6 % PAGES][:]), func=ACT.Exp, scale=-1.0)
         pairs = {3: ending_rows[:, 3:6:2, :].rearrange("p h (u x) -> p h u x", u=2)}
-        for c, kib in ((2, 164), (1, 184)):
+        for c, kib in ((2, 174), (1, 194)):
             pairs[c] = placed([P, 2, 2, BANK], BF16, "pairs%d" % c, kib)[:]
         for c in (3, 1, 2):
             nc.scalar.copy(
                 out=pairs[c][:, :, 0, :].rearrange("p h (m i t) -> p h m t i", i=RUN, t=2),
                 in_=late_planes(c).rearrange("p t (h m i) -> p h m t i", h=2, i=RUN),
             )
-        zz[0, 0] = placed([P, PACK * BANK], BF16, "zz00", 168)
+        zz[0, 0] = placed([P, PACK * BANK], BF16, "zz00", 178)
         nc.gpsimd.tensor_scalar(zz[0, 0][:].rearrange("p (m t) -> p m t", t=PACK), planes[0][:, 0, :, :].rearrange("p t m -> p m t"), 1.0, 0.0, ALU.mult, ALU.add)
 
         halves = [span(0, HALF), span(1, HALF)]
+        every = slice(0, BANK)
 
         def within(c, cols):
             return slice(BANK * c + cols.start, BANK * c + cols.stop)
@@ -448,7 +411,7 @@ def tile_list_parts_depletion_kernel(tc, tab_words, tab_scales, offs, wf, wgs, o
         def quantize_z(key, source, kib):
             width = source.shape[1] // PACK
             z_w[key] = placed([P, width], U32, "z_w" + "".join(str(i) for i in key), kib)
-            z_s[key] = placed([P, width], U8, "z_s" + "".join(str(i) for i in key), 66 + 0.5 * len(z_s))
+            z_s[key] = placed([P, width], U8, "z_s" + "".join(str(i) for i in key), 64 + 0.5 * len(z_s))
             nc.vector.quantize_mx(out=z_w[key][:].bitcast(FP8X4), scales=z_s[key][:], in_=source)
 
         def second_product(into, key, nt, start, stop):
@@ -466,7 +429,7 @@ def tile_list_parts_depletion_kernel(tc, tab_words, tab_scales, offs, wf, wgs, o
         staged = []
 
         def leave(copy, source, rows, kib=None):
-            staged.append(placed([P, BANK], F32, "staged%d" % len(staged), 76 + 2 * len(staged) if kib is None else kib))
+            staged.append(placed([P, BANK], F32, "staged%d" % len(staged), 74 + 2 * len(staged) if kib is None else kib))
             copy(out=staged[-1][:], in_=source[:])
             nc.sync.dma_start(out=rows, in_=staged[-1][:] if len(rows.shape) == 2 else by_half(staged[-1][:]))
 
@@ -492,56 +455,56 @@ def tile_list_parts_depletion_kernel(tc, tab_words, tab_scales, offs, wf, wgs, o
         for cols in halves:
             thin_last(3, cols)
         thin_last(2)
-        quantize_z((0, 3), zz[0, 3][:], 150)
+        quantize_z((0, 3), zz[0, 3][:], 4)
         for h in range(2):
             z_w[0, 3, h], z_s[0, 3, h] = z_w[0, 3][:, halves[h]], z_s[0, 3][:, halves[h]]
         for g in range(2):
             half_product(0, 3, 0, g)
-        zz[1, 3] = placed([P, PACK * BANK], BF16, "zz13", 154)
+        zz[1, 3] = placed([P, PACK * BANK], BF16, "zz13", 198)
         for h in range(2):
             deplete_pair(3, h)
             weave(nc.scalar.copy, U32, 3, span(h, 1))
         thin_last(1)
         deplete_pair(2, 0)
-        quantize_z((1, 3, 0), zz[1, 3][:, times(halves[0], PACK)], 58)
+        quantize_z((1, 3, 0), zz[1, 3][:, times(halves[0], PACK)], 8)
         for g in range(2):
             half_product(1, 3, 0, g)
             leave_half(nc.scalar.copy, 3, 0, g)
         thin_last(0)
         deplete_pair(2, 1)
-        quantize_z((1, 3, 1), zz[1, 3][:, times(halves[1], PACK)], 59)
+        quantize_z((1, 3, 1), zz[1, 3][:, times(halves[1], PACK)], 9)
         for g in range(2):
             for b in (1, 0):
                 half_product(b, 3, 1, g, first=1)
             leave_half(nc.scalar.copy, 3, 1, g)
-        zz[1, 2] = placed([P, PACK * BANK], BF16, "zz12", 144)
+        zz[1, 2] = placed([P, PACK * BANK], BF16, "zz12", 202)
         weave(nc.vector.tensor_copy, F32, 2)
-        quantize_z((0, 2), zz[0, 2][:], 154)
+        quantize_z((0, 2), zz[0, 2][:], 198)
         open_chunk(2)
-        quantize_z((1, 2), zz[1, 2][:], 60)
+        quantize_z((1, 2), zz[1, 2][:], 10)
         close_chunk(2)
         for h in range(2):
             deplete_pair(1, h)
-        quantize_z((0, 1), zz[0, 1][:], 144)
+        quantize_z((0, 1), zz[0, 1][:], 202)
         open_chunk(1)
-        zz[1, 1] = placed([P, PACK * BANK], BF16, "zz11", 50)
+        zz[1, 1] = placed([P, PACK * BANK], BF16, "zz11", 206)
         weave(nc.vector.tensor_copy, F32, 1)
-        quantize_z((0, 0, 0), zz[0, 0][:, times(halves[0], PACK)], 140)
+        quantize_z((0, 0, 0), zz[0, 0][:, times(halves[0], PACK)], 170)
         quantize_z((1, 1), zz[1, 1][:], 0)
         close_chunk(1)
         for g in range(2):
             half_product(0, 0, 0, g)
-        deplete_whole(0, 8)
-        quantize_z((0, 0, 1), zz[0, 0][:, times(halves[1], PACK)], 50)
-        quantize_z((1, 0, 0), zz[1, 0, 0][:], 2)
+        deplete_whole(0, 162)
+        quantize_z((0, 0, 1), zz[0, 0][:, times(halves[1], PACK)], 206)
+        quantize_z((1, 0, 0), zz[1, 0, 0][:], 12)
         for g in range(2):
             half_product(1, 0, 0, g)
         for g in range(2):
             half_product(0, 0, 1, g)
-        deplete_whole(1, 10)
+        deplete_whole(1, 164)
         leave_half(nc.scalar.copy, 0, 0, 0)
-        quantize_z((1, 0, 1), zz[1, 0, 1][:], 3)
-        leave_half(nc.vector.tensor_copy, 0, 0, 1, 10)
+        quantize_z((1, 0, 1), zz[1, 0, 1][:], 13)
+        leave_half(nc.vector.tensor_copy, 0, 0, 1, 164)
         for g in range(2):
             half_product(1, 0, 1, g)
         leave_half(nc.scalar.copy, 0, 1, 0)

@@ -200,11 +200,11 @@ def tile_list_parts_depletion_kernel(tc, tab_words, tab_scales, offs, wf, wgs, o
             return ap.rearrange("p (c m) -> p c m", m=BANK)
 
         front, back, page_wide = span(1, 2 * BANK), span(0, 2 * BANK), slice(0, T2)
-        planes = {2: placed([P, 2, PACK, BANK], BF16, "planes_front", 178), 0: placed([P, 2, PACK, BANK], BF16, "planes_back", 186)}
+        planes = {2: placed([P, 2, 2, BANK, 2], BF16, "planes_front", 178), 0: placed([P, 2, 2, BANK, 2], BF16, "planes_back", 186)}
 
         def deplete(t, left, cols):
             lo = cols.start // BANK
-            nc.gpsimd.tensor_tensor(planes[lo][:, :, t, :], by_chunk(left), by_chunk(stocks[0][:, t, cols]), ALU.mult)
+            nc.gpsimd.tensor_tensor(planes[lo][:, :, t // 2, :, t % 2], by_chunk(left), by_chunk(stocks[0][:, t, cols]), ALU.mult)
 
         def thin_early(t):
             kept = placed([P, T2], F32, "kept%d" % t, 162 + 8 * t)
@@ -313,7 +313,7 @@ def tile_list_parts_depletion_kernel(tc, tab_words, tab_scales, offs, wf, wgs, o
             thin(2 + t, kept_back[:, t, :], back)
             deplete(2 + t, kept_front[:, t, :], front)
         nc.gpsimd.tensor_tensor(
-            planes[0][:, :, 2:4, :].rearrange("p c t m -> p t c m"),
+            planes[0][:, :, 1, :, :].rearrange("p c m t -> p t c m"),
             kept_back[:].rearrange("p t (c m) -> p t c m", m=BANK),
             stocks[0][:, 2:4, back].rearrange("p t (c m) -> p t c m", m=BANK),
             ALU.mult,
@@ -327,48 +327,43 @@ def tile_list_parts_depletion_kernel(tc, tab_words, tab_scales, offs, wf, wgs, o
         def interleave(c, kib):
             zz[0, c] = placed([P, PACK * BANK], BF16, "zz0%d" % c, kib)
             nc.scalar.copy(
-                out=zz[0, c][:].rearrange("p (m i t) -> p m t i", i=RUN, t=PACK),
-                in_=planes[2 * (c // 2)][:, c % 2, :, :].rearrange("p t (m i) -> p m t i", i=RUN),
+                out=zz[0, c][:].bitcast(U32).rearrange("p (m i u) -> p m u i", u=2, i=2),
+                in_=planes[2 * (c // 2)][:, c % 2].rearrange("p u m t -> p u (m t)").bitcast(U32).rearrange("p u (m i) -> p m u i", i=2),
             )
 
         paired = span(1, BANK, 3)
         kept4 = placed([P, 3 * BANK], F32, "kept4", 16)
-        thin(4, kept4[:], paired)
         interleave(3, 162)
+        thin(4, kept4[:], paired)
         interleave(2, 166)
-        kept5 = placed([P, 3 * BANK], F32, "kept5", 178)
-        thin(5, kept5[:], paired)
-        ending_tile = placed([P, 12 * BANK], F32, "ending", 38)
-        ending = ending_tile[:, 2 * BANK :]
+        ending = placed([P, 23, BANK], F32, "ending", 38)
+        rows = {(4, 0): 6, (5, 0): 11, (6, 0): 16, (7, 0): 21, (6, 1): 0, (7, 1): 22, (6, 2): 2, (7, 2): 3, (6, 3): 4, (7, 3): 5}
+
+        def thin_chunks(k, into):
+            nc.scalar.activation(out=into, in_=by_chunk(pages[k % PAGES][:, paired]), func=ACT.Exp, scale=-1.0)
+
+        kept5 = ending[:, 1:6:2, :]
+        thin_chunks(5, kept5)
         for t in range(2):
-            thin(4 + t, ending[:, span(t)], span(0))
+            thin(4 + t, ending[:, rows[4 + t, 0], :], span(0))
         scatter(7, whole_list)
         interleave(1, 170)
-
-        ending_rows = ending.bitcast(BF16).rearrange("p (r x) -> p r x", x=2 * BANK)
-        late_rows = ending_tile[:].bitcast(BF16).rearrange("p (r x) -> p r x", x=BANK)
-        second_row = {3: 18, 1: 22, 2: 23}
-
-        def late_planes(c):
-            return late_rows[:, c - 1 : second_row[c] + 1 : second_row[c] - c + 1, :]
+        interleave(0, 178)
 
         def by_half(ap):
             return ap.rearrange("p (h m) -> p h m", h=2)
 
-        nc.gpsimd.tensor_tensor(ending_tile[:].bitcast(BF16)[:, span(0, 3 * BANK)], kept4[:], stocks[1][:, 0, paired], ALU.mult)
-        nc.gpsimd.tensor_tensor(late_planes(3)[:, 1, :], kept5[:, span(2)], stocks[1][:, 1, span(3)], ALU.mult)
-        nc.gpsimd.tensor_tensor(ending_rows[:, 9, :], kept5[:, span(0, BANK, 2)], stocks[1][:, 1, span(1, BANK, 2)], ALU.mult)
-        nc.scalar.activation(out=by_chunk(ending)[:, 2 : 2 + 2 * CHUNKS : 2, :], in_=by_chunk(pages[6 % PAGES][:]), func=ACT.Exp, scale=-1.0)
-        pairs = {3: ending_rows[:, 3:6:2, :].rearrange("p h (u x) -> p h u x", u=2)}
-        for c, kib in ((2, 174), (1, 194)):
-            pairs[c] = placed([P, 2, 2, BANK], BF16, "pairs%d" % c, kib)[:]
-        for c in (3, 1, 2):
-            nc.scalar.copy(
-                out=pairs[c][:, :, 0, :].rearrange("p h (m i t) -> p h m t i", i=RUN, t=2),
-                in_=late_planes(c).rearrange("p t (h m i) -> p h m t i", h=2, i=RUN),
+        def in_halves(ap):
+            return ap.rearrange("p c (h m) -> p c h m", m=HALF)
+
+        pair_rows = ending[:, 17:23, :].bitcast(BF16).rearrange("p h (u x) -> p h u x", u=2)
+        pairs = {c: pair_rows[:, span(c - 1, 2)] for c in (3, 2, 1)}
+        for t, kept in ((0, by_chunk(kept4[:])), (1, kept5)):
+            nc.gpsimd.tensor_tensor(
+                pair_rows[:, :, 0, :].rearrange("p (c h) (m t) -> p c h m t", h=2, t=2)[:, :, :, :, t], in_halves(kept), in_halves(by_chunk(stocks[1][:, t, paired])), ALU.mult
             )
-        zz[0, 0] = placed([P, PACK * BANK], BF16, "zz00", 178)
-        nc.gpsimd.tensor_scalar(zz[0, 0][:].rearrange("p (m t) -> p m t", t=PACK), planes[0][:, 0, :, :].rearrange("p t m -> p m t"), 1.0, 0.0, ALU.mult, ALU.add)
+        thin_chunks(6, ending[:, 0:5:2, :])
+        thin(6, ending[:, rows[6, 0], :], span(0))
 
         halves = [span(0, HALF), span(1, HALF)]
         every = slice(0, BANK)
@@ -380,13 +375,13 @@ def tile_list_parts_depletion_kernel(tc, tab_words, tab_scales, offs, wf, wgs, o
             return slice(cols.start * factor, cols.stop * factor)
 
         def thin_last(c, cols=every):
-            thin(7, ending[:, within(3 + 2 * c, cols)], within(c, cols))
+            thin(7, ending[:, rows[7, c], cols], within(c, cols))
 
         def deplete_pair(c, h):
             cols = halves[h]
             nc.vector.tensor_tensor(
                 pairs[c][:, h, 1, :].rearrange("p (m i t) -> p m t i", i=RUN, t=2),
-                by_chunk(ending[:, span(1 + c, 2 * BANK)])[:, :, cols].rearrange("p t (m i) -> p m t i", i=RUN),
+                ending[:, rows[6, c] : rows[7, c] + 1 : rows[7, c] - rows[6, c], cols].rearrange("p t (m i) -> p m t i", i=RUN),
                 stocks[1][:, 2:4, within(c, cols)].rearrange("p t (m i) -> p m t i", i=RUN),
                 ALU.mult,
             )
@@ -401,7 +396,7 @@ def tile_list_parts_depletion_kernel(tc, tab_words, tab_scales, offs, wf, wgs, o
             zz[1, 0, h] = placed([P, PACK * HALF], BF16, "zz10%d" % h, kib)
             nc.vector.tensor_tensor(
                 zz[1, 0, h][:].rearrange("p (m i t) -> p m t i", i=RUN, t=PACK),
-                by_chunk(ending[:, span(0, PACK * BANK)])[:, :, halves[h]].rearrange("p t (m i) -> p m t i", i=RUN),
+                ending[:, 6:22:5, halves[h]].rearrange("p t (m i) -> p m t i", i=RUN),
                 stocks[1][:, :, halves[h]].rearrange("p t (m i) -> p m t i", i=RUN),
                 ALU.mult,
             )
@@ -411,7 +406,7 @@ def tile_list_parts_depletion_kernel(tc, tab_words, tab_scales, offs, wf, wgs, o
         def quantize_z(key, source, kib):
             width = source.shape[1] // PACK
             z_w[key] = placed([P, width], U32, "z_w" + "".join(str(i) for i in key), kib)
-            z_s[key] = placed([P, width], U8, "z_s" + "".join(str(i) for i in key), 64 + 0.5 * len(z_s))
+            z_s[key] = placed([P, width], U8, "z_s" + "".join(str(i) for i in key), 16 + 0.5 * len(z_s))
             nc.vector.quantize_mx(out=z_w[key][:].bitcast(FP8X4), scales=z_s[key][:], in_=source)
 
         def second_product(into, key, nt, start, stop):
@@ -429,7 +424,7 @@ def tile_list_parts_depletion_kernel(tc, tab_words, tab_scales, offs, wf, wgs, o
         staged = []
 
         def leave(copy, source, rows, kib=None):
-            staged.append(placed([P, BANK], F32, "staged%d" % len(staged), 74 + 2 * len(staged) if kib is None else kib))
+            staged.append(placed([P, BANK], F32, "staged%d" % len(staged), (84 if len(staged) < 11 else 6) + 2 * len(staged) if kib is None else kib))
             copy(out=staged[-1][:], in_=source[:])
             nc.sync.dma_start(out=rows, in_=staged[-1][:] if len(rows.shape) == 2 else by_half(staged[-1][:]))
 

@@ -337,7 +337,7 @@ def tile_list_parts_depletion_kernel(tc, tab_words, tab_scales, offs, wf, wgs, o
         thin(4, kept4[:], paired)
         interleave(2, 166)
         ending = placed([P, 23, BANK], F32, "ending", 38)
-        rows = {(4, 0): 6, (5, 0): 11, (6, 0): 16, (7, 0): 21, (6, 1): 0, (7, 1): 22, (6, 2): 2, (7, 2): 3, (6, 3): 4, (7, 3): 5}
+        rows = {(4, 0): 6, (5, 0): 11, (6, 0): 16, (7, 0): 21, (6, 1): 0, (7, 1): 22, (6, 2): 2, (7, 2): 2, (6, 3): 4, (7, 3): 4}
 
         def thin_chunks(k, into):
             nc.scalar.activation(out=into, in_=by_chunk(pages[k % PAGES][:, paired]), func=ACT.Exp, scale=-1.0)
@@ -363,6 +363,9 @@ def tile_list_parts_depletion_kernel(tc, tab_words, tab_scales, offs, wf, wgs, o
                 pair_rows[:, :, 0, :].rearrange("p (c h) (m t) -> p c h m t", h=2, t=2)[:, :, :, :, t], in_halves(kept), in_halves(by_chunk(stocks[1][:, t, paired])), ALU.mult
             )
         thin_chunks(6, ending[:, 0:5:2, :])
+        nc.gpsimd.tensor_tensor(
+            pair_rows[:, 2:6, 1, :].rearrange("p (c h) (m t) -> p c h m t", h=2, t=2)[:, :, :, :, 0], in_halves(ending[:, 2:5:2, :]), in_halves(by_chunk(stocks[1][:, 2, front])), ALU.mult
+        )
         thin(6, ending[:, rows[6, 0], :], span(0))
 
         halves = [span(0, HALF), span(1, HALF)]
@@ -379,6 +382,9 @@ def tile_list_parts_depletion_kernel(tc, tab_words, tab_scales, offs, wf, wgs, o
 
         def deplete_pair(c, h):
             cols = halves[h]
+            if c > 1:
+                nc.vector.tensor_tensor(pairs[c][:, h, 1, :].rearrange("p (m t) -> p m t", t=2)[:, :, 1], ending[:, rows[7, c], cols], stocks[1][:, 3, within(c, cols)], ALU.mult)
+                return
             nc.vector.tensor_tensor(
                 pairs[c][:, h, 1, :].rearrange("p (m i t) -> p m t i", i=RUN, t=2),
                 ending[:, rows[6, c] : rows[7, c] + 1 : rows[7, c] - rows[6, c], cols].rearrange("p t (m i) -> p m t i", i=RUN),

from contextlib import ExitStack

import concourse.mybir as mybir
from concourse.masks import make_identity

K, H, N, T, S, T2 = 1024, 1024, 512, 2048, 1024, 2048
FLOPS = 2 * K * H * S + 2 * H * N * T2

F32 = mybir.dt.float32
BF16 = mybir.dt.bfloat16
I32 = mybir.dt.int32
U32 = mybir.dt.uint32
U16 = mybir.dt.uint16
U8 = mybir.dt.uint8
FP8X4 = mybir.dt.float8_e4m3fn_x4
FP4X4 = mybir.dt.float4_e2m1fn_x4
ACT = mybir.ActivationFunctionType
ALU = mybir.AluOpType

P = 128
PACK = 4
KP = P * PACK
BANK = 512
HALF = BANK // 2
PASSES = K // KP
CHUNKS = T2 // BANK
PAGES = 4
CAP = 43.5
SHIFT = 24.0
KIB = 1024
RUN = 4
EARLY = 256


def tile_list_parts_depletion_kernel(tc, tab_words, tab_scales, offs, wf, wgs, offs2, stock, wc_words, wc_scales, out):
    nc = tc.nc
    with ExitStack() as ctx:
        keep = ctx.enter_context(tc.tile_pool(name="keep", bufs=1))
        arena = ctx.enter_context(tc.tile_pool(name="arena", bufs=1))
        psum = ctx.enter_context(tc.psum_pool(name="psum", bufs=1))

        def held(shape, dtype, name):
            return keep.tile(shape, dtype, name=name, align_bytes=64)

        def placed(shape, dtype, name, kib):
            return arena.tile(shape, dtype, name=name, offset=int(kib * KIB), align_bytes=64)

        def span(i, width=BANK, count=1):
            return slice(width * i, width * (i + count))

        def entries(cols):
            return slice(cols.start // 16, cols.stop // 16)

        parts = keep.tile([P, S // 16], U16, name="parts")
        bins = keep.tile([P, S // 16], U16, name="bins")
        tab_s = held([P, T], U8, "tab_s")
        v_w = {(a, n): placed([P, BANK], U32, "v_w%d%d" % (a, n), 162 + 8 * n + 4 * a) for a in range(PASSES) for n in range(2)}
        v_s = [held([P, BANK], U8, "v_s%d" % n) for n in range(2)]
        pages = [held([P, T2], F32, "page0")]
        wc_w = held([P, PASSES, 2 * N], U8, "wc_w")
        wc_s = held([P, PASSES, N], U8, "wc_s")
        weights = held([P, S], F32, "weights")
        floor = held([P, 1], F32, "floor")
        identity = held([P, P], F32, "identity")
        banks = [psum.tile([P, BANK], F32, name="bank%d" % i) for i in range(8)]

        nc.vector.memset(tab_s[:].bitcast(I32), 0)
        nc.vector.memset(pages[0][:].bitcast(I32), 0)
        nc.vector.memset(wc_s[:].rearrange("p a n -> p (a n)").bitcast(I32), 0)
        nc.scalar.activation(out=floor[:], in_=pages[0][:, 0:1], func=ACT.Sigmoid, bias=-CAP)
        make_identity(nc, identity[:])

        landing = placed([P, T // 4], I32, "landing", 145)
        tab_w = [placed([P, T], I32, "tab_w%d" % a, 8 * a) for a in range(PASSES)]
        raws = {(a, b): placed([P, PACK, KP], F32, "raw%d%d" % (a, b), 16 + 8 * a + 16 * b) for a in range(PASSES) for b in range(PASSES)}
        stocks = [placed([P, PACK, T2], F32, "stock%d" % b, 74 + 32 * b) for b in range(PASSES)]

        def load_wf(a, b):
            nc.sync.dma_start(out=raws[a, b][:], in_=wf[span(a, KP), span(b, KP)].rearrange("(p j) c -> p j c", j=PACK))

        def load_stock(b, rows):
            nc.sync.dma_start(out=stocks[b][:, rows, :], in_=stock[span(b, KP), :].rearrange("(p t) m -> p t m", t=PACK)[:, rows, :])

        nc.sync.dma_start(parts[:], offs)
        for q in range(2):
            nc.sync.dma_start(out=landing[32 * q : 32 * q + 4 * PASSES, :], in_=tab_scales[:, 4 * q : 4 * q + 4, :].bitcast(I32))
        for q in range(2, 4):
            for a in range(PASSES):
                nc.sync.dma_start(out=landing[32 * q + 4 * a : 32 * q + 4 * a + 4, :], in_=tab_scales[a, 4 * q : 4 * q + 4, :].bitcast(I32))
        for a in range(PASSES):
            nc.sync.dma_start(out=tab_w[a][:], in_=tab_words[a].rearrange("p t i -> p (t i)").bitcast(I32))
            load_wf(a, 0)
        nc.sync.dma_start(bins[:], offs2)
        for a in range(PASSES):
            load_wf(a, 1)
        nc.sync.dma_start(out=weights[:], in_=wgs)
        for b in range(PASSES):
            for u in range(2):
                load_stock(b, span(u, 2))
        nc.sync.dma_start(out=wc_w[:].bitcast(I32), in_=wc_words.rearrange("a p n -> p a n").bitcast(I32))
        for q in range(4):
            nc.sync.dma_start(out=wc_s[32 * q : 32 * q + 4, :, :].bitcast(I32), in_=wc_scales[:, 4 * q : 4 * q + 4, :].rearrange("a r n -> r a n").bitcast(I32))

        for q in range(4):
            rows = slice(32 * q, 32 * q + 4 * PASSES)
            nc.vector.tensor_copy(out=tab_s[rows, :].bitcast(I32), in_=landing[rows, :])
        for kib in (138, 146):
            pages.append(placed([P, T2], F32, "page%d" % len(pages), kib))
            nc.gpsimd.memset(pages[-1][:].bitcast(I32), 0)

        def gather_words(a):
            for n in range(2):
                nc.vector.tensor_copy(v_w[a, n][:], tab_w[a][:].bitcast(U32).indirect(parts[:, entries(span(n))]))

        grouped, wf_w, wf_s = {}, {}, {}

        def round_wf(copy, a, b, lo, hi):
            whole = placed([P, (hi - lo) * KP], BF16, "grouped%d%d%d" % (a, b, lo), 48 + 4 * a + 8 * b + lo)
            src = raws[a, b][:].rearrange("p j (m t) -> p m j t", t=PACK)
            copy(out=whole[:].rearrange("p (t m j) -> p m j t", t=hi - lo, j=PACK), in_=src[:, :, :, lo:hi])
            grouped[a, b, lo] = whole

        def quantize_wf(a, b, t, count, source):
            place = 2 * a + 4 * b + t / 2
            codes = placed([P, count * P], U32, "wf_w%d%d%d" % (a, b, t), 64 + place)
            scales = placed([P, count * P], U8, "wf_s%d%d%d" % (a, b, t), 72 + place / 4)
            nc.vector.quantize_mx(out=codes[:].bitcast(FP8X4), scales=scales[:], in_=grouped[a, b, source][:, span(t - source, KP, count)])
            for i in range(count):
                wf_w[a, b, t + i], wf_s[a, b, t + i] = codes[:, span(i, P)], scales[:, span(i, P)]
            wf_w[a, b], wf_s[a, b] = codes[:], scales[:]

        for n in range(2):
            nc.vector.tensor_copy(v_s[n][:], tab_s[:].indirect(parts[:, entries(span(n))]))
        gather_words(0)
        round_wf(nc.scalar.copy, 0, 0, 0, 2)
        round_wf(nc.scalar.copy, 0, 0, 2, 4)
        quantize_wf(0, 0, 0, 2, 0)
        gather_words(1)
        quantize_wf(0, 0, 2, 2, 2)
        round_wf(nc.vector.tensor_copy, 1, 0, 0, 2)
        round_wf(nc.scalar.copy, 1, 0, 2, 4)
        quantize_wf(1, 0, 0, 1, 0)
        quantize_wf(1, 0, 1, 1, 0)
        quantize_wf(1, 0, 2, 2, 2)
        for a in range(PASSES):
            round_wf(nc.vector.tensor_copy, a, 1, 0, PACK)
            quantize_wf(a, 1, 0, PACK, 0)

        first = [(k, span(n)) for k in range(3) for n in range(2)] + [(3, span(0, EARLY))]
        for a in range(PASSES):
            for g, (k, cols) in enumerate(first):
                n, width = cols.start // BANK, cols.stop - cols.start
                nc.tensor.matmul_mx(
                    out=banks[g][:, :width],
                    lhsT=wf_w[a, 0, k].bitcast(FP8X4),
                    lhsT_scale=wf_s[a, 0, k],
                    rhs=v_w[a, n][:, :width].bitcast(FP8X4),
                    rhs_scale=v_s[n][4 * a : P, :width],
                    start=(a == 0),
                    stop=(a == PASSES - 1),
                )

        places = {0: 8, 1: 0, 2: 4, 3: 154}
        logs = {k: placed([P, S if k < 3 else EARLY], F32, "logs%d" % k, places[k]) for k in range(4)}
        rates = {k: placed([P, S], F32, "rates%d" % k, places[k - 1] if k else 60) for k in range(4)}

        def in_bank(g, cols):
            return banks[g][:, cols.start % BANK : (cols.stop - 1) % BANK + 1]

        def weigh(k, cols):
            nc.gpsimd.tensor_tensor(rates[k][:, cols], rates[k][:, cols], weights[:, cols], ALU.mult)

        def scatter(k, cols):
            nc.vector.tensor_copy(pages[k % PAGES][:].indirect(bins[:, entries(cols)]), rates[k][:, cols])

        whole_list = slice(0, S)
        for g, (k, cols) in enumerate(first):
            nc.scalar.activation(out=logs[k][:, cols], in_=in_bank(g, cols), func=ACT.Sigmoid, scale=-1.0)
        pieces = [(0, 0, slice(0, P)), (0, 0, slice(P, BANK))] + [(g, k, cols) for g, (k, cols) in enumerate(first) if g > 0]
        for g, k, cols in pieces:
            nc.scalar.activation(out=logs[k][:, cols], in_=logs[k][:, cols], func=ACT.Ln, bias=floor[:])
        for g, k, cols in pieces:
            nc.vector.scalar_tensor_tensor(out=rates[k][:, cols], in0=logs[k][:, cols], scalar=-1.0, in1=in_bank(g, cols), op0=ALU.mult, op1=ALU.max)
            if k in (0, 3):
                weigh(k, cols)
            elif cols.stop == S:
                weigh(k, whole_list)
        for g, k, cols in pieces[:3]:
            scatter(k, cols)
        pages.append(placed([P, T2], F32, "page3", 154))
        nc.gpsimd.memset(pages[-1][:].bitcast(I32), 0)
        scatter(1, whole_list)
        scatter(2, whole_list)
        scatter(3, span(0, EARLY))

        def thin(k, into, cols):
            nc.scalar.activation(out=into, in_=pages[k % PAGES][:, cols], func=ACT.Exp, scale=-1.0)

        def by_chunk(ap):
            return ap.rearrange("p (c m) -> p c m", m=BANK)

        front, back, page_wide = span(1, 2 * BANK), span(0, 2 * BANK), slice(0, T2)
        planes = {2: placed([P, 2, 2, BANK, 2], BF16, "planes_front", 178), 0: placed([P, 2, 2, BANK, 2], BF16, "planes_back", 186)}

        def deplete(t, left, cols):
            lo = cols.start // BANK
            nc.gpsimd.tensor_tensor(planes[lo][:, :, t // 2, :, t % 2], by_chunk(left), by_chunk(stocks[0][:, t, cols]), ALU.mult)

        def thin_early(t):
            kept = placed([P, T2], F32, "kept%d" % t, 162 + 8 * t)
            for cols in (front, back):
                thin(t, kept[:, cols], cols)
                deplete(t, kept[:, cols], cols)

        terms = placed([P, PACK, 2, S], F32, "terms", 16)
        terms3 = placed([P, 2, S - EARLY], F32, "terms3", 48)
        blocks = S // P
        skipped = EARLY // P

        def turned_product(into, jt, codes, scales):
            n, q = divmod(jt, PACK)
            for a in range(PASSES):
                nc.tensor.matmul_mx(
                    out=into,
                    lhsT=v_w[a, n][:, span(q, P)].bitcast(FP8X4),
                    lhsT_scale=v_s[n][4 * a : P, span(q, P)],
                    rhs=codes[a].bitcast(FP8X4),
                    rhs_scale=scales[a],
                    start=(a == 0),
                    stop=(a == PASSES - 1),
                )

        groups = []
        for lo in range(0, blocks - skipped, PACK):
            count = min(PACK, blocks - skipped - lo)
            groups.append((range(lo, lo + count), terms3[:, 0, span(lo, P, count)], terms3[:, 1, span(lo, P, count)]))
        for jt in (0, 1, 2, 4, 3, 5, 6, 7):
            groups.append((jt, terms[:, :, 0, span(jt, P)], terms[:, :, 1, span(jt, P)]))

        def lift(g):
            which, lifted, decay = groups[g]
            source = banks[(g % 3 + len(first)) % 8]
            if isinstance(which, int):
                turned_product(source[:], which, [wf_w[a, 1] for a in range(PASSES)], [wf_s[a, 1] for a in range(PASSES)])
                sums = source[:].rearrange("p (t m) -> p t m", t=PACK)
            else:
                for i, block in enumerate(which):
                    turned_product(source[:, span(i, P)], skipped + block, [wf_w[a, 0, 3] for a in range(PASSES)], [wf_s[a, 0, 3] for a in range(PASSES)])
                sums = source[:, span(0, P, len(which))]
            nc.scalar.activation(out=lifted, in_=sums, func=ACT.Relu, bias=SHIFT)

        lift(0)
        for g in range(len(groups)):
            if g + 1 < len(groups):
                lift(g + 1)
            nc.scalar.activation(out=groups[g][2], in_=groups[g][1], func=ACT.Exp, scale=-1.0, bias=SHIFT)
            if g == 4:
                thin_early(0)
            if g == len(groups) - 2:
                thin_early(1)

        def both(k):
            return terms3 if k == 3 else terms[:, k - PACK]

        def shifted(k, cols):
            return slice(cols.start - EARLY, cols.stop - EARLY) if k == 3 else cols

        def logarithm(k, cols):
            part = both(k)[:, 1, shifted(k, cols)]
            nc.scalar.activation(out=part, in_=part, func=ACT.Ln, bias=1.0)

        def turn_back(k, cols, g):
            lo = shifted(k, cols).start // P
            for q in range((cols.stop - cols.start) // P):
                for term in range(2):
                    nc.tensor.matmul(banks[g][:, span(q, P)], lhsT=both(k)[:, term, span(lo + q, P)], rhs=identity[:], is_transpose=True, start=(term == 0), stop=(term == 1))

        def lower(k, cols, g):
            nc.scalar.activation(out=rates[k][:, cols], in_=banks[g][:, : cols.stop - cols.start], func=ACT.Copy, bias=-SHIFT)

        def turn_tile(k):
            logarithm(k, whole_list)
            for n in range(2):
                turn_back(k, span(n), (2 * k + 3 + n) % 8)

        def lower_tile(k):
            rates[k] = placed([P, S], F32, "rates%d" % k, places[k - 5] if k > 4 else 12)
            for n in range(2):
                lower(k, span(n), (2 * k + 3 + n) % 8)

        rest = [slice(EARLY, BANK), span(1)]
        for g, cols in enumerate(rest):
            logarithm(3, cols)
            turn_back(3, cols, 1 + g)
        lower(3, rest[0], 1)
        weigh(3, rest[0])
        scatter(3, rest[0])
        turn_tile(4)
        lower(3, rest[1], 2)
        weigh(3, rest[1])
        scatter(3, rest[1])
        for k in range(4, 7):
            turn_tile(k + 1)
            lower_tile(k)
            weigh(k, whole_list)
        for k in (4, 5):
            scatter(k, whole_list)

        kept_front = placed([P, 2, 2 * BANK], F32, "kept_front", 30)
        kept_back = placed([P, 2, 2 * BANK], F32, "kept_back", 38)
        for t in range(2):
            thin(2 + t, kept_front[:, t, :], front)
            thin(2 + t, kept_back[:, t, :], back)
            deplete(2 + t, kept_front[:, t, :], front)
        nc.gpsimd.tensor_tensor(
            planes[0][:, :, 1, :, :].rearrange("p c m t -> p t c m"),
            kept_back[:].rearrange("p t (c m) -> p t c m", m=BANK),
            stocks[0][:, 2:4, back].rearrange("p t (c m) -> p t c m", m=BANK),
            ALU.mult,
        )
        scatter(6, whole_list)
        lower_tile(7)
        weigh(7, whole_list)

        zz = {}

        def interleave(c, kib):
            zz[0, c] = placed([P, PACK * BANK], BF16, "zz0%d" % c, kib)
            nc.scalar.copy(
                out=zz[0, c][:].bitcast(U32).rearrange("p (m i u) -> p m u i", u=2, i=2),
                in_=planes[2 * (c // 2)][:, c % 2].rearrange("p u m t -> p u (m t)").bitcast(U32).rearrange("p u (m i) -> p m u i", i=2),
            )

        paired = span(1, BANK, 3)
        kept4 = placed([P, 3 * BANK], F32, "kept4", 16)
        interleave(3, 162)
        thin(4, kept4[:], paired)
        interleave(2, 166)
        ending = placed([P, 23, BANK], F32, "ending", 38)
        rows = {(4, 0): 6, (5, 0): 11, (6, 0): 16, (7, 0): 21, (6, 1): 0, (7, 1): 22, (6, 2): 2, (7, 2): 2, (6, 3): 4, (7, 3): 4}

        def thin_chunks(k, into):
            nc.scalar.activation(out=into, in_=by_chunk(pages[k % PAGES][:, paired]), func=ACT.Exp, scale=-1.0)

        kept5 = ending[:, 1:6:2, :]
        thin_chunks(5, kept5)
        for t in range(2):
            thin(4 + t, ending[:, rows[4 + t, 0], :], span(0))
        scatter(7, whole_list)
        interleave(1, 170)
        interleave(0, 178)

        def by_half(ap):
            return ap.rearrange("p (h m) -> p h m", h=2)

        def in_halves(ap):
            return ap.rearrange("p c (h m) -> p c h m", m=HALF)

        pair_rows = ending[:, 17:23, :].bitcast(BF16).rearrange("p h (u x) -> p h u x", u=2)
        pairs = {c: pair_rows[:, span(c - 1, 2)] for c in (3, 2, 1)}
        for t, kept in ((0, by_chunk(kept4[:])), (1, kept5)):
            nc.gpsimd.tensor_tensor(
                pair_rows[:, :, 0, :].rearrange("p (c h) (m t) -> p c h m t", h=2, t=2)[:, :, :, :, t], in_halves(kept), in_halves(by_chunk(stocks[1][:, t, paired])), ALU.mult
            )
        thin_chunks(6, ending[:, 0:5:2, :])
        nc.gpsimd.tensor_tensor(
            pair_rows[:, 2:6, 1, :].rearrange("p (c h) (m t) -> p c h m t", h=2, t=2)[:, :, :, :, 0], in_halves(ending[:, 2:5:2, :]), in_halves(by_chunk(stocks[1][:, 2, front])), ALU.mult
        )
        thin(6, ending[:, rows[6, 0], :], span(0))

        halves = [span(0, HALF), span(1, HALF)]
        every = slice(0, BANK)

        def within(c, cols):
            return slice(BANK * c + cols.start, BANK * c + cols.stop)

        def times(cols, factor):
            return slice(cols.start * factor, cols.stop * factor)

        def thin_last(c, cols=every):
            thin(7, ending[:, rows[7, c], cols], within(c, cols))

        def deplete_pair(c, h):
            cols = halves[h]
            if c > 1:
                nc.vector.tensor_tensor(pairs[c][:, h, 1, :].rearrange("p (m t) -> p m t", t=2)[:, :, 1], ending[:, rows[7, c], cols], stocks[1][:, 3, within(c, cols)], ALU.mult)
                return
            nc.vector.tensor_tensor(
                pairs[c][:, h, 1, :].rearrange("p (m i t) -> p m t i", i=RUN, t=2),
                ending[:, rows[6, c] : rows[7, c] + 1 : rows[7, c] - rows[6, c], cols].rearrange("p t (m i) -> p m t i", i=RUN),
                stocks[1][:, 2:4, within(c, cols)].rearrange("p t (m i) -> p m t i", i=RUN),
                ALU.mult,
            )

        def weave(copy, word, c, hs=slice(0, 2)):
            copy(
                out=zz[1, c][:].bitcast(word).rearrange("p (h m i u) -> p h m u i", h=2, u=2, i=2)[:, hs],
                in_=pairs[c].bitcast(word).rearrange("p h u (m i) -> p h m u i", i=2)[:, hs],
            )

        def deplete_whole(h, kib):
            zz[1, 0, h] = placed([P, PACK * HALF], BF16, "zz10%d" % h, kib)
            nc.vector.tensor_tensor(
                zz[1, 0, h][:].rearrange("p (m i t) -> p m t i", i=RUN, t=PACK),
                ending[:, 6:22:5, halves[h]].rearrange("p t (m i) -> p m t i", i=RUN),
                stocks[1][:, :, halves[h]].rearrange("p t (m i) -> p m t i", i=RUN),
                ALU.mult,
            )

        z_w, z_s = {}, {}

        def quantize_z(key, source, kib):
            width = source.shape[1] // PACK
            z_w[key] = placed([P, width], U32, "z_w" + "".join(str(i) for i in key), kib)
            z_s[key] = placed([P, width], U8, "z_s" + "".join(str(i) for i in key), 16 + 0.5 * len(z_s))
            nc.vector.quantize_mx(out=z_w[key][:].bitcast(FP8X4), scales=z_s[key][:], in_=source)

        def second_product(into, key, nt, start, stop):
            b = key[0]
            nc.tensor.matmul_mx(
                out=into,
                lhsT=wc_w[:, b, span(nt, 2 * P)].bitcast(FP4X4),
                lhsT_scale=wc_s[:, b, span(nt, P)],
                rhs=z_w[key][:, :].bitcast(FP8X4),
                rhs_scale=z_s[key][:, :],
                start=start,
                stop=stop,
            )

        staged = []

        def leave(copy, source, rows, kib=None):
            staged.append(placed([P, BANK], F32, "staged%d" % len(staged), (84 if len(staged) < 11 else 6) + 2 * len(staged) if kib is None else kib))
            copy(out=staged[-1][:], in_=source[:])
            nc.sync.dma_start(out=rows, in_=staged[-1][:] if len(rows.shape) == 2 else by_half(staged[-1][:]))

        def open_chunk(c):
            for nt in range(N // P):
                second_product(banks[4 * (1 - c % 2) + nt][:], (0, c), nt, True, False)

        def close_chunk(c):
            for nt in range(N // P):
                second_product(banks[4 * (1 - c % 2) + nt][:], (1, c), nt, False, True)
                leave(nc.scalar.copy, banks[4 * (1 - c % 2) + nt], out[span(nt, P), span(c)])

        def half_bank(c, h, g):
            return banks[4 * (1 - c % 2) + 2 * h + g]

        def half_product(b, c, h, g, first=0):
            for i in range(2):
                second_product(half_bank(c, h, g)[:, span(i, HALF)], (b, c, h), 2 * g + i, (b, i) == (first, 0), (b, i) == (1 - first, 1))

        def leave_half(copy, c, h, g, kib=None):
            leave(copy, half_bank(c, h, g), out[span(g, 2 * P), within(c, halves[h])].rearrange("(i p) m -> p i m", p=P), kib)

        for cols in halves:
            thin_last(3, cols)
        thin_last(2)
        quantize_z((0, 3), zz[0, 3][:], 4)
        for h in range(2):
            z_w[0, 3, h], z_s[0, 3, h] = z_w[0, 3][:, halves[h]], z_s[0, 3][:, halves[h]]
        for g in range(2):
            half_product(0, 3, 0, g)
        zz[1, 3] = placed([P, PACK * BANK], BF16, "zz13", 198)
        for h in range(2):
            deplete_pair(3, h)
            weave(nc.scalar.copy, U32, 3, span(h, 1))
        thin_last(1)
        deplete_pair(2, 0)
        quantize_z((1, 3, 0), zz[1, 3][:, times(halves[0], PACK)], 8)
        for g in range(2):
            half_product(1, 3, 0, g)
            leave_half(nc.scalar.copy, 3, 0, g)
        thin_last(0)
        deplete_pair(2, 1)
        quantize_z((1, 3, 1), zz[1, 3][:, times(halves[1], PACK)], 9)
        for g in range(2):
            for b in (1, 0):
                half_product(b, 3, 1, g, first=1)
            leave_half(nc.scalar.copy, 3, 1, g)
        zz[1, 2] = placed([P, PACK * BANK], BF16, "zz12", 202)
        weave(nc.vector.tensor_copy, F32, 2)
        quantize_z((0, 2), zz[0, 2][:], 198)
        open_chunk(2)
        quantize_z((1, 2), zz[1, 2][:], 10)
        close_chunk(2)
        for h in range(2):
            deplete_pair(1, h)
        quantize_z((0, 1), zz[0, 1][:], 202)
        open_chunk(1)
        zz[1, 1] = placed([P, PACK * BANK], BF16, "zz11", 206)
        weave(nc.vector.tensor_copy, F32, 1)
        quantize_z((0, 0, 0), zz[0, 0][:, times(halves[0], PACK)], 170)
        quantize_z((1, 1), zz[1, 1][:], 0)
        close_chunk(1)
        for g in range(2):
            half_product(0, 0, 0, g)
        deplete_whole(0, 162)
        quantize_z((0, 0, 1), zz[0, 0][:, times(halves[1], PACK)], 206)
        quantize_z((1, 0, 0), zz[1, 0, 0][:], 12)
        for g in range(2):
            half_product(1, 0, 0, g)
        for g in range(2):
            half_product(0, 0, 1, g)
        deplete_whole(1, 164)
        leave_half(nc.scalar.copy, 0, 0, 0)
        quantize_z((1, 0, 1), zz[1, 0, 1][:], 13)
        leave_half(nc.vector.tensor_copy, 0, 0, 1, 164)
        for g in range(2):
            half_product(1, 0, 1, g)
        leave_half(nc.scalar.copy, 0, 1, 0)
        leave_half(nc.vector.tensor_copy, 0, 1, 1)
